import numpy as np
import ml_dtypes


def mxq(x, axis, fmt="e4m3"):
    dtype, down = {"e4m3": (ml_dtypes.float8_e4m3fn, 7), "e5m2": (ml_dtypes.float8_e5m2, 14)}[fmt]
    v = np.moveaxis(np.asarray(x, np.float32).astype(ml_dtypes.bfloat16).astype(np.float64), axis, -1)
    blocks = v.reshape(v.shape[:-1] + (-1, 32))
    amax = np.abs(blocks).max(-1, keepdims=True)
    byte = np.maximum(np.where(amax > 0, np.frexp(amax)[1] - 1 + 127, 0) - down, 1)
    scale = np.exp2(byte - 127.0)
    codes = (blocks / scale).astype(np.float32).astype(dtype).astype(np.float64)
    return np.moveaxis((codes * scale).reshape(v.shape), -1, axis)


WIDE = False


def mx_kscale(k):
    if not WIDE:
        return np.ones(k)
    levels = np.array([10, -10, 5, -5, 0])
    if k % 512:
        return np.exp2(np.random.permutation(np.resize(levels, k // 32))).repeat(32)
    a = np.empty((k // 512, 16))
    for p in range(k // 512):
        a[p, :8] = np.random.permutation(np.resize(levels, 8))
        for g in range(8):
            far = levels[np.abs(levels - a[p, g]) >= 10]
            a[p, g + 8] = far[np.random.randint(len(far))]
    return np.exp2(a.ravel()).repeat(32)


def f64(x):
    return np.asarray(x).astype(np.float64)


def striped(idx):
    return np.tile(idx.reshape(-1, 16).T, (8, 1)).astype(np.uint16)


def unstriped(offs):
    return offs[:16].T.reshape(-1).astype(np.int64)


E2M1 = np.array([0.0, 0.5, 1.0, 1.5, 2.0, 3.0, 4.0, 6.0, -0.0, -0.5, -1.0, -1.5, -2.0, -3.0, -4.0, -6.0])


def pack_weight(w, fmt):
    k, n = w.shape
    w = f64(np.asarray(w, np.float32).astype(ml_dtypes.bfloat16)).reshape(k // 32, 32, n)
    amax = np.abs(w).max(1)
    if fmt == "e4m3":
        byte = np.frexp(amax)[1] - 1 + 127 - 7
    else:
        mant, ex = np.frexp(amax / 6.0)
        byte = np.where(mant > 0.5, ex, ex - 1) + 127
    byte = np.clip(np.where(amax > 0, byte, 1), 1, 254)
    scaled = (w * np.exp2(127.0 - byte)[:, None, :]).reshape(k, n).astype(np.float32)
    by_word = np.ascontiguousarray(scaled.reshape(k // 512, 128, 4, n).transpose(0, 1, 3, 2))
    if fmt == "e4m3":
        words = by_word.astype(ml_dtypes.float8_e4m3fn).view(np.uint8)
    else:
        c = by_word.astype(ml_dtypes.float4_e2m1fn).view(np.uint8) & 0xF
        words = (c[..., 0::2] | (c[..., 1::2] << 4)).reshape(k // 512, 128, 2 * n)
    return np.ascontiguousarray(words), np.ascontiguousarray(byte.astype(np.uint8).reshape(k // 512, 16, n))


def unpack_weight(words, scales, fmt):
    g, _, n = scales.shape
    words = np.ascontiguousarray(words).reshape(g, 128, n, -1)
    if fmt == "e4m3":
        vals = words.view(ml_dtypes.float8_e4m3fn).astype(np.float64)
    else:
        nib = np.empty((g, 128, n, 4), np.uint8)
        nib[..., 0::2] = words & 0xF
        nib[..., 1::2] = words >> 4
        vals = E2M1[nib]
    vals = vals * np.repeat(np.exp2(scales.astype(np.float64) - 127.0), 8, axis=1)[..., None]
    return vals.transpose(0, 1, 3, 2).reshape(g * 512, n)


def silu(v):
    return v / (1.0 + np.exp(-np.maximum(v, -700.0)))


K, T, E, C, H, HS, N = 1024, 640, 10, 128, 512, 1024, 128


def by_expert(wq, xq):
    return np.concatenate([wq[e].T @ xq[:, e * C:(e + 1) * C] for e in range(E)], axis=1)


def setup_inputs():
    n = np.random.standard_normal
    s = mx_kscale(K)
    u = mx_kscale(H)
    v = mx_kscale(HS)
    first = np.random.permutation(np.repeat(np.arange(E), T // E))
    second = (first + 1 + np.random.permutation(np.repeat(np.arange(E - 1), -(-T // (E - 1)))[:T])) % E
    while np.bincount(second, minlength=E).max() != T // E:
        load = np.bincount(second, minlength=E); hi, lo = int(load.argmax()), int(load.argmin())
        t = np.flatnonzero((second == hi) & (first != lo))[0]; second[t] = lo
    slot_token = np.empty(E * C, np.int64); pos = np.empty((2, T), np.int64); fill = np.zeros(E, np.int64)
    place = np.stack([np.random.permutation(C) for _ in range(E)])
    for r, deal in enumerate((first, second)):
        for t in np.random.permutation(T):
            e = deal[t]; j = e * C + place[e, fill[e]]; fill[e] += 1; slot_token[j] = t; pos[r, t] = j
    g = np.random.uniform(0.2, 0.8, T)
    x = pack_weight(n((K, T)) * s[:, None], "e4m3")
    w1 = [pack_weight(m, "e2m1") for m in n((E, K, H)) / np.sqrt(K) / s[None, :, None] * u]
    w2 = [pack_weight(m, "e2m1") for m in n((E, H, N)) / np.sqrt(H) / u[None, :, None]]
    w1s = pack_weight(n((K, HS)) / np.sqrt(K) / s[:, None] * v, "e4m3")
    w2s = pack_weight(n((HS, N)) / np.sqrt(HS) / v[:, None], "e4m3")
    return {
        "x_words": x[0],
        "x_scales": x[1],
        "w1_words": np.stack([m[0] for m in w1]),
        "w1_scales": np.stack([m[1] for m in w1]),
        "w2_words": np.stack([m[0] for m in w2]),
        "w2_scales": np.stack([m[1] for m in w2]),
        "w1s_words": w1s[0],
        "w1s_scales": w1s[1],
        "w2s_words": w2s[0],
        "w2s_scales": w2s[1],
        "gate": np.stack([np.tile(g, (128, 1)), np.tile(1.0 - g, (128, 1))]).astype(np.float32),
        "offs": striped(slot_token),
        "pos1": striped(pos[0]),
        "pos2": striped(pos[1]),
    }


def reference(x_words, x_scales, w1_words, w1_scales, w2_words, w2_scales, w1s_words, w1s_scales, w2s_words, w2s_scales, gate, offs, pos1, pos2):
    w1 = np.stack([unpack_weight(w1_words[e], w1_scales[e], "e2m1") for e in range(E)])
    w2 = np.stack([unpack_weight(w2_words[e], w2_scales[e], "e2m1") for e in range(E)])
    w1s = unpack_weight(w1s_words, w1s_scales, "e4m3")
    w2s = unpack_weight(w2s_words, w2s_scales, "e4m3")
    idx = unstriped(offs)
    x = unpack_weight(x_words, x_scales, "e4m3")
    hs = silu(w1s.T @ x)
    ys = w2s.T @ mxq(hs, 0, "e4m3")
    h = silu(by_expert(w1, x[:, idx]))
    y = by_expert(w2, mxq(h, 0, "e4m3"))
    c = sum(f64(gate[r, :1]) * y[:, unstriped(p)] for r, p in enumerate((pos1, pos2)))
    return ys + c

@@ -1,0 +1,309 @@
+from contextlib import ExitStack
+
+import concourse.mybir as mybir
+from concourse.masks import make_identity
+
+K, T, E, C, H, HS, N = 1024, 640, 10, 128, 512, 1024, 128
+FLOPS = 2 * (K * H + H * N) * E * C + 2 * (K * HS + HS * N) * T
+
+F32 = mybir.dt.float32
+BF16 = mybir.dt.bfloat16
+I32 = mybir.dt.int32
+U32 = mybir.dt.uint32
+U16 = mybir.dt.uint16
+U8 = mybir.dt.uint8
+FP8X4 = mybir.dt.float8_e4m3fn_x4
+FP4X4 = mybir.dt.float4_e2m1fn_x4
+SILU = mybir.ActivationFunctionType.Silu
+MULT = mybir.AluOpType.mult
+ADD = mybir.AluOpType.add
+
+P = 128
+W = 512
+PASSES = 2
+SLOTS = E * C
+XS_WINDOW = 1024
+
+
+def tile_moe_shf_mlp_silu_kernel(
+    tc, x_words, x_scales, w1_words, w1_scales, w2_words, w2_scales, w1s_words, w1s_scales,
+    w2s_words, w2s_scales, gate, offs, pos1, pos2, out,
+):
+    nc = tc.nc
+    with ExitStack() as ctx:
+        keep = ctx.enter_context(tc.tile_pool(name="keep", bufs=1))
+        work = ctx.enter_context(tc.tile_pool(name="work", bufs=3))
+        psum = ctx.enter_context(tc.psum_pool(name="psum", bufs=1))
+
+        ring = ctx.enter_context(tc.tile_pool(name="ring", bufs=4))
+
+        def plane(name, nbytes, engine):
+            t = keep.tile([P, nbytes // 4], I32, name=name, align_bytes=64)
+            engine.memset(t[:], 0)
+            return t
+
+        def load_plane(queues, t, rows):
+            groups = rows.shape[0]
+            src = rows.rearrange("g (q r) w -> r q g w", r=4)
+            for r in range(4):
+                queues[r].dma_start(
+                    out=t[r:P:32, :].rearrange("q (g w) -> q g w", g=groups),
+                    in_=src[r].bitcast(I32),
+                )
+
+        def load_packed_plane(queues, t, rows):
+            width = rows.shape[2] // 4
+            for q in range(4):
+                queues[q].dma_start(
+                    out=t[32 * q : 32 * q + 8, 0:width], in_=rows[:, 4 * q : 4 * q + 4, :].bitcast(I32)
+                )
+
+        offs_t = keep.tile([P, SLOTS // 16], U16, name="offs_t")
+        pos1_t = keep.tile([P, T // 16], U16, name="pos1_t")
+        pos2_t = keep.tile([P, T // 16], U16, name="pos2_t")
+        xw = keep.tile([P, PASSES * T], I32, name="xw", align_bytes=64)
+        w1s_t = {}
+        w1_t = {}
+        w2s_t = keep.tile([P, 2 * N], I32, name="w2s_t", align_bytes=64)
+        ident = keep.tile([P, P], F32, name="ident")
+        y_sb = keep.tile([P, SLOTS], F32, name="y_sb")
+
+        xs = plane("xs", XS_WINDOW, nc.gpsimd)
+        w1s_p = plane("w1s_p", HS, nc.gpsimd)
+        w1_p = plane("w1_p", E * PASSES * H, nc.vector)
+        moved = [plane("moved_%d" % c, SLOTS // 2, nc.vector) for c in range(2)]
+        w2_p = plane("w2_p", E * N, nc.vector)
+        w2s_p = plane("w2s_p", 2 * N, nc.vector)
+
+        def load_w1s(h):
+            w1s_t[h] = ring.tile([P, PASSES * W], I32, name="w1s_%d" % h, tag="ring", align_bytes=64)
+            nc.sync.dma_start(
+                out=w1s_t[h][:].rearrange("p (s l) -> p s l", s=PASSES),
+                in_=w1s_words.rearrange("s p l d -> p s (l d)")[:, :, 4 * W * h : 4 * W * (h + 1)].bitcast(I32),
+            )
+
+        def load_w1(g):
+            w1_t[g] = ring.tile([P, 2 * PASSES * 2 * H], U8, name="w1_%d" % g, tag="ring", align_bytes=64)
+            nc.sync.dma_start(
+                out=w1_t[g][:].bitcast(I32).rearrange("p (a b) -> p a b", a=2 * PASSES),
+                in_=w1_words[2 * g : 2 * g + 2].rearrange("e s p b -> p (e s) b").bitcast(I32),
+            )
+
+        nc.sync.dma_start(offs_t[:], offs)
+        nc.sync.dma_start(
+            out=xw[:].rearrange("p (s t) -> p s t", s=PASSES),
+            in_=x_words.rearrange("s p t d -> p s (t d)").bitcast(I32),
+        )
+        load_packed_plane([nc.sync] * 4, xs, x_scales)
+        load_w1s(0)
+        warm = ring.tile([P, 8], F32, name="warm", tag="ring", align_bytes=64)
+        nc.gpsimd.memset(warm[:], 0.0)
+        nc.scalar.activation(warm[:], warm[:], SILU)
+        load_packed_plane([nc.sync] * 4, w1s_p, w1s_scales)
+        make_identity(nc, ident[:])
+        load_plane([nc.sync] * 4, w1_p, w1_scales.rearrange("e s b i -> (e s) b i"))
+        load_plane([nc.gpsimd] * 4, w2_p, w2_scales.rearrange("e s b i -> (e s) b i"))
+        load_plane([nc.gpsimd] * 4, w2s_p, w2s_scales)
+        nc.gpsimd.dma_start(
+            out=w2s_t[:].rearrange("p (s n) -> p s n", s=2),
+            in_=w2s_words.rearrange("s p n d -> p s (n d)").bitcast(I32),
+        )
+        load_w1(0)
+        load_w1(1)
+        load_w1(2)
+        w2_t = ring.tile([P, E * 2 * N], U8, name="w2_t", tag="ring", align_bytes=64)
+        nc.sync.dma_start(
+            out=w2_t[:].bitcast(I32).rearrange("p (e b) -> p e b", e=E),
+            in_=w2_words.rearrange("e s p b -> p (e s) b").bitcast(I32),
+        )
+        load_w1(3)
+        load_w1(4)
+        load_w1s(1)
+        gate_t = ring.tile([P, 2 * T], F32, name="gate_t", tag="ring", align_bytes=64)
+        nc.sync.dma_start(out=gate_t[:].rearrange("p (r t) -> p r t", r=2), in_=gate.rearrange("r p t -> p r t"))
+        nc.sync.dma_start(pos1_t[:], pos1)
+        nc.sync.dma_start(pos2_t[:], pos2)
+
+        xs_b = xs[:].bitcast(U8)
+        w1s_pb = w1s_p[:].bitcast(U8)
+        w1_pb = w1_p[:].bitcast(U8)
+        w2_pb = w2_p[:].bitcast(U8)
+        w2s_pb = w2s_p[:].bitcast(U8)
+
+        gathered = {}
+
+        half = SLOTS // 2
+        slot_scales = []
+
+        def gather_scales(c):
+            gs = keep.tile([P, half], U8, name="gs_%d" % c, align_bytes=64)
+            nc.vector.tensor_copy(gs[:], xs_b.indirect(offs_t[:, half // 16 * c : half // 16 * (c + 1)]))
+            nc.sync.dma_start(out=moved[c][0:112, :], in_=gs[:].bitcast(I32)[4:116, :])
+            slot_scales.append((gs[:], moved[c][:].bitcast(U8)))
+
+        def gather(g):
+            cols = offs_t[:, 16 * g : 16 * (g + 1)]
+            for s in range(PASSES):
+                gw = keep.tile([P, 2 * C], U32, name="gw_%d_%d" % (g, s), align_bytes=64)
+                nc.vector.tensor_copy(gw[:], xw[:, T * s : T * (s + 1)].bitcast(U32).indirect(cols))
+                gathered[(g, s)] = gw
+
+        units = [[("s", 0, 0), ("s", 1, 0)], [("s", 2, 0), ("s", 3, 0)], [("s", 4, 0)]]
+        units += [[("r", 2 * g, 0), ("r", 2 * g + 1, 0)] for g in range(E // 2)]
+        units += [[("s", 0, 1), ("s", 1, 1)], [("s", 2, 1), ("s", 3, 1)], [("s", 4, 1)]]
+        turn_on_vector = (5, 6, 7)
+        hidden = {}
+        codes = {}
+
+        w1s_perm = keep.tile([P, PASSES * W], I32, name="w1s_perm", align_bytes=64)
+        w1s_perm_p = keep.tile([P, W], U8, name="w1s_perm_p", align_bytes=64)
+
+        def permute_w1s():
+            nc.vector.tensor_copy(
+                w1s_perm_p[:].rearrange("p (t m) -> p t m", t=4),
+                w1s_pb[:, W : 2 * W].rearrange("p (m t) -> p t m", t=4),
+            )
+            nc.vector.tensor_copy(
+                w1s_perm[:].rearrange("p (s t a i) -> p s a t i", s=PASSES, t=4, i=4),
+                w1s_t[1][:].rearrange("p (s a i t) -> p s a t i", s=PASSES, t=4, i=4),
+            )
+
+        def first_layer(u):
+            hb = work.tile([P, 2 * W], BF16, name="hb", align_bytes=64)
+            for b, (kind, j, h) in enumerate(units[u]):
+                acc = psum.tile([P, W], F32, name="acc", bufs=4)
+                if h == 1:
+                    for t in range(4):
+                        for s in range(PASSES):
+                            c0 = T * s + P * j
+                            nc.tensor.matmul_mx(
+                                out=acc[:, P * t : P * (t + 1)],
+                                lhsT=w1s_perm[:, W * s + P * t : W * s + P * (t + 1)].bitcast(FP8X4),
+                                lhsT_scale=w1s_perm_p[4 * s : P, P * t : P * (t + 1)],
+                                rhs=xw[:, c0 : c0 + P].bitcast(FP8X4),
+                                rhs_scale=xs_b[4 * s : P, P * j : P * (j + 1)],
+                                start=(s == 0), stop=(s == PASSES - 1),
+                            )
+                    nc.scalar.activation(
+                        hb[:, W * b : W * (b + 1)].rearrange("p (r t) -> p r t", t=4),
+                        acc[:].rearrange("p (t r) -> p r t", t=4),
+                        SILU,
+                    )
+                    continue
+                for s in range(PASSES):
+                    if kind == "s":
+                        c0 = T * s + P * j
+                        nc.tensor.matmul_mx(
+                            out=acc[:],
+                            lhsT=xw[:, c0 : c0 + P].bitcast(FP8X4),
+                            lhsT_scale=xs_b[4 * s : P, P * j : P * (j + 1)],
+                            rhs=w1s_t[h][:, W * s : W * (s + 1)].bitcast(FP8X4),
+                            rhs_scale=w1s_pb[4 * s : P, W * h : W * (h + 1)],
+                            start=(s == 0), stop=(s == PASSES - 1),
+                        )
+                    else:
+                        gw = gathered[(j // 2, s)]
+                        gs = slot_scales[j // 5][s]
+                        a = PASSES * (j % 2) + s
+                        es = PASSES * j + s
+                        nc.tensor.matmul_mx(
+                            out=acc[:],
+                            lhsT=gw[:, C * (j % 2) : C * (j % 2 + 1)].bitcast(FP8X4),
+                            lhsT_scale=gs[:, C * (j % 5) : C * (j % 5 + 1)],
+                            rhs=w1_t[j // 2][:, 2 * H * a : 2 * H * (a + 1)].bitcast(FP4X4),
+                            rhs_scale=w1_pb[:, H * es : H * (es + 1)],
+                            start=(s == 0), stop=(s == PASSES - 1),
+                        )
+                nc.scalar.activation(
+                    hb[:, W * b : W * (b + 1)].rearrange("r (u p e) -> r u p e", u=2, e=2),
+                    acc[:].rearrange("r (p u e) -> r u p e", u=2, e=2),
+                    SILU,
+                )
+            hidden[u] = hb
+
+        def turn(u):
+            nb = len(units[u])
+            if units[u][0][2] == 1:
+                grouped = hidden[u]
+            else:
+                words = hidden[u][:].bitcast(F32)
+                turned = psum.tile([P, W], F32, name="turned", bufs=1)
+                for j in range(2 * nb):
+                    nc.tensor.transpose(turned[:, P * j : P * (j + 1)], words[:, P * j : P * (j + 1)], ident[:])
+                grouped = work.tile([P, 2 * W], BF16, name="grouped", align_bytes=64)
+                dst = grouped[:, 0 : W * nb].bitcast(F32).rearrange("p (b r u) -> p b r u", b=nb, u=2)
+                src = turned[:, 0 : 2 * P * nb].rearrange("p (b u r) -> p b r u", b=nb, u=2)
+                if u in turn_on_vector:
+                    nc.vector.tensor_copy(dst, src)
+                else:
+                    nc.scalar.copy(dst, src)
+            hw = keep.tile([P, nb * P], U32, name="hw_%d" % u, align_bytes=64)
+            hs = keep.tile([P, nb * P], U8, name="hs_%d" % u, align_bytes=64)
+            nc.vector.quantize_mx(out=hw[:].bitcast(FP8X4), scales=hs[:], in_=grouped[:, 0 : W * nb])
+            for b, blk in enumerate(units[u]):
+                codes[blk] = (hw[:, P * b : P * (b + 1)], hs[:, P * b : P * (b + 1)])
+
+        combined = {}
+
+        def combine(t0, t1):
+            parts = []
+            for r, pos_t in enumerate((pos1_t, pos2_t)):
+                part = keep.tile([P, t1 - t0], F32, name="part_%d_%d" % (t0, r))
+                nc.vector.tensor_tensor(
+                    part[:], y_sb[:].indirect(pos_t[:, t0 // 16 : t1 // 16]), gate_t[:, T * r + t0 : T * r + t1], MULT
+                )
+                parts.append(part)
+            both = keep.tile([P, t1 - t0], F32, name="both_%d" % t0)
+            nc.vector.tensor_tensor(both[:], parts[0][:], parts[1][:], ADD)
+            combined[t0] = both
+
+        def second_layer(u):
+            blocks = units[u]
+            if blocks[0][0] == "r":
+                y = psum.tile([P, 2 * C], F32, name="y", bufs=3)
+                for b, blk in enumerate(blocks):
+                    e = blk[1]
+                    hw, hs = codes[blk]
+                    nc.tensor.matmul_mx(
+                        out=y[:, C * b : C * (b + 1)],
+                        lhsT=w2_t[:, 2 * N * e : 2 * N * (e + 1)].bitcast(FP4X4),
+                        lhsT_scale=w2_pb[:, N * e : N * (e + 1)],
+                        rhs=hw.bitcast(FP8X4), rhs_scale=hs, start=True, stop=True,
+                    )
+                e0 = blocks[0][1]
+                nc.scalar.copy(y_sb[:, C * e0 : C * (e0 + 2)], y[:])
+                return
+            tiles = [j for (kind, j, h) in blocks if h == 1]
+            if not tiles:
+                return
+            y = psum.tile([P, 2 * C], F32, name="y", bufs=3)
+            for b, j in enumerate(tiles):
+                for h in range(2):
+                    hw, hs = codes[("s", j, h)]
+                    nc.tensor.matmul_mx(
+                        out=y[:, P * b : P * (b + 1)],
+                        lhsT=w2s_t[:, N * h : N * (h + 1)].bitcast(FP8X4),
+                        lhsT_scale=w2s_pb[:, N * h : N * (h + 1)],
+                        rhs=hw.bitcast(FP8X4), rhs_scale=hs, start=(h == 0), stop=(h == 1),
+                    )
+            t0 = P * tiles[0]
+            width = P * len(tiles)
+            combine(t0, t0 + width)
+            res = keep.tile([P, width], F32, name="res_%d" % t0)
+            nc.vector.tensor_tensor(res[:], y[:, 0:width], combined[t0][:], ADD)
+            nc.sync.dma_start(out[:, t0 : t0 + width], res[:])
+
+        n_units = len(units)
+        for step in range(n_units + 2):
+            if step in (0, 3):
+                gather_scales(step // 3)
+            if step == 7:
+                permute_w1s()
+            if step < n_units:
+                if units[step][0][0] == "r":
+                    gather(units[step][0][1] // 2)
+                first_layer(step)
+            if 0 <= step - 1 < n_units:
+                turn(step - 1)
+            if 0 <= step - 2 < n_units:
+                second_layer(step - 2)

@@ -23,6 +23,7 @@ W = 512
 PASSES = 2
 SLOTS = E * C
 XS_WINDOW = 1024
+CFG = {'ms': 'ggvvvvv', 'w1p_split': 4, 'chunks': [0, 6, 10], 'queue': {'w1pa': 'y', 'w1pb': 'g', 'w2p': 'y', 'w2sp': 'g', 'move': 'y', 'w2s': 'y'}, 'w1sp_q': 'yyyy', 'units': [[('s', 0, 0), ('s', 1, 0)], [('s', 2, 0), ('s', 3, 0)], [('r', 0, 0), ('r', 1, 0)], [('r', 2, 0), ('r', 3, 0)], [('r', 4, 0), ('r', 5, 0)], [('r', 6, 0), ('r', 7, 0)], [('r', 8, 0), ('r', 9, 0)], [('s', 4, 0)], [('s', 0, 1), ('s', 1, 1)], [('s', 2, 1), ('s', 3, 1)], [('s', 4, 1)]], 'tv': [5, 7], 'yv': [2, 6], 'pm': [0], 'fin': {8: [0, 1], 9: [2, 3], 10: [4]}, 'A': [1], 'bufs': [4, 2, 2], 'plan': [('ld', 'offs'), ('ld', 'xs'), ('ld', 'x0'), ('ld', 'w0a'), ('ld', 'w1sp'), ('ld', 'x1'), ('ld', 'w0b'), ('sg', 0), ('ld', 'w1_0'), ('ld', 'w1pa'), ('mv', 0), ('ld', 'w1_1'), ('ld', 'w2'), ('ld', 'w1pb'), ('ld', 'w1_2'), ('ld', 'w2p'), ('ld', 'w1_3'), ('sg', 1), ('mv', 1), ('ld', 'w1_4'), ('ld', 'w1s1'), ('ld', 'w2s'), ('ld', 'w2sp'), ('ld', 'pos1'), ('ld', 'pos2'), ('ld', 'gate'), ('g', 0), ('l1', 0), ('g', 1), ('l1', 1), ('t', 0), ('g', 2), ('l1', 2), ('q', 0), ('t', 1), ('g', 3), ('l1', 3), ('q', 1), ('t', 2), ('l2', 0), ('g', 4), ('l1', 4), ('q', 2), ('t', 3), ('l2', 1), ('l1', 5), ('q', 3), ('t', 4), ('l2', 2), ('ps', 1), ('pw', 1), ('l1', 6), ('q', 4), ('t', 5), ('l2', 3), ('l1', 7), ('q', 5), ('t', 6), ('l2', 4), ('l1', 8), ('q', 6), ('t', 7), ('l2', 5), ('l1', 9), ('q', 7), ('t', 8), ('l2', 6), ('ft', 0, 256, 0), ('l1', 10), ('q', 8), ('ft', 0, 256, 1), ('t', 9), ('l2', 7), ('ft', 256, 512, 0), ('q', 9), ('ad', 0, 256), ('t', 10), ('l2', 8), ('ft', 256, 512, 1), ('q', 10), ('fin', 0, 256), ('l2', 9), ('ft', 512, 640, 0), ('l2', 10), ('ad', 256, 512), ('ft', 512, 640, 1), ('fin', 256, 512), ('ad', 512, 640), ('fin', 512, 640)]}
 
 
 def tile_moe_shf_mlp_silu_kernel(
@@ -32,10 +33,10 @@ def tile_moe_shf_mlp_silu_kernel(
     nc = tc.nc
     with ExitStack() as ctx:
         keep = ctx.enter_context(tc.tile_pool(name="keep", bufs=1))
-        work = ctx.enter_context(tc.tile_pool(name="work", bufs=3))
+        work = ctx.enter_context(tc.tile_pool(name="work", bufs=4))
         psum = ctx.enter_context(tc.psum_pool(name="psum", bufs=1))
 
-        ring = ctx.enter_context(tc.tile_pool(name="ring", bufs=4))
+        ring = ctx.enter_context(tc.tile_pool(name="ring", bufs=1))
 
         def plane(name, nbytes, engine):
             t = keep.tile([P, nbytes // 4], I32, name=name, align_bytes=64)
@@ -68,78 +69,114 @@ def tile_moe_shf_mlp_silu_kernel(
         ident = keep.tile([P, P], F32, name="ident")
         y_sb = keep.tile([P, SLOTS], F32, name="y_sb")
 
-        xs = plane("xs", XS_WINDOW, nc.gpsimd)
-        w1s_p = plane("w1s_p", HS, nc.gpsimd)
-        w1_p = plane("w1_p", E * PASSES * H, nc.vector)
-        moved = [plane("moved_%d" % c, SLOTS // 2, nc.vector) for c in range(2)]
-        w2_p = plane("w2_p", E * N, nc.vector)
-        w2s_p = plane("w2s_p", 2 * N, nc.vector)
+        eng = {"v": nc.vector, "g": nc.gpsimd, "y": nc.sync, "s": nc.scalar}
+        xs = plane("xs", XS_WINDOW, eng[CFG["ms"][0]])
+        w1s_p = plane("w1s_p", HS, eng[CFG["ms"][1]])
+        split = CFG["w1p_split"]
+        w1_pa = plane("w1_pa", split * PASSES * H, eng[CFG["ms"][2]])
+        chunks = CFG["chunks"]
+        moved = [plane("moved_%d" % c, C * (chunks[c + 1] - chunks[c]), eng[CFG["ms"][3]]) for c in range(len(chunks) - 1)]
+        w1_pb = plane("w1_pb", (E - split) * PASSES * H, eng[CFG["ms"][4]]) if split < E else None
+        w2_p = plane("w2_p", E * N, eng[CFG["ms"][5]])
+        w2s_p = plane("w2s_p", 2 * N, eng[CFG["ms"][6]])
+        warm = keep.tile([P, 8], F32, name="warm")
+        nc.gpsimd.memset(warm[:], 0.0)
+        nc.scalar.activation(warm[:], warm[:], SILU)
+        make_identity(nc, ident[:])
+        w2_t = keep.tile([P, E * 2 * N], U8, name="w2_t", align_bytes=64)
+        gate_t = keep.tile([P, 2 * T], F32, name="gate_t", align_bytes=64)
 
         def load_w1s(h):
-            w1s_t[h] = ring.tile([P, PASSES * W], I32, name="w1s_%d" % h, tag="ring", align_bytes=64)
+            w1s_t[h] = ring.tile([P, PASSES * W], I32, name="w1s_%d" % h, tag="slot_%d" % (5 + h), align_bytes=64)
             nc.sync.dma_start(
                 out=w1s_t[h][:].rearrange("p (s l) -> p s l", s=PASSES),
                 in_=w1s_words.rearrange("s p l d -> p s (l d)")[:, :, 4 * W * h : 4 * W * (h + 1)].bitcast(I32),
             )
 
         def load_w1(g):
-            w1_t[g] = ring.tile([P, 2 * PASSES * 2 * H], U8, name="w1_%d" % g, tag="ring", align_bytes=64)
+            w1_t[g] = ring.tile([P, 2 * PASSES * 2 * H], U8, name="w1_%d" % g, tag="slot_%d" % g, align_bytes=64)
             nc.sync.dma_start(
                 out=w1_t[g][:].bitcast(I32).rearrange("p (a b) -> p a b", a=2 * PASSES),
                 in_=w1_words[2 * g : 2 * g + 2].rearrange("e s p b -> p (e s) b").bitcast(I32),
             )
 
-        nc.sync.dma_start(offs_t[:], offs)
-        nc.sync.dma_start(
-            out=xw[:].rearrange("p (s t) -> p s t", s=PASSES),
-            in_=x_words.rearrange("s p t d -> p s (t d)").bitcast(I32),
-        )
-        load_packed_plane([nc.sync] * 4, xs, x_scales)
-        load_w1s(0)
-        warm = ring.tile([P, 8], F32, name="warm", tag="ring", align_bytes=64)
-        nc.gpsimd.memset(warm[:], 0.0)
-        nc.scalar.activation(warm[:], warm[:], SILU)
-        load_packed_plane([nc.sync] * 4, w1s_p, w1s_scales)
-        make_identity(nc, ident[:])
-        load_plane([nc.sync] * 4, w1_p, w1_scales.rearrange("e s b i -> (e s) b i"))
-        load_plane([nc.gpsimd] * 4, w2_p, w2_scales.rearrange("e s b i -> (e s) b i"))
-        load_plane([nc.gpsimd] * 4, w2s_p, w2s_scales)
-        nc.gpsimd.dma_start(
-            out=w2s_t[:].rearrange("p (s n) -> p s n", s=2),
-            in_=w2s_words.rearrange("s p n d -> p s (n d)").bitcast(I32),
-        )
-        load_w1(0)
-        load_w1(1)
-        load_w1(2)
-        w2_t = ring.tile([P, E * 2 * N], U8, name="w2_t", tag="ring", align_bytes=64)
-        nc.sync.dma_start(
-            out=w2_t[:].bitcast(I32).rearrange("p (e b) -> p e b", e=E),
-            in_=w2_words.rearrange("e s p b -> p (e s) b").bitcast(I32),
-        )
-        load_w1(3)
-        load_w1(4)
-        load_w1s(1)
-        gate_t = ring.tile([P, 2 * T], F32, name="gate_t", tag="ring", align_bytes=64)
-        nc.sync.dma_start(out=gate_t[:].rearrange("p (r t) -> p r t", r=2), in_=gate.rearrange("r p t -> p r t"))
-        nc.sync.dma_start(pos1_t[:], pos1)
-        nc.sync.dma_start(pos2_t[:], pos2)
+        def load(name):
+            q = eng[CFG["queue"].get(name, "y")]
+            if name == "offs":
+                nc.sync.dma_start(offs_t[:], offs)
+            elif name == "pos1":
+                nc.sync.dma_start(pos1_t[:], pos1)
+            elif name == "pos2":
+                nc.sync.dma_start(pos2_t[:], pos2)
+            elif name == "x":
+                q.dma_start(
+                    out=xw[:].rearrange("p (s t) -> p s t", s=PASSES),
+                    in_=x_words.rearrange("s p t d -> p s (t d)").bitcast(I32),
+                )
+            elif name in ("x0", "x1"):
+                s = int(name[1])
+                q.dma_start(out=xw[:, T * s : T * (s + 1)], in_=x_words[s].rearrange("p t d -> p (t d)").bitcast(I32))
+            elif name == "xs":
+                load_packed_plane([q] * 4, xs, x_scales)
+            elif name == "w1sp":
+                load_packed_plane([eng[c] for c in CFG["w1sp_q"]], w1s_p, w1s_scales)
+            elif name == "w1pa":
+                load_plane([q] * 4, w1_pa, w1_scales[0:split].rearrange("e s b i -> (e s) b i"))
+            elif name == "w1pb":
+                load_plane([q] * 4, w1_pb, w1_scales[split:E].rearrange("e s b i -> (e s) b i"))
+            elif name == "w2p":
+                load_plane([q] * 4, w2_p, w2_scales.rearrange("e s b i -> (e s) b i"))
+            elif name == "w2sp":
+                load_plane([q] * 4, w2s_p, w2s_scales)
+            elif name in ("w0a", "w0b"):
+                s = int(name == "w0b")
+                if s == 0:
+                    w1s_t[0] = ring.tile([P, PASSES * W], I32, name="w1s_0", tag="slot_5", align_bytes=64)
+                q.dma_start(
+                    out=w1s_t[0][:, W * s : W * (s + 1)],
+                    in_=w1s_words[s].rearrange("p l d -> p (l d)")[:, 0 : 4 * W].bitcast(I32),
+                )
+            elif name.startswith("w1s"):
+                load_w1s(int(name[3]))
+            elif name.startswith("w1_"):
+                load_w1(int(name[3]))
+            elif name == "w2":
+                q.dma_start(
+                    out=w2_t[:].bitcast(I32).rearrange("p (e b) -> p e b", e=E),
+                    in_=w2_words.rearrange("e s p b -> p (e s) b").bitcast(I32),
+                )
+            elif name == "w2s":
+                q.dma_start(
+                    out=w2s_t[:].rearrange("p (s n) -> p s n", s=2),
+                    in_=w2s_words.rearrange("s p n d -> p s (n d)").bitcast(I32),
+                )
+            elif name == "gate":
+                q.dma_start(out=gate_t[:].rearrange("p (r t) -> p r t", r=2), in_=gate.rearrange("r p t -> p r t"))
 
         xs_b = xs[:].bitcast(U8)
         w1s_pb = w1s_p[:].bitcast(U8)
-        w1_pb = w1_p[:].bitcast(U8)
+        w1_planes = [w1_pa[:].bitcast(U8), w1_pb[:].bitcast(U8) if split < E else None]
         w2_pb = w2_p[:].bitcast(U8)
         w2s_pb = w2s_p[:].bitcast(U8)
 
         gathered = {}
 
-        half = SLOTS // 2
-        slot_scales = []
+        slot_scales = {}
+        picked = {}
 
         def gather_scales(c):
-            gs = keep.tile([P, half], U8, name="gs_%d" % c, align_bytes=64)
-            nc.vector.tensor_copy(gs[:], xs_b.indirect(offs_t[:, half // 16 * c : half // 16 * (c + 1)]))
-            nc.sync.dma_start(out=moved[c][0:112, :], in_=gs[:].bitcast(I32)[4:116, :])
-            slot_scales.append((gs[:], moved[c][:].bitcast(U8)))
+            e0, e1 = chunks[c], chunks[c + 1]
+            gs = keep.tile([P, C * (e1 - e0)], U8, name="gs_%d" % c, align_bytes=64)
+            nc.vector.tensor_copy(gs[:], xs_b.indirect(offs_t[:, C // 16 * e0 : C // 16 * e1]))
+            picked[c] = gs
+
+        def move_scales(c):
+            e0, e1 = chunks[c], chunks[c + 1]
+            gs = picked[c]
+            eng[CFG["queue"].get("move", "y")].dma_start(out=moved[c][0:112, :], in_=gs[:].bitcast(I32)[4:116, :])
+            for e in range(e0, e1):
+                cols = slice(C * (e - e0), C * (e - e0 + 1))
+                slot_scales[e] = (gs[:, cols], moved[c][:].bitcast(U8)[:, cols])
 
         def gather(g):
             cols = offs_t[:, 16 * g : 16 * (g + 1)]
@@ -148,38 +185,52 @@ def tile_moe_shf_mlp_silu_kernel(
                 nc.vector.tensor_copy(gw[:], xw[:, T * s : T * (s + 1)].bitcast(U32).indirect(cols))
                 gathered[(g, s)] = gw
 
-        units = [[("s", 0, 0), ("s", 1, 0)], [("s", 2, 0), ("s", 3, 0)], [("s", 4, 0)]]
-        units += [[("r", 2 * g, 0), ("r", 2 * g + 1, 0)] for g in range(E // 2)]
-        units += [[("s", 0, 1), ("s", 1, 1)], [("s", 2, 1), ("s", 3, 1)], [("s", 4, 1)]]
-        turn_on_vector = (5, 6, 7)
+        units = CFG["units"]
+        turn_on_vector = CFG["tv"]
+        groups = {}
         hidden = {}
         codes = {}
 
-        w1s_perm = keep.tile([P, PASSES * W], I32, name="w1s_perm", align_bytes=64)
-        w1s_perm_p = keep.tile([P, W], U8, name="w1s_perm_p", align_bytes=64)
+        turned_halves = CFG["A"]
+        w1s_perm = {h: keep.tile([P, PASSES * W], I32, name="w1s_perm_%d" % h, align_bytes=64) for h in turned_halves}
+        w1s_perm_p = {h: keep.tile([P, W], U8, name="w1s_perm_p_%d" % h, align_bytes=64) for h in turned_halves}
 
-        def permute_w1s():
+        def permute_scales(h):
             nc.vector.tensor_copy(
-                w1s_perm_p[:].rearrange("p (t m) -> p t m", t=4),
-                w1s_pb[:, W : 2 * W].rearrange("p (m t) -> p t m", t=4),
+                w1s_perm_p[h][:].rearrange("p (t m) -> p t m", t=4),
+                w1s_pb[:, W * h : W * (h + 1)].rearrange("p (m t) -> p t m", t=4),
             )
+
+        def permute_words(h):
             nc.vector.tensor_copy(
-                w1s_perm[:].rearrange("p (s t a i) -> p s a t i", s=PASSES, t=4, i=4),
-                w1s_t[1][:].rearrange("p (s a i t) -> p s a t i", s=PASSES, t=4, i=4),
+                w1s_perm[h][:].rearrange("p (s t a i) -> p s a t i", s=PASSES, t=4, i=4),
+                w1s_t[h][:].rearrange("p (s a i t) -> p s a t i", s=PASSES, t=4, i=4),
             )
 
         def first_layer(u):
             hb = work.tile([P, 2 * W], BF16, name="hb", align_bytes=64)
+            accs = [psum.tile([P, W], F32, name="acc", bufs=CFG["bufs"][0]) for b in units[u]]
+            early = u in CFG["pm"]
+            if early:
+                for b, (kind, j, h) in enumerate(units[u]):
+                    nc.tensor.matmul_mx(
+                        out=accs[b][:],
+                        lhsT=xw[:, P * j : P * (j + 1)].bitcast(FP8X4),
+                        lhsT_scale=xs_b[0:P, P * j : P * (j + 1)],
+                        rhs=w1s_t[h][:, 0:W].bitcast(FP8X4),
+                        rhs_scale=w1s_pb[0:P, W * h : W * (h + 1)],
+                        start=True, stop=False,
+                    )
             for b, (kind, j, h) in enumerate(units[u]):
-                acc = psum.tile([P, W], F32, name="acc", bufs=4)
-                if h == 1:
+                acc = accs[b]
+                if kind == "s" and h in turned_halves:
                     for t in range(4):
                         for s in range(PASSES):
                             c0 = T * s + P * j
                             nc.tensor.matmul_mx(
                                 out=acc[:, P * t : P * (t + 1)],
-                                lhsT=w1s_perm[:, W * s + P * t : W * s + P * (t + 1)].bitcast(FP8X4),
-                                lhsT_scale=w1s_perm_p[4 * s : P, P * t : P * (t + 1)],
+                                lhsT=w1s_perm[h][:, W * s + P * t : W * s + P * (t + 1)].bitcast(FP8X4),
+                                lhsT_scale=w1s_perm_p[h][4 * s : P, P * t : P * (t + 1)],
                                 rhs=xw[:, c0 : c0 + P].bitcast(FP8X4),
                                 rhs_scale=xs_b[4 * s : P, P * j : P * (j + 1)],
                                 start=(s == 0), stop=(s == PASSES - 1),
@@ -190,7 +241,7 @@ def tile_moe_shf_mlp_silu_kernel(
                         SILU,
                     )
                     continue
-                for s in range(PASSES):
+                for s in range(int(early), PASSES):
                     if kind == "s":
                         c0 = T * s + P * j
                         nc.tensor.matmul_mx(
@@ -203,15 +254,15 @@ def tile_moe_shf_mlp_silu_kernel(
                         )
                     else:
                         gw = gathered[(j // 2, s)]
-                        gs = slot_scales[j // 5][s]
+                        gs = slot_scales[j][s]
                         a = PASSES * (j % 2) + s
-                        es = PASSES * j + s
+                        es = PASSES * (j - split * int(j >= split)) + s
                         nc.tensor.matmul_mx(
                             out=acc[:],
                             lhsT=gw[:, C * (j % 2) : C * (j % 2 + 1)].bitcast(FP8X4),
-                            lhsT_scale=gs[:, C * (j % 5) : C * (j % 5 + 1)],
+                            lhsT_scale=gs,
                             rhs=w1_t[j // 2][:, 2 * H * a : 2 * H * (a + 1)].bitcast(FP4X4),
-                            rhs_scale=w1_pb[:, H * es : H * (es + 1)],
+                            rhs_scale=w1_planes[int(j >= split)][:, H * es : H * (es + 1)],
                             start=(s == 0), stop=(s == PASSES - 1),
                         )
                 nc.scalar.activation(
@@ -223,11 +274,11 @@ def tile_moe_shf_mlp_silu_kernel(
 
         def turn(u):
             nb = len(units[u])
-            if units[u][0][2] == 1:
+            if units[u][0][0] == "s" and units[u][0][2] in turned_halves:
                 grouped = hidden[u]
             else:
                 words = hidden[u][:].bitcast(F32)
-                turned = psum.tile([P, W], F32, name="turned", bufs=1)
+                turned = psum.tile([P, W], F32, name="turned", bufs=CFG["bufs"][1])
                 for j in range(2 * nb):
                     nc.tensor.transpose(turned[:, P * j : P * (j + 1)], words[:, P * j : P * (j + 1)], ident[:])
                 grouped = work.tile([P, 2 * W], BF16, name="grouped", align_bytes=64)
@@ -237,30 +288,43 @@ def tile_moe_shf_mlp_silu_kernel(
                     nc.vector.tensor_copy(dst, src)
                 else:
                     nc.scalar.copy(dst, src)
+            groups[u] = grouped
+
+        def quantize(u):
+            nb = len(units[u])
+            grouped = groups[u]
             hw = keep.tile([P, nb * P], U32, name="hw_%d" % u, align_bytes=64)
             hs = keep.tile([P, nb * P], U8, name="hs_%d" % u, align_bytes=64)
             nc.vector.quantize_mx(out=hw[:].bitcast(FP8X4), scales=hs[:], in_=grouped[:, 0 : W * nb])
             for b, blk in enumerate(units[u]):
                 codes[blk] = (hw[:, P * b : P * (b + 1)], hs[:, P * b : P * (b + 1)])
 
+        parts = {}
         combined = {}
+        shared_sums = {}
+
+        def fetch(t0, t1, r):
+            part = keep.tile([P, t1 - t0], F32, name="part_%d_%d" % (t0, r))
+            nc.vector.tensor_tensor(
+                part[:], y_sb[:].indirect((pos1_t, pos2_t)[r][:, t0 // 16 : t1 // 16]),
+                gate_t[:, T * r + t0 : T * r + t1], MULT,
+            )
+            parts[(t0, r)] = part
 
         def combine(t0, t1):
-            parts = []
-            for r, pos_t in enumerate((pos1_t, pos2_t)):
-                part = keep.tile([P, t1 - t0], F32, name="part_%d_%d" % (t0, r))
-                nc.vector.tensor_tensor(
-                    part[:], y_sb[:].indirect(pos_t[:, t0 // 16 : t1 // 16]), gate_t[:, T * r + t0 : T * r + t1], MULT
-                )
-                parts.append(part)
             both = keep.tile([P, t1 - t0], F32, name="both_%d" % t0)
-            nc.vector.tensor_tensor(both[:], parts[0][:], parts[1][:], ADD)
+            nc.vector.tensor_tensor(both[:], parts[(t0, 0)][:], parts[(t0, 1)][:], ADD)
             combined[t0] = both
+
+        def finish(t0, t1):
+            res = keep.tile([P, t1 - t0], F32, name="res_%d" % t0)
+            nc.vector.tensor_tensor(res[:], shared_sums[t0][:, 0 : t1 - t0], combined[t0][:], ADD)
+            nc.sync.dma_start(out[:, t0:t1], res[:])
 
         def second_layer(u):
             blocks = units[u]
             if blocks[0][0] == "r":
-                y = psum.tile([P, 2 * C], F32, name="y", bufs=3)
+                y = psum.tile([P, 2 * C], F32, name="y", bufs=CFG["bufs"][2])
                 for b, blk in enumerate(blocks):
                     e = blk[1]
                     hw, hs = codes[blk]
@@ -271,12 +335,15 @@ def tile_moe_shf_mlp_silu_kernel(
                         rhs=hw.bitcast(FP8X4), rhs_scale=hs, start=True, stop=True,
                     )
                 e0 = blocks[0][1]
-                nc.scalar.copy(y_sb[:, C * e0 : C * (e0 + 2)], y[:])
+                if u in CFG["yv"]:
+                    nc.vector.tensor_copy(y_sb[:, C * e0 : C * (e0 + 2)], y[:])
+                else:
+                    nc.scalar.copy(y_sb[:, C * e0 : C * (e0 + 2)], y[:])
                 return
-            tiles = [j for (kind, j, h) in blocks if h == 1]
+            tiles = CFG["fin"].get(u, [])
             if not tiles:
                 return
-            y = psum.tile([P, 2 * C], F32, name="y", bufs=3)
+            y = psum.tile([P, 2 * C], F32, name="y", bufs=CFG["bufs"][2])
             for b, j in enumerate(tiles):
                 for h in range(2):
                     hw, hs = codes[("s", j, h)]
@@ -286,24 +353,9 @@ def tile_moe_shf_mlp_silu_kernel(
                         lhsT_scale=w2s_pb[:, N * h : N * (h + 1)],
                         rhs=hw.bitcast(FP8X4), rhs_scale=hs, start=(h == 0), stop=(h == 1),
                     )
-            t0 = P * tiles[0]
-            width = P * len(tiles)
-            combine(t0, t0 + width)
-            res = keep.tile([P, width], F32, name="res_%d" % t0)
-            nc.vector.tensor_tensor(res[:], y[:, 0:width], combined[t0][:], ADD)
-            nc.sync.dma_start(out[:, t0 : t0 + width], res[:])
+            shared_sums[P * tiles[0]] = y
 
-        n_units = len(units)
-        for step in range(n_units + 2):
-            if step in (0, 3):
-                gather_scales(step // 3)
-            if step == 7:
-                permute_w1s()
-            if step < n_units:
-                if units[step][0][0] == "r":
-                    gather(units[step][0][1] // 2)
-                first_layer(step)
-            if 0 <= step - 1 < n_units:
-                turn(step - 1)
-            if 0 <= step - 2 < n_units:
-                second_layer(step - 2)
+        steps = {"ld": load, "sg": gather_scales, "mv": move_scales, "g": gather, "l1": first_layer, "t": turn, "q": quantize,
+                 "l2": second_layer, "ps": permute_scales, "pw": permute_words, "ad": combine, "ft": fetch, "fin": finish}
+        for item in CFG["plan"]:
+            steps[item[0]](*item[1:])

@@ -23,7 +23,7 @@ W = 512
 PASSES = 2
 SLOTS = E * C
 XS_WINDOW = 1024
-CFG = {'ms': 'ggvvvvv', 'w1p_split': 4, 'chunks': [0, 6, 10], 'queue': {'w1pa': 'y', 'w1pb': 'g', 'w2p': 'y', 'w2sp': 'g', 'move': 'y', 'w2s': 'y'}, 'w1sp_q': 'yyyy', 'units': [[('s', 0, 0), ('s', 1, 0)], [('s', 2, 0), ('s', 3, 0)], [('r', 0, 0), ('r', 1, 0)], [('r', 2, 0), ('r', 3, 0)], [('r', 4, 0), ('r', 5, 0)], [('r', 6, 0), ('r', 7, 0)], [('r', 8, 0), ('r', 9, 0)], [('s', 4, 0)], [('s', 0, 1), ('s', 1, 1)], [('s', 2, 1), ('s', 3, 1)], [('s', 4, 1)]], 'tv': [5, 7], 'yv': [2, 6], 'pm': [0], 'fin': {8: [0, 1], 9: [2, 3], 10: [4]}, 'A': [1], 'bufs': [4, 2, 2], 'plan': [('ld', 'offs'), ('ld', 'xs'), ('ld', 'x0'), ('ld', 'w0a'), ('ld', 'w1sp'), ('ld', 'x1'), ('ld', 'w0b'), ('sg', 0), ('ld', 'w1_0'), ('ld', 'w1pa'), ('mv', 0), ('ld', 'w1_1'), ('ld', 'w2'), ('ld', 'w1pb'), ('ld', 'w1_2'), ('ld', 'w2p'), ('ld', 'w1_3'), ('sg', 1), ('mv', 1), ('ld', 'w1_4'), ('ld', 'w1s1'), ('ld', 'w2s'), ('ld', 'w2sp'), ('ld', 'pos1'), ('ld', 'pos2'), ('ld', 'gate'), ('g', 0), ('l1', 0), ('g', 1), ('l1', 1), ('t', 0), ('g', 2), ('l1', 2), ('q', 0), ('t', 1), ('g', 3), ('l1', 3), ('q', 1), ('t', 2), ('l2', 0), ('g', 4), ('l1', 4), ('q', 2), ('t', 3), ('l2', 1), ('l1', 5), ('q', 3), ('t', 4), ('l2', 2), ('ps', 1), ('pw', 1), ('l1', 6), ('q', 4), ('t', 5), ('l2', 3), ('l1', 7), ('q', 5), ('t', 6), ('l2', 4), ('l1', 8), ('q', 6), ('t', 7), ('l2', 5), ('l1', 9), ('q', 7), ('t', 8), ('l2', 6), ('ft', 0, 256, 0), ('l1', 10), ('q', 8), ('ft', 0, 256, 1), ('t', 9), ('l2', 7), ('ft', 256, 512, 0), ('q', 9), ('ad', 0, 256), ('t', 10), ('l2', 8), ('ft', 256, 512, 1), ('q', 10), ('fin', 0, 256), ('l2', 9), ('ft', 512, 640, 0), ('l2', 10), ('ad', 256, 512), ('ft', 512, 640, 1), ('fin', 256, 512), ('ad', 512, 640), ('fin', 512, 640)]}
+CFG = {'ms': 'ggvvvgg', 'w1p_split': 4, 'chunks': [0, 5, 10], 'queue': {'w1pa': 'y', 'w1pb': 'g', 'w2p': 'y', 'w2sp': 'y', 'move': 'g', 'w2s': 'y'}, 'w1sp_q': 'yyyy', 'units': [[('s', 0, 0), ('s', 1, 0)], [('s', 2, 0), ('s', 3, 0)], [('r', 0, 0), ('r', 1, 0)], [('r', 2, 0), ('r', 3, 0)], [('r', 4, 0), ('r', 5, 0)], [('r', 6, 0), ('r', 7, 0)], [('r', 8, 0), ('r', 9, 0)], [('s', 4, 0)], [('s', 0, 1), ('s', 1, 1)], [('s', 2, 1), ('s', 3, 1)], [('s', 4, 1)]], 'tv': [3, 4, 5, 6], 'yv': [], 'pm': [0], 'fin': {8: [0, 1], 9: [2, 3], 10: [4]}, 'A': [1], 'bufs': [4, 2, 2], 'perm_slot': 4, 'plan': [('ld', 'offs'), ('ld', 'xs'), ('ld', 'x0'), ('ld', 'w0a'), ('ld', 'w1sp'), ('ld', 'x1'), ('ld', 'w0b'), ('ld', 'w1pa'), ('sg', 0), ('mv', 0), ('ld', 'w1pb'), ('ld', 'w1_0'), ('ld', 'w1_1'), ('ld', 'w1_2'), ('ld', 'w1_3'), ('ld', 'w2p'), ('ld', 'w2'), ('ld', 'w1_4'), ('ld', 'w1s1'), ('ld', 'gate'), ('ld', 'pos1'), ('ld', 'pos2'), ('ld', 'w2s'), ('ld', 'w2sp'), ('g', 0), ('l1', 0), ('l1', 1), ('t', 0), ('g', 1), ('sg', 1), ('mv', 1), ('l1', 2), ('t', 1), ('g', 2), ('l1', 3), ('t', 2), ('g', 3), ('g', 4), ('q', 0), ('q', 1), ('ps', 1), ('l1', 4), ('t', 3), ('q', 2), ('l1', 5), ('t', 4), ('q', 3), ('l2', 2), ('l1', 6), ('t', 5), ('q', 4), ('l2', 3), ('l1', 7), ('t', 6), ('q', 5), ('l2', 4), ('pw', 1), ('q', 6), ('l2', 5), ('t', 7), ('l2', 6), ('l1', 8), ('t', 8), ('l1', 9), ('t', 9), ('l1', 10), ('t', 10), ('q', 7), ('ft', 0, 256, 0), ('ft', 0, 256, 1), ('ft', 256, 512, 0), ('ft', 256, 512, 1), ('q', 8), ('l2', 8), ('ft', 512, 640, 0), ('ft', 512, 640, 1), ('q', 9), ('l2', 9), ('ad', 0, 256), ('ad', 256, 512), ('q', 10), ('l2', 10), ('fin', 0, 256), ('ad', 512, 640), ('fin', 256, 512), ('fin', 512, 640)]}
 
 
 def tile_moe_shf_mlp_silu_kernel(
@@ -192,7 +192,7 @@ def tile_moe_shf_mlp_silu_kernel(
         codes = {}
 
         turned_halves = CFG["A"]
-        w1s_perm = {h: keep.tile([P, PASSES * W], I32, name="w1s_perm_%d" % h, align_bytes=64) for h in turned_halves}
+        w1s_perm = {}
         w1s_perm_p = {h: keep.tile([P, W], U8, name="w1s_perm_p_%d" % h, align_bytes=64) for h in turned_halves}
 
         def permute_scales(h):
@@ -202,6 +202,9 @@ def tile_moe_shf_mlp_silu_kernel(
             )
 
         def permute_words(h):
+            w1s_perm[h] = ring.tile(
+                [P, PASSES * W], I32, name="w1s_perm_%d" % h, tag="slot_%d" % CFG.get("perm_slot", 9), align_bytes=64
+            )
             nc.vector.tensor_copy(
                 w1s_perm[h][:].rearrange("p (s t a i) -> p s a t i", s=PASSES, t=4, i=4),
                 w1s_t[h][:].rearrange("p (s a i t) -> p s a t i", s=PASSES, t=4, i=4),

@@ -22,8 +22,9 @@ P = 128
 W = 512
 PASSES = 2
 SLOTS = E * C
-XS_WINDOW = 1024
-CFG = {'ms': 'ggvvvgg', 'w1p_split': 4, 'chunks': [0, 5, 10], 'queue': {'w1pa': 'y', 'w1pb': 'g', 'w2p': 'y', 'w2sp': 'y', 'move': 'g', 'w2s': 'y'}, 'w1sp_q': 'yyyy', 'units': [[('s', 0, 0), ('s', 1, 0)], [('s', 2, 0), ('s', 3, 0)], [('r', 0, 0), ('r', 1, 0)], [('r', 2, 0), ('r', 3, 0)], [('r', 4, 0), ('r', 5, 0)], [('r', 6, 0), ('r', 7, 0)], [('r', 8, 0), ('r', 9, 0)], [('s', 4, 0)], [('s', 0, 1), ('s', 1, 1)], [('s', 2, 1), ('s', 3, 1)], [('s', 4, 1)]], 'tv': [3, 4, 5, 6], 'yv': [], 'pm': [0], 'fin': {8: [0, 1], 9: [2, 3], 10: [4]}, 'A': [1], 'bufs': [4, 2, 2], 'perm_slot': 4, 'plan': [('ld', 'offs'), ('ld', 'xs'), ('ld', 'x0'), ('ld', 'w0a'), ('ld', 'w1sp'), ('ld', 'x1'), ('ld', 'w0b'), ('ld', 'w1pa'), ('sg', 0), ('mv', 0), ('ld', 'w1pb'), ('ld', 'w1_0'), ('ld', 'w1_1'), ('ld', 'w1_2'), ('ld', 'w1_3'), ('ld', 'w2p'), ('ld', 'w2'), ('ld', 'w1_4'), ('ld', 'w1s1'), ('ld', 'gate'), ('ld', 'pos1'), ('ld', 'pos2'), ('ld', 'w2s'), ('ld', 'w2sp'), ('g', 0), ('l1', 0), ('l1', 1), ('t', 0), ('g', 1), ('sg', 1), ('mv', 1), ('l1', 2), ('t', 1), ('g', 2), ('l1', 3), ('t', 2), ('g', 3), ('g', 4), ('q', 0), ('q', 1), ('ps', 1), ('l1', 4), ('t', 3), ('q', 2), ('l1', 5), ('t', 4), ('q', 3), ('l2', 2), ('l1', 6), ('t', 5), ('q', 4), ('l2', 3), ('l1', 7), ('t', 6), ('q', 5), ('l2', 4), ('pw', 1), ('q', 6), ('l2', 5), ('t', 7), ('l2', 6), ('l1', 8), ('t', 8), ('l1', 9), ('t', 9), ('l1', 10), ('t', 10), ('q', 7), ('ft', 0, 256, 0), ('ft', 0, 256, 1), ('ft', 256, 512, 0), ('ft', 256, 512, 1), ('q', 8), ('l2', 8), ('ft', 512, 640, 0), ('ft', 512, 640, 1), ('q', 9), ('l2', 9), ('ad', 0, 256), ('ad', 256, 512), ('q', 10), ('l2', 10), ('fin', 0, 256), ('ad', 512, 640), ('fin', 256, 512), ('fin', 512, 640)]}
+PAIR = 2 * PASSES * 2 * H
+XS_WINDOW = 1792
+CFG = {'queue': {'w2p': 'g', 'w2sp': 'g'}, 'gch': [0, 2, 4, 6, 8, 10], 'w1sp_q': 'yyyy', 'units': [[('s', 0, 0), ('s', 1, 0)], [('s', 2, 0), ('s', 3, 0)], [('s', 4, 0)], [('r', 0, 0), ('r', 1, 0)], [('r', 2, 0), ('r', 3, 0)], [('r', 4, 0), ('r', 5, 0)], [('r', 6, 0), ('r', 7, 0)], [('r', 8, 0), ('r', 9, 0)], [('s', 0, 1), ('s', 1, 1)], [('s', 2, 1), ('s', 3, 1)], [('s', 4, 1)]], 'tv': [5, 6, 7], 'yv': [], 'pm': [0], 'fin': {8: [0, 1], 9: [2, 3], 10: [4]}, 'A': [1], 'bufs': [4, 2, 2], 'perm_slot': 4, 'plan': [('setup',), ('ld', 'offs'), ('ld', 'xs'), ('ld', 'x0'), ('ld', 'w0a'), ('ld', 'w1sp'), ('ld', 'x1'), ('ld', 'w0b'), ('ld', 'w1pa'), ('ld', 'w2p'), ('sg',), ('late',), ('ld', 'w1_0'), ('ld', 'w1_1'), ('ld', 'w1_2'), ('ld', 'w1_3'), ('ld', 'w2'), ('ld', 'w1_4'), ('ld', 'w1s1'), ('ld', 'w2s'), ('ld', 'pos1'), ('ld', 'pos2'), ('ld', 'w2sp'), ('g', 0, 0), ('g', 0, 1), ('l1', 0), ('g', 1, 0), ('g', 1, 1), ('l1', 1), ('t', 0), ('g', 2, 0), ('g', 2, 1), ('l1', 2), ('t', 1), ('q', 0), ('g', 3, 0), ('g', 3, 1), ('l1', 3), ('t', 2), ('q', 1), ('g', 4, 0), ('g', 4, 1), ('l1', 4), ('ld', 'gate'), ('t', 3), ('q', 2), ('ps', 1), ('l1', 5), ('q', 3), ('t', 4), ('l1', 6), ('q', 4), ('t', 5), ('l2', 3), ('l1', 7), ('q', 5), ('t', 6), ('l2', 4), ('pw', 1), ('q', 6), ('t', 7), ('l2', 5), ('l1', 8), ('t', 8), ('q', 7), ('l2', 6), ('l2', 7), ('l1', 9), ('t', 9), ('l1', 10), ('t', 10), ('q', 8), ('ft', 0, 256, 0), ('ft', 0, 256, 1), ('l2', 8), ('ft', 256, 512, 0), ('ad', 0, 256), ('q', 9), ('ft', 256, 512, 1), ('fin', 0, 256), ('l2', 9), ('ft', 512, 640, 0), ('ad', 256, 512), ('q', 10), ('ft', 512, 640, 1), ('fin', 256, 512), ('l2', 10), ('ad', 512, 640), ('fin', 512, 640)]}
 
 
 def tile_moe_shf_mlp_silu_kernel(
@@ -65,38 +66,44 @@ def tile_moe_shf_mlp_silu_kernel(
         xw = keep.tile([P, PASSES * T], I32, name="xw", align_bytes=64)
         w1s_t = {}
         w1_t = {}
-        w2s_t = keep.tile([P, 2 * N], I32, name="w2s_t", align_bytes=64)
         ident = keep.tile([P, P], F32, name="ident")
         y_sb = keep.tile([P, SLOTS], F32, name="y_sb")
 
         eng = {"v": nc.vector, "g": nc.gpsimd, "y": nc.sync, "s": nc.scalar}
-        xs = plane("xs", XS_WINDOW, eng[CFG["ms"][0]])
-        w1s_p = plane("w1s_p", HS, eng[CFG["ms"][1]])
-        split = CFG["w1p_split"]
-        w1_pa = plane("w1_pa", split * PASSES * H, eng[CFG["ms"][2]])
-        chunks = CFG["chunks"]
-        moved = [plane("moved_%d" % c, C * (chunks[c + 1] - chunks[c]), eng[CFG["ms"][3]]) for c in range(len(chunks) - 1)]
-        w1_pb = plane("w1_pb", (E - split) * PASSES * H, eng[CFG["ms"][4]]) if split < E else None
-        w2_p = plane("w2_p", E * N, eng[CFG["ms"][5]])
-        w2s_p = plane("w2s_p", 2 * N, eng[CFG["ms"][6]])
-        warm = keep.tile([P, 8], F32, name="warm")
-        nc.gpsimd.memset(warm[:], 0.0)
-        nc.scalar.activation(warm[:], warm[:], SILU)
+        window = ring.tile([P, XS_WINDOW // 4], I32, name="window", tag="late", align_bytes=64)
+        nc.gpsimd.memset(window[:], 0)
+        w1s_p = plane("w1s_p", HS, nc.gpsimd)
+        split = E
+        w1_pa = plane("w1_pa", E * PASSES * H, nc.vector)
         make_identity(nc, ident[:])
-        w2_t = keep.tile([P, E * 2 * N], U8, name="w2_t", align_bytes=64)
-        gate_t = keep.tile([P, 2 * T], F32, name="gate_t", align_bytes=64)
+        w2_p = plane("w2_p", E * N, nc.gpsimd)
+        warm = keep.tile([P, 8], F32, name="warm")
+        nc.vector.memset(warm[:], 0.0)
+        nc.scalar.activation(warm[:], warm[:], SILU)
+        xs = keep.tile([P, T // 4], I32, name="xs", align_bytes=64)
+        held = {}
+
+        def open_late():
+            late = ring.tile([P, 6 * PAIR + 2 * E * N + 8 * N], U8, name="late", tag="late", align_bytes=64)
+            for g in range(E // 2):
+                w1_t[g] = late[:, PAIR * g : PAIR * (g + 1)]
+            w1s_t[1] = late[:, 5 * PAIR : 6 * PAIR].bitcast(I32)
+            held["w2"] = late[:, 6 * PAIR : 6 * PAIR + 2 * E * N]
+            held["w2s"] = late[:, 6 * PAIR + 2 * E * N : 6 * PAIR + 2 * E * N + 8 * N].bitcast(I32)
+
+        def setup():
+            held["moved"] = plane("moved", SLOTS, nc.vector)
+            held["w2s_p"] = plane("w2s_p", 2 * N, nc.vector)
 
         def load_w1s(h):
-            w1s_t[h] = ring.tile([P, PASSES * W], I32, name="w1s_%d" % h, tag="slot_%d" % (5 + h), align_bytes=64)
             nc.sync.dma_start(
-                out=w1s_t[h][:].rearrange("p (s l) -> p s l", s=PASSES),
+                out=w1s_t[h].rearrange("p (s l) -> p s l", s=PASSES),
                 in_=w1s_words.rearrange("s p l d -> p s (l d)")[:, :, 4 * W * h : 4 * W * (h + 1)].bitcast(I32),
             )
 
         def load_w1(g):
-            w1_t[g] = ring.tile([P, 2 * PASSES * 2 * H], U8, name="w1_%d" % g, tag="slot_%d" % g, align_bytes=64)
             nc.sync.dma_start(
-                out=w1_t[g][:].bitcast(I32).rearrange("p (a b) -> p a b", a=2 * PASSES),
+                out=w1_t[g].bitcast(I32).rearrange("p (a b) -> p a b", a=2 * PASSES),
                 in_=w1_words[2 * g : 2 * g + 2].rearrange("e s p b -> p (e s) b").bitcast(I32),
             )
 
@@ -117,21 +124,19 @@ def tile_moe_shf_mlp_silu_kernel(
                 s = int(name[1])
                 q.dma_start(out=xw[:, T * s : T * (s + 1)], in_=x_words[s].rearrange("p t d -> p (t d)").bitcast(I32))
             elif name == "xs":
-                load_packed_plane([q] * 4, xs, x_scales)
+                load_packed_plane([q] * 4, window, x_scales)
             elif name == "w1sp":
                 load_packed_plane([eng[c] for c in CFG["w1sp_q"]], w1s_p, w1s_scales)
             elif name == "w1pa":
                 load_plane([q] * 4, w1_pa, w1_scales[0:split].rearrange("e s b i -> (e s) b i"))
-            elif name == "w1pb":
-                load_plane([q] * 4, w1_pb, w1_scales[split:E].rearrange("e s b i -> (e s) b i"))
             elif name == "w2p":
                 load_plane([q] * 4, w2_p, w2_scales.rearrange("e s b i -> (e s) b i"))
             elif name == "w2sp":
-                load_plane([q] * 4, w2s_p, w2s_scales)
+                load_plane([q] * 4, held["w2s_p"], w2s_scales)
             elif name in ("w0a", "w0b"):
                 s = int(name == "w0b")
                 if s == 0:
-                    w1s_t[0] = ring.tile([P, PASSES * W], I32, name="w1s_0", tag="slot_5", align_bytes=64)
+                    w1s_t[0] = ring.tile([P, PASSES * W], I32, name="w1s_0", align_bytes=64)[:]
                 q.dma_start(
                     out=w1s_t[0][:, W * s : W * (s + 1)],
                     in_=w1s_words[s].rearrange("p l d -> p (l d)")[:, 0 : 4 * W].bitcast(I32),
@@ -142,48 +147,46 @@ def tile_moe_shf_mlp_silu_kernel(
                 load_w1(int(name[3]))
             elif name == "w2":
                 q.dma_start(
-                    out=w2_t[:].bitcast(I32).rearrange("p (e b) -> p e b", e=E),
+                    out=held["w2"].bitcast(I32).rearrange("p (e b) -> p e b", e=E),
                     in_=w2_words.rearrange("e s p b -> p (e s) b").bitcast(I32),
                 )
             elif name == "w2s":
                 q.dma_start(
-                    out=w2s_t[:].rearrange("p (s n) -> p s n", s=2),
+                    out=held["w2s"].rearrange("p (s n) -> p s n", s=2),
                     in_=w2s_words.rearrange("s p n d -> p s (n d)").bitcast(I32),
                 )
             elif name == "gate":
-                q.dma_start(out=gate_t[:].rearrange("p (r t) -> p r t", r=2), in_=gate.rearrange("r p t -> p r t"))
+                held["gate"] = ring.tile([P, 2 * T], F32, name="gate_t", tag="gw_0_0", align_bytes=64)
+                q.dma_start(out=held["gate"][:].rearrange("p (r t) -> p r t", r=2), in_=gate.rearrange("r p t -> p r t"))
 
         xs_b = xs[:].bitcast(U8)
         w1s_pb = w1s_p[:].bitcast(U8)
-        w1_planes = [w1_pa[:].bitcast(U8), w1_pb[:].bitcast(U8) if split < E else None]
+        w1_planes = [w1_pa[:].bitcast(U8)]
         w2_pb = w2_p[:].bitcast(U8)
-        w2s_pb = w2s_p[:].bitcast(U8)
 
         gathered = {}
 
         slot_scales = {}
-        picked = {}
 
-        def gather_scales(c):
-            e0, e1 = chunks[c], chunks[c + 1]
-            gs = keep.tile([P, C * (e1 - e0)], U8, name="gs_%d" % c, align_bytes=64)
-            nc.vector.tensor_copy(gs[:], xs_b.indirect(offs_t[:, C // 16 * e0 : C // 16 * e1]))
-            picked[c] = gs
+        cuts = CFG["gch"]
 
-        def move_scales(c):
-            e0, e1 = chunks[c], chunks[c + 1]
-            gs = picked[c]
-            eng[CFG["queue"].get("move", "y")].dma_start(out=moved[c][0:112, :], in_=gs[:].bitcast(I32)[4:116, :])
+        def gather_scales():
+            nc.vector.tensor_copy(xs[:], window[:, 0 : T // 4])
+            gs = keep.tile([P, SLOTS], U8, name="gs", align_bytes=64)
+            nc.vector.tensor_copy(gs[:], window[:].bitcast(U8).indirect(offs_t[:]))
+            nc.sync.dma_start(out=held["moved"][0:112, :], in_=gs[:].bitcast(I32)[4:116, :])
+            for e in range(E):
+                slot_scales[(e, 0)] = gs[:, C * e : C * (e + 1)]
+                slot_scales[(e, 1)] = held["moved"][:].bitcast(U8)[:, C * e : C * (e + 1)]
+
+        def gather(g, s):
+            e0, e1 = cuts[g], cuts[g + 1]
+            gw = ring.tile([P, (e1 - e0) * C], U32, name="gw_%d_%d" % (g, s), tag="gw_%d_%d" % (g, s), align_bytes=64)
+            nc.vector.tensor_copy(
+                gw[:], xw[:, T * s : T * (s + 1)].bitcast(U32).indirect(offs_t[:, 8 * e0 : 8 * e1])
+            )
             for e in range(e0, e1):
-                cols = slice(C * (e - e0), C * (e - e0 + 1))
-                slot_scales[e] = (gs[:, cols], moved[c][:].bitcast(U8)[:, cols])
-
-        def gather(g):
-            cols = offs_t[:, 16 * g : 16 * (g + 1)]
-            for s in range(PASSES):
-                gw = keep.tile([P, 2 * C], U32, name="gw_%d_%d" % (g, s), align_bytes=64)
-                nc.vector.tensor_copy(gw[:], xw[:, T * s : T * (s + 1)].bitcast(U32).indirect(cols))
-                gathered[(g, s)] = gw
+                gathered[(e, s)] = gw[:, C * (e - e0) : C * (e - e0 + 1)]
 
         units = CFG["units"]
         turn_on_vector = CFG["tv"]
@@ -203,11 +206,11 @@ def tile_moe_shf_mlp_silu_kernel(
 
         def permute_words(h):
             w1s_perm[h] = ring.tile(
-                [P, PASSES * W], I32, name="w1s_perm_%d" % h, tag="slot_%d" % CFG.get("perm_slot", 9), align_bytes=64
+                [P, PASSES * W], I32, name="w1s_perm_%d" % h, tag="gw_%d_1" % CFG["perm_slot"], align_bytes=64
             )
             nc.vector.tensor_copy(
                 w1s_perm[h][:].rearrange("p (s t a i) -> p s a t i", s=PASSES, t=4, i=4),
-                w1s_t[h][:].rearrange("p (s a i t) -> p s a t i", s=PASSES, t=4, i=4),
+                w1s_t[h].rearrange("p (s a i t) -> p s a t i", s=PASSES, t=4, i=4),
             )
 
         def first_layer(u):
@@ -256,13 +259,13 @@ def tile_moe_shf_mlp_silu_kernel(
                             start=(s == 0), stop=(s == PASSES - 1),
                         )
                     else:
-                        gw = gathered[(j // 2, s)]
-                        gs = slot_scales[j][s]
+                        gw = gathered[(j, s)]
+                        gs = slot_scales[(j, s)]
                         a = PASSES * (j % 2) + s
                         es = PASSES * (j - split * int(j >= split)) + s
                         nc.tensor.matmul_mx(
                             out=acc[:],
-                            lhsT=gw[:, C * (j % 2) : C * (j % 2 + 1)].bitcast(FP8X4),
+                            lhsT=gw.bitcast(FP8X4),
                             lhsT_scale=gs,
                             rhs=w1_t[j // 2][:, 2 * H * a : 2 * H * (a + 1)].bitcast(FP4X4),
                             rhs_scale=w1_planes[int(j >= split)][:, H * es : H * (es + 1)],
@@ -310,7 +313,7 @@ def tile_moe_shf_mlp_silu_kernel(
             part = keep.tile([P, t1 - t0], F32, name="part_%d_%d" % (t0, r))
             nc.vector.tensor_tensor(
                 part[:], y_sb[:].indirect((pos1_t, pos2_t)[r][:, t0 // 16 : t1 // 16]),
-                gate_t[:, T * r + t0 : T * r + t1], MULT,
+                held["gate"][:, T * r + t0 : T * r + t1], MULT,
             )
             parts[(t0, r)] = part
 
@@ -333,7 +336,7 @@ def tile_moe_shf_mlp_silu_kernel(
                     hw, hs = codes[blk]
                     nc.tensor.matmul_mx(
                         out=y[:, C * b : C * (b + 1)],
-                        lhsT=w2_t[:, 2 * N * e : 2 * N * (e + 1)].bitcast(FP4X4),
+                        lhsT=held["w2"][:, 2 * N * e : 2 * N * (e + 1)].bitcast(FP4X4),
                         lhsT_scale=w2_pb[:, N * e : N * (e + 1)],
                         rhs=hw.bitcast(FP8X4), rhs_scale=hs, start=True, stop=True,
                     )
@@ -352,13 +355,13 @@ def tile_moe_shf_mlp_silu_kernel(
                     hw, hs = codes[("s", j, h)]
                     nc.tensor.matmul_mx(
                         out=y[:, P * b : P * (b + 1)],
-                        lhsT=w2s_t[:, N * h : N * (h + 1)].bitcast(FP8X4),
-                        lhsT_scale=w2s_pb[:, N * h : N * (h + 1)],
+                        lhsT=held["w2s"][:, N * h : N * (h + 1)].bitcast(FP8X4),
+                        lhsT_scale=held["w2s_p"][:].bitcast(U8)[:, N * h : N * (h + 1)],
                         rhs=hw.bitcast(FP8X4), rhs_scale=hs, start=(h == 0), stop=(h == 1),
                     )
             shared_sums[P * tiles[0]] = y
 
-        steps = {"ld": load, "sg": gather_scales, "mv": move_scales, "g": gather, "l1": first_layer, "t": turn, "q": quantize,
+        steps = {"ld": load, "sg": gather_scales, "late": open_late, "setup": setup, "g": gather, "l1": first_layer, "t": turn, "q": quantize,
                  "l2": second_layer, "ps": permute_scales, "pw": permute_words, "ad": combine, "ft": fetch, "fin": finish}
         for item in CFG["plan"]:
             steps[item[0]](*item[1:])

@@ -20,11 +20,17 @@ ADD = mybir.AluOpType.add
 
 P = 128
 W = 512
-PASSES = 2
+PASSES = K // W
 SLOTS = E * C
-PAIR = 2 * PASSES * 2 * H
-XS_WINDOW = 1792
-CFG = {'queue': {'w2p': 'g', 'w2sp': 'g'}, 'gch': [0, 2, 4, 6, 8, 10], 'w1sp_q': 'yyyy', 'units': [[('s', 0, 0), ('s', 1, 0)], [('s', 2, 0), ('s', 3, 0)], [('s', 4, 0)], [('r', 0, 0), ('r', 1, 0)], [('r', 2, 0), ('r', 3, 0)], [('r', 4, 0), ('r', 5, 0)], [('r', 6, 0), ('r', 7, 0)], [('r', 8, 0), ('r', 9, 0)], [('s', 0, 1), ('s', 1, 1)], [('s', 2, 1), ('s', 3, 1)], [('s', 4, 1)]], 'tv': [5, 6, 7], 'yv': [], 'pm': [0], 'fin': {8: [0, 1], 9: [2, 3], 10: [4]}, 'A': [1], 'bufs': [4, 2, 2], 'perm_slot': 4, 'plan': [('setup',), ('ld', 'offs'), ('ld', 'xs'), ('ld', 'x0'), ('ld', 'w0a'), ('ld', 'w1sp'), ('ld', 'x1'), ('ld', 'w0b'), ('ld', 'w1pa'), ('ld', 'w2p'), ('sg',), ('late',), ('ld', 'w1_0'), ('ld', 'w1_1'), ('ld', 'w1_2'), ('ld', 'w1_3'), ('ld', 'w2'), ('ld', 'w1_4'), ('ld', 'w1s1'), ('ld', 'w2s'), ('ld', 'pos1'), ('ld', 'pos2'), ('ld', 'w2sp'), ('g', 0, 0), ('g', 0, 1), ('l1', 0), ('g', 1, 0), ('g', 1, 1), ('l1', 1), ('t', 0), ('g', 2, 0), ('g', 2, 1), ('l1', 2), ('t', 1), ('q', 0), ('g', 3, 0), ('g', 3, 1), ('l1', 3), ('t', 2), ('q', 1), ('g', 4, 0), ('g', 4, 1), ('l1', 4), ('ld', 'gate'), ('t', 3), ('q', 2), ('ps', 1), ('l1', 5), ('q', 3), ('t', 4), ('l1', 6), ('q', 4), ('t', 5), ('l2', 3), ('l1', 7), ('q', 5), ('t', 6), ('l2', 4), ('pw', 1), ('q', 6), ('t', 7), ('l2', 5), ('l1', 8), ('t', 8), ('q', 7), ('l2', 6), ('l2', 7), ('l1', 9), ('t', 9), ('l1', 10), ('t', 10), ('q', 8), ('ft', 0, 256, 0), ('ft', 0, 256, 1), ('l2', 8), ('ft', 256, 512, 0), ('ad', 0, 256), ('q', 9), ('ft', 256, 512, 1), ('fin', 0, 256), ('l2', 9), ('ft', 512, 640, 0), ('ad', 256, 512), ('q', 10), ('ft', 512, 640, 1), ('fin', 256, 512), ('l2', 10), ('ad', 512, 640), ('fin', 512, 640)]}
+TILES = T // P
+EXPERT_BYTES = PASSES * 2 * H
+SCALE_WINDOW = 1024
+LIVE_ROWS = 100
+WORD_GATHERS = [(0, 3), (3, 6), (6, 8), (8, 10)]
+WEIGHT_LOADS = [(0, 1), (1, 3), (3, 5), (5, 7), (7, 9), (9, 10)]
+HEAD_TILES = 3
+TOKEN_CHUNKS = [(0, 4), (4, 5)]
+TURNS_ON_SCALAR = 1
 
 
 def tile_moe_shf_mlp_silu_kernel(
@@ -34,334 +40,289 @@ def tile_moe_shf_mlp_silu_kernel(
     nc = tc.nc
     with ExitStack() as ctx:
         keep = ctx.enter_context(tc.tile_pool(name="keep", bufs=1))
-        work = ctx.enter_context(tc.tile_pool(name="work", bufs=4))
         psum = ctx.enter_context(tc.psum_pool(name="psum", bufs=1))
 
-        ring = ctx.enter_context(tc.tile_pool(name="ring", bufs=1))
+        def zeroed_plane(name, nbytes, engine):
+            plane = keep.tile([P, nbytes // 4], I32, name=name, align_bytes=64)
+            engine.memset(plane[:], 0)
+            return plane
 
-        def plane(name, nbytes, engine):
-            t = keep.tile([P, nbytes // 4], I32, name=name, align_bytes=64)
-            engine.memset(t[:], 0)
-            return t
-
-        def load_plane(queues, t, rows):
+        def load_planes_side_by_side(queue, plane, rows):
             groups = rows.shape[0]
             src = rows.rearrange("g (q r) w -> r q g w", r=4)
             for r in range(4):
-                queues[r].dma_start(
-                    out=t[r:P:32, :].rearrange("q (g w) -> q g w", g=groups),
-                    in_=src[r].bitcast(I32),
+                queue.dma_start(
+                    out=plane[r:P:32, :].rearrange("q (g w) -> q g w", g=groups), in_=src[r].bitcast(I32)
                 )
 
-        def load_packed_plane(queues, t, rows):
+        def load_planes_stacked(queue, plane, rows):
             width = rows.shape[2] // 4
             for q in range(4):
-                queues[q].dma_start(
-                    out=t[32 * q : 32 * q + 8, 0:width], in_=rows[:, 4 * q : 4 * q + 4, :].bitcast(I32)
+                queue.dma_start(
+                    out=plane[32 * q : 32 * q + 8, 0:width], in_=rows[:, 4 * q : 4 * q + 4, :].bitcast(I32)
                 )
+
+        window = keep.tile([P, SCALE_WINDOW // 4], I32, name="window", align_bytes=64)
+        nc.gpsimd.memset(window[:, 0 : T // 4], 0)
+        w1s_plane = zeroed_plane("w1s_plane", HS, nc.gpsimd)
+        nc.gpsimd.memset(window[:, T // 4 :], 0)
+        w1_plane = zeroed_plane("w1_plane", E * PASSES * H, nc.vector)
+        moved = zeroed_plane("moved", SLOTS, nc.gpsimd)
+        ident = keep.tile([P, P], F32, name="ident")
+        make_identity(nc, ident[:])
+        w2_plane = zeroed_plane("w2_plane", E * N, nc.gpsimd)
+        w2s_plane = zeroed_plane("w2s_plane", 2 * N, nc.gpsimd)
 
         offs_t = keep.tile([P, SLOTS // 16], U16, name="offs_t")
-        pos1_t = keep.tile([P, T // 16], U16, name="pos1_t")
-        pos2_t = keep.tile([P, T // 16], U16, name="pos2_t")
+        nc.sync.dma_start(offs_t[:], offs)
+        load_planes_stacked(nc.sync, window, x_scales)
         xw = keep.tile([P, PASSES * T], I32, name="xw", align_bytes=64)
-        w1s_t = {}
-        w1_t = {}
-        ident = keep.tile([P, P], F32, name="ident")
-        y_sb = keep.tile([P, SLOTS], F32, name="y_sb")
-
-        eng = {"v": nc.vector, "g": nc.gpsimd, "y": nc.sync, "s": nc.scalar}
-        window = ring.tile([P, XS_WINDOW // 4], I32, name="window", tag="late", align_bytes=64)
-        nc.gpsimd.memset(window[:], 0)
-        w1s_p = plane("w1s_p", HS, nc.gpsimd)
-        split = E
-        w1_pa = plane("w1_pa", E * PASSES * H, nc.vector)
-        make_identity(nc, ident[:])
-        w2_p = plane("w2_p", E * N, nc.gpsimd)
-        warm = keep.tile([P, 8], F32, name="warm")
-        nc.vector.memset(warm[:], 0.0)
-        nc.scalar.activation(warm[:], warm[:], SILU)
-        xs = keep.tile([P, T // 4], I32, name="xs", align_bytes=64)
-        held = {}
-
-        def open_late():
-            late = ring.tile([P, 6 * PAIR + 2 * E * N + 8 * N], U8, name="late", tag="late", align_bytes=64)
-            for g in range(E // 2):
-                w1_t[g] = late[:, PAIR * g : PAIR * (g + 1)]
-            w1s_t[1] = late[:, 5 * PAIR : 6 * PAIR].bitcast(I32)
-            held["w2"] = late[:, 6 * PAIR : 6 * PAIR + 2 * E * N]
-            held["w2s"] = late[:, 6 * PAIR + 2 * E * N : 6 * PAIR + 2 * E * N + 8 * N].bitcast(I32)
-
-        def setup():
-            held["moved"] = plane("moved", SLOTS, nc.vector)
-            held["w2s_p"] = plane("w2s_p", 2 * N, nc.vector)
-
-        def load_w1s(h):
+        def load_w1s(dst, half):
             nc.sync.dma_start(
-                out=w1s_t[h].rearrange("p (s l) -> p s l", s=PASSES),
-                in_=w1s_words.rearrange("s p l d -> p s (l d)")[:, :, 4 * W * h : 4 * W * (h + 1)].bitcast(I32),
+                out=dst.rearrange("p (s l) -> p s l", s=PASSES),
+                in_=w1s_words.rearrange("s p l d -> p s (l d)")[:, :, 4 * W * half : 4 * W * (half + 1)].bitcast(I32),
             )
 
-        def load_w1(g):
-            nc.sync.dma_start(
-                out=w1_t[g].bitcast(I32).rearrange("p (a b) -> p a b", a=2 * PASSES),
-                in_=w1_words[2 * g : 2 * g + 2].rearrange("e s p b -> p (e s) b").bitcast(I32),
-            )
+        w1s_first = keep.tile([P, PASSES * W], I32, name="w1s_first", align_bytes=64)
+        load_w1s(w1s_first[:], 0)
+        nc.sync.dma_start(
+            out=xw[:].rearrange("p (s t) -> p s t", s=PASSES),
+            in_=x_words.rearrange("s p t d -> p s (t d)").bitcast(I32),
+        )
+        load_planes_stacked(nc.sync, w1s_plane, w1s_scales)
+        load_planes_side_by_side(nc.sync, w1_plane, w1_scales.rearrange("e s b i -> (e s) b i"))
 
-        def load(name):
-            q = eng[CFG["queue"].get(name, "y")]
-            if name == "offs":
-                nc.sync.dma_start(offs_t[:], offs)
-            elif name == "pos1":
-                nc.sync.dma_start(pos1_t[:], pos1)
-            elif name == "pos2":
-                nc.sync.dma_start(pos2_t[:], pos2)
-            elif name == "x":
-                q.dma_start(
-                    out=xw[:].rearrange("p (s t) -> p s t", s=PASSES),
-                    in_=x_words.rearrange("s p t d -> p s (t d)").bitcast(I32),
-                )
-            elif name in ("x0", "x1"):
-                s = int(name[1])
-                q.dma_start(out=xw[:, T * s : T * (s + 1)], in_=x_words[s].rearrange("p t d -> p (t d)").bitcast(I32))
-            elif name == "xs":
-                load_packed_plane([q] * 4, window, x_scales)
-            elif name == "w1sp":
-                load_packed_plane([eng[c] for c in CFG["w1sp_q"]], w1s_p, w1s_scales)
-            elif name == "w1pa":
-                load_plane([q] * 4, w1_pa, w1_scales[0:split].rearrange("e s b i -> (e s) b i"))
-            elif name == "w2p":
-                load_plane([q] * 4, w2_p, w2_scales.rearrange("e s b i -> (e s) b i"))
-            elif name == "w2sp":
-                load_plane([q] * 4, held["w2s_p"], w2s_scales)
-            elif name in ("w0a", "w0b"):
-                s = int(name == "w0b")
-                if s == 0:
-                    w1s_t[0] = ring.tile([P, PASSES * W], I32, name="w1s_0", align_bytes=64)[:]
-                q.dma_start(
-                    out=w1s_t[0][:, W * s : W * (s + 1)],
-                    in_=w1s_words[s].rearrange("p l d -> p (l d)")[:, 0 : 4 * W].bitcast(I32),
-                )
-            elif name.startswith("w1s"):
-                load_w1s(int(name[3]))
-            elif name.startswith("w1_"):
-                load_w1(int(name[3]))
-            elif name == "w2":
-                q.dma_start(
-                    out=held["w2"].bitcast(I32).rearrange("p (e b) -> p e b", e=E),
-                    in_=w2_words.rearrange("e s p b -> p (e s) b").bitcast(I32),
-                )
-            elif name == "w2s":
-                q.dma_start(
-                    out=held["w2s"].rearrange("p (s n) -> p s n", s=2),
-                    in_=w2s_words.rearrange("s p n d -> p s (n d)").bitcast(I32),
-                )
-            elif name == "gate":
-                held["gate"] = ring.tile([P, 2 * T], F32, name="gate_t", tag="gw_0_0", align_bytes=64)
-                q.dma_start(out=held["gate"][:].rearrange("p (r t) -> p r t", r=2), in_=gate.rearrange("r p t -> p r t"))
-
-        xs_b = xs[:].bitcast(U8)
-        w1s_pb = w1s_p[:].bitcast(U8)
-        w1_planes = [w1_pa[:].bitcast(U8)]
-        w2_pb = w2_p[:].bitcast(U8)
-
-        gathered = {}
-
-        slot_scales = {}
-
-        cuts = CFG["gch"]
-
-        def gather_scales():
-            nc.vector.tensor_copy(xs[:], window[:, 0 : T // 4])
-            gs = keep.tile([P, SLOTS], U8, name="gs", align_bytes=64)
-            nc.vector.tensor_copy(gs[:], window[:].bitcast(U8).indirect(offs_t[:]))
-            nc.sync.dma_start(out=held["moved"][0:112, :], in_=gs[:].bitcast(I32)[4:116, :])
-            for e in range(E):
-                slot_scales[(e, 0)] = gs[:, C * e : C * (e + 1)]
-                slot_scales[(e, 1)] = held["moved"][:].bitcast(U8)[:, C * e : C * (e + 1)]
-
-        def gather(g, s):
-            e0, e1 = cuts[g], cuts[g + 1]
-            gw = ring.tile([P, (e1 - e0) * C], U32, name="gw_%d_%d" % (g, s), tag="gw_%d_%d" % (g, s), align_bytes=64)
+        slot_scales = keep.tile([P, SLOTS], U8, name="slot_scales", align_bytes=64)
+        half = SLOTS // 2
+        for g in range(2):
             nc.vector.tensor_copy(
-                gw[:], xw[:, T * s : T * (s + 1)].bitcast(U32).indirect(offs_t[:, 8 * e0 : 8 * e1])
+                slot_scales[:, half * g : half * (g + 1)],
+                window[:].bitcast(U8).indirect(offs_t[:, half // 16 * g : half // 16 * (g + 1)]),
             )
+
+        def move_scale_rows(g):
+            cols = slice(half // 4 * g, half // 4 * (g + 1))
+            nc.sync.dma_start(out=moved[0:LIVE_ROWS, cols], in_=slot_scales[:].bitcast(I32)[4 : 4 + LIVE_ROWS, cols])
+
+        slot_planes = [slot_scales[:], moved[:].bitcast(U8)]
+
+        late = keep.tile([P, E * EXPERT_BYTES + 2 * E * N + 4 * PASSES * W + 8 * N], U8, name="late", align_bytes=64)
+        w1_t = late[:, 0 : E * EXPERT_BYTES]
+        w2_t = late[:, E * EXPERT_BYTES : E * EXPERT_BYTES + 2 * E * N]
+        at = E * EXPERT_BYTES + 2 * E * N
+        w1s_second = late[:, at : at + 4 * PASSES * W].bitcast(I32)
+        w2s_t = late[:, at + 4 * PASSES * W :].bitcast(I32)
+        for i, (e0, e1) in enumerate(WEIGHT_LOADS):
+            if i in (0, 2):
+                move_scale_rows(i // 2)
+            if i == 2:
+                load_w1s(w1s_second, 1)
+            nc.sync.dma_start(
+                out=w1_t[:, EXPERT_BYTES * e0 : EXPERT_BYTES * e1].bitcast(I32).rearrange("p (a b) -> p a b", a=PASSES * (e1 - e0)),
+                in_=w1_words[e0:e1].rearrange("e s p b -> p (e s) b").bitcast(I32),
+            )
+        load_planes_side_by_side(nc.sync, w2_plane, w2_scales.rearrange("e s b i -> (e s) b i"))
+        nc.sync.dma_start(
+            out=w2_t.bitcast(I32).rearrange("p (e b) -> p e b", e=E),
+            in_=w2_words.rearrange("e s p b -> p (e s) b").bitcast(I32),
+        )
+        gate_t = keep.tile([P, 2 * T], F32, name="gate_t")
+        nc.sync.dma_start(out=gate_t[:].rearrange("p (r t) -> p r t", r=2), in_=gate.rearrange("r p t -> p r t"))
+        pos_t = [keep.tile([P, T // 16], U16, name="pos%d_t" % (r + 1)) for r in range(2)]
+        nc.sync.dma_start(pos_t[0][:], pos1)
+        nc.sync.dma_start(pos_t[1][:], pos2)
+        nc.sync.dma_start(
+            out=w2s_t.rearrange("p (s n) -> p s n", s=2), in_=w2s_words.rearrange("s p n d -> p s (n d)").bitcast(I32)
+        )
+        load_planes_side_by_side(nc.sync, w2s_plane, w2s_scales)
+
+        xs_b = window[:].bitcast(U8)
+        w1s_plane_b = w1s_plane[:].bitcast(U8)
+        w1_plane_b = w1_plane[:].bitcast(U8)
+
+        slot_words = {}
+        for e0, e1 in WORD_GATHERS:
+            for s in range(PASSES):
+                name = "slot_words_%d_%d" % (e0, s)
+                gathered = keep.tile([P, (e1 - e0) * C], U32, name=name, tag=name, align_bytes=64)
+                nc.vector.tensor_copy(
+                    gathered[:], xw[:, T * s : T * (s + 1)].bitcast(U32).indirect(offs_t[:, 8 * e0 : 8 * e1])
+                )
+                for e in range(e0, e1):
+                    slot_words[(e, s)] = gathered[:, C * (e - e0) : C * (e - e0 + 1)]
+
+        w1s_perm = []
+        w1s_perm_plane = []
+        for h, raw in enumerate((w1s_first[:], w1s_second)):
+            words = keep.tile([P, PASSES * W], I32, name="w1s_perm_%d" % h, align_bytes=64)
+            plane = keep.tile([P, W], U8, name="w1s_perm_plane_%d" % h, align_bytes=64)
+            for s in range(PASSES):
+                nc.gpsimd.tensor_copy(
+                    words[:, W * s : W * (s + 1)].rearrange("p (t a i) -> p a t i", t=4, i=4),
+                    raw[:, W * s : W * (s + 1)].rearrange("p (a i t) -> p a t i", t=4, i=4),
+                )
+            nc.gpsimd.tensor_copy(
+                plane[:].rearrange("p (t m) -> p t m", t=4),
+                w1s_plane_b[:, W * h : W * (h + 1)].rearrange("p (m t) -> p t m", t=4),
+            )
+            w1s_perm.append(words)
+            w1s_perm_plane.append(plane)
+
+        def first_layer_routed(e0, e1):
+            hidden = keep.tile([P, (e1 - e0) * W], BF16, name="hidden_%d" % e0, align_bytes=64)
             for e in range(e0, e1):
-                gathered[(e, s)] = gw[:, C * (e - e0) : C * (e - e0 + 1)]
-
-        units = CFG["units"]
-        turn_on_vector = CFG["tv"]
-        groups = {}
-        hidden = {}
-        codes = {}
-
-        turned_halves = CFG["A"]
-        w1s_perm = {}
-        w1s_perm_p = {h: keep.tile([P, W], U8, name="w1s_perm_p_%d" % h, align_bytes=64) for h in turned_halves}
-
-        def permute_scales(h):
-            nc.vector.tensor_copy(
-                w1s_perm_p[h][:].rearrange("p (t m) -> p t m", t=4),
-                w1s_pb[:, W * h : W * (h + 1)].rearrange("p (m t) -> p t m", t=4),
-            )
-
-        def permute_words(h):
-            w1s_perm[h] = ring.tile(
-                [P, PASSES * W], I32, name="w1s_perm_%d" % h, tag="gw_%d_1" % CFG["perm_slot"], align_bytes=64
-            )
-            nc.vector.tensor_copy(
-                w1s_perm[h][:].rearrange("p (s t a i) -> p s a t i", s=PASSES, t=4, i=4),
-                w1s_t[h].rearrange("p (s a i t) -> p s a t i", s=PASSES, t=4, i=4),
-            )
-
-        def first_layer(u):
-            hb = work.tile([P, 2 * W], BF16, name="hb", align_bytes=64)
-            accs = [psum.tile([P, W], F32, name="acc", bufs=CFG["bufs"][0]) for b in units[u]]
-            early = u in CFG["pm"]
-            if early:
-                for b, (kind, j, h) in enumerate(units[u]):
+                acc = psum.tile([P, W], F32, name="acc", bufs=4)
+                for s in range(PASSES):
+                    a = PASSES * e + s
                     nc.tensor.matmul_mx(
-                        out=accs[b][:],
-                        lhsT=xw[:, P * j : P * (j + 1)].bitcast(FP8X4),
-                        lhsT_scale=xs_b[0:P, P * j : P * (j + 1)],
-                        rhs=w1s_t[h][:, 0:W].bitcast(FP8X4),
-                        rhs_scale=w1s_pb[0:P, W * h : W * (h + 1)],
-                        start=True, stop=False,
+                        out=acc[:],
+                        lhsT=slot_words[(e, s)].bitcast(FP8X4),
+                        lhsT_scale=slot_planes[s][:, C * e : C * (e + 1)],
+                        rhs=w1_t[:, 2 * H * a : 2 * H * (a + 1)].bitcast(FP4X4),
+                        rhs_scale=w1_plane_b[:, H * a : H * (a + 1)],
+                        start=(s == 0), stop=(s == PASSES - 1),
                     )
-            for b, (kind, j, h) in enumerate(units[u]):
-                acc = accs[b]
-                if kind == "s" and h in turned_halves:
-                    for t in range(4):
-                        for s in range(PASSES):
-                            c0 = T * s + P * j
-                            nc.tensor.matmul_mx(
-                                out=acc[:, P * t : P * (t + 1)],
-                                lhsT=w1s_perm[h][:, W * s + P * t : W * s + P * (t + 1)].bitcast(FP8X4),
-                                lhsT_scale=w1s_perm_p[h][4 * s : P, P * t : P * (t + 1)],
-                                rhs=xw[:, c0 : c0 + P].bitcast(FP8X4),
-                                rhs_scale=xs_b[4 * s : P, P * j : P * (j + 1)],
-                                start=(s == 0), stop=(s == PASSES - 1),
-                            )
-                    nc.scalar.activation(
-                        hb[:, W * b : W * (b + 1)].rearrange("p (r t) -> p r t", t=4),
-                        acc[:].rearrange("p (t r) -> p r t", t=4),
-                        SILU,
-                    )
-                    continue
-                for s in range(int(early), PASSES):
-                    if kind == "s":
-                        c0 = T * s + P * j
-                        nc.tensor.matmul_mx(
-                            out=acc[:],
-                            lhsT=xw[:, c0 : c0 + P].bitcast(FP8X4),
-                            lhsT_scale=xs_b[4 * s : P, P * j : P * (j + 1)],
-                            rhs=w1s_t[h][:, W * s : W * (s + 1)].bitcast(FP8X4),
-                            rhs_scale=w1s_pb[4 * s : P, W * h : W * (h + 1)],
-                            start=(s == 0), stop=(s == PASSES - 1),
-                        )
-                    else:
-                        gw = gathered[(j, s)]
-                        gs = slot_scales[(j, s)]
-                        a = PASSES * (j % 2) + s
-                        es = PASSES * (j - split * int(j >= split)) + s
-                        nc.tensor.matmul_mx(
-                            out=acc[:],
-                            lhsT=gw.bitcast(FP8X4),
-                            lhsT_scale=gs,
-                            rhs=w1_t[j // 2][:, 2 * H * a : 2 * H * (a + 1)].bitcast(FP4X4),
-                            rhs_scale=w1_planes[int(j >= split)][:, H * es : H * (es + 1)],
-                            start=(s == 0), stop=(s == PASSES - 1),
-                        )
                 nc.scalar.activation(
-                    hb[:, W * b : W * (b + 1)].rearrange("r (u p e) -> r u p e", u=2, e=2),
+                    hidden[:, W * (e - e0) : W * (e - e0 + 1)].rearrange("r (u p e) -> r u p e", u=2, e=2),
                     acc[:].rearrange("r (p u e) -> r u p e", u=2, e=2),
                     SILU,
                 )
-            hidden[u] = hb
+            return hidden
 
-        def turn(u):
-            nb = len(units[u])
-            if units[u][0][0] == "s" and units[u][0][2] in turned_halves:
-                grouped = hidden[u]
+        def turn(e0, e1, hidden):
+            nb = e1 - e0
+            words = hidden[:].bitcast(F32)
+            turned = psum.tile([P, W], F32, name="turned", bufs=2)
+            for j in range(2 * nb):
+                nc.tensor.transpose(turned[:, P * j : P * (j + 1)], words[:, P * j : P * (j + 1)], ident[:])
+            grouped = keep.tile([P, nb * W], BF16, name="grouped_%d" % e0, align_bytes=64)
+            dst = grouped[:].bitcast(F32).rearrange("p (b r u) -> p b r u", b=nb, u=2)
+            src = turned[:, 0 : 2 * P * nb].rearrange("p (b u r) -> p b r u", b=nb, u=2)
+            if e1 <= TURNS_ON_SCALAR:
+                nc.scalar.copy(dst, src)
             else:
-                words = hidden[u][:].bitcast(F32)
-                turned = psum.tile([P, W], F32, name="turned", bufs=CFG["bufs"][1])
-                for j in range(2 * nb):
-                    nc.tensor.transpose(turned[:, P * j : P * (j + 1)], words[:, P * j : P * (j + 1)], ident[:])
-                grouped = work.tile([P, 2 * W], BF16, name="grouped", align_bytes=64)
-                dst = grouped[:, 0 : W * nb].bitcast(F32).rearrange("p (b r u) -> p b r u", b=nb, u=2)
-                src = turned[:, 0 : 2 * P * nb].rearrange("p (b u r) -> p b r u", b=nb, u=2)
-                if u in turn_on_vector:
-                    nc.vector.tensor_copy(dst, src)
-                else:
-                    nc.scalar.copy(dst, src)
-            groups[u] = grouped
+                nc.vector.tensor_copy(dst, src)
+            return grouped
 
-        def quantize(u):
-            nb = len(units[u])
-            grouped = groups[u]
-            hw = keep.tile([P, nb * P], U32, name="hw_%d" % u, align_bytes=64)
-            hs = keep.tile([P, nb * P], U8, name="hs_%d" % u, align_bytes=64)
-            nc.vector.quantize_mx(out=hw[:].bitcast(FP8X4), scales=hs[:], in_=grouped[:, 0 : W * nb])
-            for b, blk in enumerate(units[u]):
-                codes[blk] = (hw[:, P * b : P * (b + 1)], hs[:, P * b : P * (b + 1)])
+        def quantize(name, values, width):
+            words = keep.tile([P, width], U32, name="codes_" + name, align_bytes=64)
+            scales = keep.tile([P, width], U8, name="scales_" + name, align_bytes=64)
+            nc.vector.quantize_mx(out=words[:].bitcast(FP8X4), scales=scales[:], in_=values)
+            return words, scales
 
-        parts = {}
-        combined = {}
-        shared_sums = {}
+        codes = {}
 
-        def fetch(t0, t1, r):
-            part = keep.tile([P, t1 - t0], F32, name="part_%d_%d" % (t0, r))
-            nc.vector.tensor_tensor(
-                part[:], y_sb[:].indirect((pos1_t, pos2_t)[r][:, t0 // 16 : t1 // 16]),
-                held["gate"][:, T * r + t0 : T * r + t1], MULT,
+        def quantize_routed(e0, e1, grouped):
+            words, scales = quantize("routed_%d" % e0, grouped[:], (e1 - e0) * C)
+            for e in range(e0, e1):
+                codes[e] = (words[:, C * (e - e0) : C * (e - e0 + 1)], scales[:, C * (e - e0) : C * (e - e0 + 1)])
+
+        y_sb = keep.tile([P, SLOTS], F32, name="y_sb")
+
+        def second_layer_routed(e0, e1):
+            y = psum.tile([P, W], F32, name="acc", bufs=4)
+            for e in range(e0, e1):
+                nc.tensor.matmul_mx(
+                    out=y[:, C * (e - e0) : C * (e - e0 + 1)],
+                    lhsT=w2_t[:, 2 * N * e : 2 * N * (e + 1)].bitcast(FP4X4),
+                    lhsT_scale=w2_plane[:].bitcast(U8)[:, N * e : N * (e + 1)],
+                    rhs=codes[e][0].bitcast(FP8X4), rhs_scale=codes[e][1],
+                    start=True, stop=True,
+                )
+            if e1 < E:
+                nc.scalar.copy(y_sb[:, C * e0 : C * e1], y[:, 0 : C * (e1 - e0)])
+            else:
+                nc.vector.tensor_copy(y_sb[:, C * e0 : C * e1], y[:, 0 : C * (e1 - e0)])
+
+        hs = [keep.tile([P, TILES * W], BF16, name="hs_%d" % h, align_bytes=64) for h in range(2)]
+
+        def first_layer_shared(j, h):
+            acc = psum.tile([P, W], F32, name="acc", bufs=4)
+            for t in range(4):
+                for s in range(PASSES):
+                    nc.tensor.matmul_mx(
+                        out=acc[:, P * t : P * (t + 1)],
+                        lhsT=w1s_perm[h][:, W * s + P * t : W * s + P * (t + 1)].bitcast(FP8X4),
+                        lhsT_scale=w1s_perm_plane[h][4 * s : P, P * t : P * (t + 1)],
+                        rhs=xw[:, T * s + P * j : T * s + P * (j + 1)].bitcast(FP8X4),
+                        rhs_scale=xs_b[4 * s : P, P * j : P * (j + 1)],
+                        start=(s == 0), stop=(s == PASSES - 1),
+                    )
+            nc.scalar.activation(
+                hs[h][:, W * j : W * (j + 1)].rearrange("p (r t) -> p r t", t=4),
+                acc[:].rearrange("p (t r) -> p r t", t=4),
+                SILU,
             )
-            parts[(t0, r)] = part
 
-        def combine(t0, t1):
-            both = keep.tile([P, t1 - t0], F32, name="both_%d" % t0)
-            nc.vector.tensor_tensor(both[:], parts[(t0, 0)][:], parts[(t0, 1)][:], ADD)
-            combined[t0] = both
+        shared = [(j, h) for h in range(2) for j in range(TILES - 1)] + [(TILES - 1, h) for h in range(2)]
+        for j, h in shared[:HEAD_TILES]:
+            first_layer_shared(j, h)
+        units = WEIGHT_LOADS
+        hidden = {}
+        grouped = {}
+        for step in range(len(units) + 2):
+            if step < len(units):
+                hidden[step] = first_layer_routed(*units[step])
+            if 0 <= step - 1 < len(units):
+                grouped[step - 1] = turn(*units[step - 1], hidden[step - 1])
+            if 0 <= step - 2 < len(units):
+                quantize_routed(*units[step - 2], grouped[step - 2])
+        for e0, e1 in [(0, 4), (4, 8), (8, 10)]:
+            second_layer_routed(e0, e1)
+        for j, h in shared[HEAD_TILES:]:
+            first_layer_shared(j, h)
+
+        parts = [keep.tile([P, T], F32, name="part_%d" % r) for r in range(2)]
+        both = keep.tile([P, T], F32, name="both")
+        result = keep.tile([P, T], F32, name="result")
+        chunks = [(P * j0, P * j1) for j0, j1 in TOKEN_CHUNKS]
+        hs_codes = {}
+
+        def fetch(r, t0, t1):
+            nc.vector.tensor_tensor(
+                parts[r][:, t0:t1], y_sb[:].indirect(pos_t[r][:, t0 // 16 : t1 // 16]), gate_t[:, T * r + t0 : T * r + t1], MULT
+            )
+
+        def quantize_shared(h, t0, t1):
+            hs_codes[(h, t0)] = quantize("shared_%d_%d" % (h, t0), hs[h][:, 4 * t0 : 4 * t1], t1 - t0)
+
+        sums = {}
+
+        def second_layer_shared(t0, t1):
+            ys = psum.tile([P, W], F32, name="ys", bufs=2)
+            for h in range(2):
+                words, scales = hs_codes[(h, t0)]
+                nc.tensor.matmul_mx(
+                    out=ys[:, 0 : t1 - t0],
+                    lhsT=w2s_t[:, N * h : N * (h + 1)].bitcast(FP8X4),
+                    lhsT_scale=w2s_plane[:].bitcast(U8)[:, N * h : N * (h + 1)],
+                    rhs=words[:].bitcast(FP8X4), rhs_scale=scales[:],
+                    start=(h == 0), stop=(h == 1),
+                )
+            for j in range(t0 // P, t1 // P):
+                sums[P * j] = ys[:, P * j - t0 :]
+
+        def add_parts(t0, t1):
+            nc.vector.tensor_tensor(both[:, t0:t1], parts[0][:, t0:t1], parts[1][:, t0:t1], ADD)
 
         def finish(t0, t1):
-            res = keep.tile([P, t1 - t0], F32, name="res_%d" % t0)
-            nc.vector.tensor_tensor(res[:], shared_sums[t0][:, 0 : t1 - t0], combined[t0][:], ADD)
-            nc.sync.dma_start(out[:, t0:t1], res[:])
+            nc.vector.tensor_tensor(result[:, t0:t1], sums[t0][:, 0 : t1 - t0], both[:, t0:t1], ADD)
+            nc.sync.dma_start(out[:, t0:t1], result[:, t0:t1])
 
-        def second_layer(u):
-            blocks = units[u]
-            if blocks[0][0] == "r":
-                y = psum.tile([P, 2 * C], F32, name="y", bufs=CFG["bufs"][2])
-                for b, blk in enumerate(blocks):
-                    e = blk[1]
-                    hw, hs = codes[blk]
-                    nc.tensor.matmul_mx(
-                        out=y[:, C * b : C * (b + 1)],
-                        lhsT=held["w2"][:, 2 * N * e : 2 * N * (e + 1)].bitcast(FP4X4),
-                        lhsT_scale=w2_pb[:, N * e : N * (e + 1)],
-                        rhs=hw.bitcast(FP8X4), rhs_scale=hs, start=True, stop=True,
-                    )
-                e0 = blocks[0][1]
-                if u in CFG["yv"]:
-                    nc.vector.tensor_copy(y_sb[:, C * e0 : C * (e0 + 2)], y[:])
-                else:
-                    nc.scalar.copy(y_sb[:, C * e0 : C * (e0 + 2)], y[:])
-                return
-            tiles = CFG["fin"].get(u, [])
-            if not tiles:
-                return
-            y = psum.tile([P, 2 * C], F32, name="y", bufs=CFG["bufs"][2])
-            for b, j in enumerate(tiles):
-                for h in range(2):
-                    hw, hs = codes[("s", j, h)]
-                    nc.tensor.matmul_mx(
-                        out=y[:, P * b : P * (b + 1)],
-                        lhsT=held["w2s"][:, N * h : N * (h + 1)].bitcast(FP8X4),
-                        lhsT_scale=held["w2s_p"][:].bitcast(U8)[:, N * h : N * (h + 1)],
-                        rhs=hw.bitcast(FP8X4), rhs_scale=hs, start=(h == 0), stop=(h == 1),
-                    )
-            shared_sums[P * tiles[0]] = y
-
-        steps = {"ld": load, "sg": gather_scales, "late": open_late, "setup": setup, "g": gather, "l1": first_layer, "t": turn, "q": quantize,
-                 "l2": second_layer, "ps": permute_scales, "pw": permute_words, "ad": combine, "ft": fetch, "fin": finish}
-        for item in CFG["plan"]:
-            steps[item[0]](*item[1:])
+        stores = [(0, 2 * P), (2 * P, 4 * P), (4 * P, T)]
+        fetch(0, 0, T)
+        quantize_shared(0, *chunks[0])
+        fetch(1, *stores[0])
+        quantize_shared(1, *chunks[0])
+        second_layer_shared(*chunks[0])
+        fetch(1, *stores[1])
+        add_parts(*stores[0])
+        quantize_shared(0, *chunks[1])
+        quantize_shared(1, *chunks[1])
+        second_layer_shared(*chunks[1])
+        finish(*stores[0])
+        fetch(1, *stores[2])
+        add_parts(*stores[1])
+        add_parts(*stores[2])
+        finish(*stores[1])
+        finish(*stores[2])

@@ -24,13 +24,12 @@ PASSES = K // W
 SLOTS = E * C
 TILES = T // P
 EXPERT_BYTES = PASSES * 2 * H
-SCALE_WINDOW = 1024
+SCALE_WINDOW = 1792
+EARLY = 4
 LIVE_ROWS = 100
 WORD_GATHERS = [(0, 3), (3, 6), (6, 8), (8, 10)]
-WEIGHT_LOADS = [(0, 1), (1, 3), (3, 5), (5, 7), (7, 9), (9, 10)]
 HEAD_TILES = 3
 TOKEN_CHUNKS = [(0, 4), (4, 5)]
-TURNS_ON_SCALAR = 1
 
 
 def tile_moe_shf_mlp_silu_kernel(
@@ -41,6 +40,9 @@ def tile_moe_shf_mlp_silu_kernel(
     with ExitStack() as ctx:
         keep = ctx.enter_context(tc.tile_pool(name="keep", bufs=1))
         psum = ctx.enter_context(tc.psum_pool(name="psum", bufs=1))
+
+        def bank(b):
+            return psum.tile([P, W], F32, name="bank_%d" % b, tag="bank_%d" % b)
 
         def zeroed_plane(name, nbytes, engine):
             plane = keep.tile([P, nbytes // 4], I32, name=name, align_bytes=64)
@@ -65,121 +67,127 @@ def tile_moe_shf_mlp_silu_kernel(
         window = keep.tile([P, SCALE_WINDOW // 4], I32, name="window", align_bytes=64)
         nc.gpsimd.memset(window[:, 0 : T // 4], 0)
         w1s_plane = zeroed_plane("w1s_plane", HS, nc.gpsimd)
-        nc.gpsimd.memset(window[:, T // 4 :], 0)
-        w1_plane = zeroed_plane("w1_plane", E * PASSES * H, nc.vector)
-        moved = zeroed_plane("moved", SLOTS, nc.gpsimd)
+        early_planes = zeroed_plane("early_planes", EARLY * PASSES * H, nc.vector)
+        nc.vector.memset(window[:, T // 4 :], 0)
+        moved = zeroed_plane("moved", SLOTS, nc.vector)
+        w2_planes = zeroed_plane("w2_planes", E * N, nc.gpsimd)
+        w2s_planes = zeroed_plane("w2s_planes", 2 * N, nc.gpsimd)
         ident = keep.tile([P, P], F32, name="ident")
         make_identity(nc, ident[:])
-        w2_plane = zeroed_plane("w2_plane", E * N, nc.gpsimd)
-        w2s_plane = zeroed_plane("w2s_plane", 2 * N, nc.gpsimd)
 
         offs_t = keep.tile([P, SLOTS // 16], U16, name="offs_t")
-        nc.sync.dma_start(offs_t[:], offs)
-        load_planes_stacked(nc.sync, window, x_scales)
         xw = keep.tile([P, PASSES * T], I32, name="xw", align_bytes=64)
-        def load_w1s(dst, half):
-            nc.sync.dma_start(
-                out=dst.rearrange("p (s l) -> p s l", s=PASSES),
-                in_=w1s_words.rearrange("s p l d -> p s (l d)")[:, :, 4 * W * half : 4 * W * (half + 1)].bitcast(I32),
-            )
-
-        w1s_first = keep.tile([P, PASSES * W], I32, name="w1s_first", align_bytes=64)
-        load_w1s(w1s_first[:], 0)
-        nc.sync.dma_start(
-            out=xw[:].rearrange("p (s t) -> p s t", s=PASSES),
-            in_=x_words.rearrange("s p t d -> p s (t d)").bitcast(I32),
-        )
-        load_planes_stacked(nc.sync, w1s_plane, w1s_scales)
-        load_planes_side_by_side(nc.sync, w1_plane, w1_scales.rearrange("e s b i -> (e s) b i"))
-
+        w1s_raw = [
+            keep.tile([P, PASSES * W], I32, name="w1s_raw_%d" % h, tag="w1s_raw_%d" % h, align_bytes=64) for h in range(2)
+        ]
+        pos_t = [keep.tile([P, T // 16], U16, name="pos%d_t" % (r + 1)) for r in range(2)]
+        w2_t = keep.tile([P, 2 * E * N], U8, name="w2_t", align_bytes=64)
+        w2s_t = keep.tile([P, 2 * N], I32, name="w2s_t", align_bytes=64)
+        gate_t = keep.tile([P, 2 * T], F32, name="gate_t")
         slot_scales = keep.tile([P, SLOTS], U8, name="slot_scales", align_bytes=64)
-        half = SLOTS // 2
-        for g in range(2):
-            nc.vector.tensor_copy(
-                slot_scales[:, half * g : half * (g + 1)],
-                window[:].bitcast(U8).indirect(offs_t[:, half // 16 * g : half // 16 * (g + 1)]),
-            )
-
-        def move_scale_rows(g):
-            cols = slice(half // 4 * g, half // 4 * (g + 1))
-            nc.sync.dma_start(out=moved[0:LIVE_ROWS, cols], in_=slot_scales[:].bitcast(I32)[4 : 4 + LIVE_ROWS, cols])
-
         slot_planes = [slot_scales[:], moved[:].bitcast(U8)]
+        slot_words = {}
+        w1_t = {}
 
-        late = keep.tile([P, E * EXPERT_BYTES + 2 * E * N + 4 * PASSES * W + 8 * N], U8, name="late", align_bytes=64)
-        w1_t = late[:, 0 : E * EXPERT_BYTES]
-        w2_t = late[:, E * EXPERT_BYTES : E * EXPERT_BYTES + 2 * E * N]
-        at = E * EXPERT_BYTES + 2 * E * N
-        w1s_second = late[:, at : at + 4 * PASSES * W].bitcast(I32)
-        w2s_t = late[:, at + 4 * PASSES * W :].bitcast(I32)
-        for i, (e0, e1) in enumerate(WEIGHT_LOADS):
-            if i in (0, 2):
-                move_scale_rows(i // 2)
-            if i == 2:
-                load_w1s(w1s_second, 1)
+        def load_w1(e0, e1):
+            pair = keep.tile([P, (e1 - e0) * EXPERT_BYTES], U8, name="w1_%d" % e0, align_bytes=64)
+            for e in range(e0, e1):
+                w1_t[e] = pair[:, EXPERT_BYTES * (e - e0) : EXPERT_BYTES * (e - e0 + 1)]
             nc.sync.dma_start(
-                out=w1_t[:, EXPERT_BYTES * e0 : EXPERT_BYTES * e1].bitcast(I32).rearrange("p (a b) -> p a b", a=PASSES * (e1 - e0)),
+                out=pair[:].bitcast(I32).rearrange("p (a b) -> p a b", a=PASSES * (e1 - e0)),
                 in_=w1_words[e0:e1].rearrange("e s p b -> p (e s) b").bitcast(I32),
             )
-        load_planes_side_by_side(nc.sync, w2_plane, w2_scales.rearrange("e s b i -> (e s) b i"))
-        nc.sync.dma_start(
-            out=w2_t.bitcast(I32).rearrange("p (e b) -> p e b", e=E),
-            in_=w2_words.rearrange("e s p b -> p (e s) b").bitcast(I32),
-        )
-        gate_t = keep.tile([P, 2 * T], F32, name="gate_t")
-        nc.sync.dma_start(out=gate_t[:].rearrange("p (r t) -> p r t", r=2), in_=gate.rearrange("r p t -> p r t"))
-        pos_t = [keep.tile([P, T // 16], U16, name="pos%d_t" % (r + 1)) for r in range(2)]
-        nc.sync.dma_start(pos_t[0][:], pos1)
-        nc.sync.dma_start(pos_t[1][:], pos2)
-        nc.sync.dma_start(
-            out=w2s_t.rearrange("p (s n) -> p s n", s=2), in_=w2s_words.rearrange("s p n d -> p s (n d)").bitcast(I32)
-        )
-        load_planes_side_by_side(nc.sync, w2s_plane, w2s_scales)
 
-        xs_b = window[:].bitcast(U8)
-        w1s_plane_b = w1s_plane[:].bitcast(U8)
-        w1_plane_b = w1_plane[:].bitcast(U8)
-
-        slot_words = {}
-        for e0, e1 in WORD_GATHERS:
+        def gather_words(e0, e1):
             for s in range(PASSES):
-                name = "slot_words_%d_%d" % (e0, s)
-                gathered = keep.tile([P, (e1 - e0) * C], U32, name=name, tag=name, align_bytes=64)
+                gathered = keep.tile([P, (e1 - e0) * C], U32, name="slot_words_%d_%d" % (e0, s), align_bytes=64)
                 nc.vector.tensor_copy(
                     gathered[:], xw[:, T * s : T * (s + 1)].bitcast(U32).indirect(offs_t[:, 8 * e0 : 8 * e1])
                 )
                 for e in range(e0, e1):
                     slot_words[(e, s)] = gathered[:, C * (e - e0) : C * (e - e0 + 1)]
 
-        w1s_perm = []
-        w1s_perm_plane = []
-        for h, raw in enumerate((w1s_first[:], w1s_second)):
-            words = keep.tile([P, PASSES * W], I32, name="w1s_perm_%d" % h, align_bytes=64)
-            plane = keep.tile([P, W], U8, name="w1s_perm_plane_%d" % h, align_bytes=64)
-            for s in range(PASSES):
-                nc.gpsimd.tensor_copy(
-                    words[:, W * s : W * (s + 1)].rearrange("p (t a i) -> p a t i", t=4, i=4),
-                    raw[:, W * s : W * (s + 1)].rearrange("p (a i t) -> p a t i", t=4, i=4),
-                )
-            nc.gpsimd.tensor_copy(
-                plane[:].rearrange("p (t m) -> p t m", t=4),
+        xs_b = window[:].bitcast(U8)
+        w1s_plane_b = w1s_plane[:].bitcast(U8)
+        w2_plane = w2_planes[:].bitcast(U8)
+        w2s_plane = w2s_planes[:].bitcast(U8)
+        w1s_perm = {}
+        w1s_perm_plane = {}
+
+        def permute_words(h, engine, tag, cuts):
+            w1s_perm[h] = keep.tile([P, PASSES * W], I32, name="w1s_perm_%d" % h, tag=tag, align_bytes=64)
+            dst = w1s_perm[h][:].rearrange("p (s t a i) -> p s a t i", s=PASSES, t=4, i=4)
+            src = w1s_raw[h][:].rearrange("p (s a i t) -> p s a t i", s=PASSES, t=4, i=4)
+            for s0, s1 in cuts:
+                engine.tensor_copy(dst[:, s0:s1], src[:, s0:s1])
+
+        def permute_plane(h, engine):
+            w1s_perm_plane[h] = keep.tile([P, W], U8, name="w1s_perm_plane_%d" % h, align_bytes=64)
+            engine.tensor_copy(
+                w1s_perm_plane[h][:].rearrange("p (t m) -> p t m", t=4),
                 w1s_plane_b[:, W * h : W * (h + 1)].rearrange("p (m t) -> p t m", t=4),
             )
-            w1s_perm.append(words)
-            w1s_perm_plane.append(plane)
+
+        nc.sync.dma_start(offs_t[:], offs)
+        load_planes_stacked(nc.sync, window, x_scales)
+        for s in range(PASSES):
+            nc.sync.dma_start(
+                w1s_raw[0][:, W * s : W * (s + 1)], w1s_words[s].rearrange("p l d -> p (l d)")[:, 0 : 4 * W].bitcast(I32)
+            )
+        load_planes_stacked(nc.sync, w1s_plane, w1s_scales)
+        nc.sync.dma_start(
+            out=xw[:].rearrange("p (s t) -> p s t", s=PASSES),
+            in_=x_words.rearrange("s p t d -> p s (t d)").bitcast(I32),
+        )
+        w1_rows = w1_scales.rearrange("e s b i -> (e s) b i")
+        load_planes_side_by_side(nc.sync, early_planes, w1_rows[0 : PASSES * EARLY])
+        load_w1(0, 2)
+        nc.vector.tensor_copy(slot_scales[:], xs_b.indirect(offs_t[:]))
+        nc.sync.dma_start(out=moved[0:LIVE_ROWS, :], in_=slot_scales[:].bitcast(I32)[4 : 4 + LIVE_ROWS, :])
+        load_w1(2, 4)
+        permute_words(0, nc.gpsimd, "w1s_perm_0", [(0, 1), (1, 2)])
+        permute_plane(0, nc.vector)
+        later_planes = keep.tile(
+            [P, (E - EARLY) * PASSES * H // 4], I32, name="later_planes", tag="w1s_raw_0", align_bytes=64
+        )
+        nc.gpsimd.memset(later_planes[:], 0)
+        load_planes_side_by_side(nc.sync, later_planes, w1_rows[PASSES * EARLY :])
+        load_w1(4, 6)
+        load_w1(6, 8)
+        load_planes_side_by_side(nc.sync, w2_planes, w2_scales.rearrange("e s b i -> (e s) b i"))
+        load_w1(8, 10)
+        nc.sync.dma_start(
+            out=w2_t[:].bitcast(I32).rearrange("p (e b) -> p e b", e=E),
+            in_=w2_words.rearrange("e s p b -> p (e s) b").bitcast(I32),
+        )
+        nc.sync.dma_start(out=gate_t[:].rearrange("p (r t) -> p r t", r=2), in_=gate.rearrange("r p t -> p r t"))
+        nc.sync.dma_start(
+            out=w1s_raw[1][:].rearrange("p (s l) -> p s l", s=PASSES),
+            in_=w1s_words.rearrange("s p l d -> p s (l d)")[:, :, 4 * W : 8 * W].bitcast(I32),
+        )
+        nc.sync.dma_start(pos_t[0][:], pos1)
+        nc.sync.dma_start(pos_t[1][:], pos2)
+        nc.sync.dma_start(
+            out=w2s_t[:].rearrange("p (s n) -> p s n", s=2), in_=w2s_words.rearrange("s p n d -> p s (n d)").bitcast(I32)
+        )
+        load_planes_side_by_side(nc.sync, w2s_planes, w2s_scales)
+
+        permute_plane(1, nc.gpsimd)
+        for e0, e1 in WORD_GATHERS:
+            gather_words(e0, e1)
 
         def first_layer_routed(e0, e1):
             hidden = keep.tile([P, (e1 - e0) * W], BF16, name="hidden_%d" % e0, align_bytes=64)
             for e in range(e0, e1):
-                acc = psum.tile([P, W], F32, name="acc", bufs=4)
+                acc = bank(e % 6)
                 for s in range(PASSES):
-                    a = PASSES * e + s
+                    planes, a = (early_planes, PASSES * e + s) if e < EARLY else (later_planes, PASSES * (e - EARLY) + s)
                     nc.tensor.matmul_mx(
                         out=acc[:],
                         lhsT=slot_words[(e, s)].bitcast(FP8X4),
                         lhsT_scale=slot_planes[s][:, C * e : C * (e + 1)],
-                        rhs=w1_t[:, 2 * H * a : 2 * H * (a + 1)].bitcast(FP4X4),
-                        rhs_scale=w1_plane_b[:, H * a : H * (a + 1)],
+                        rhs=w1_t[e][:, 2 * H * s : 2 * H * (s + 1)].bitcast(FP4X4),
+                        rhs_scale=planes[:].bitcast(U8)[:, H * a : H * (a + 1)],
                         start=(s == 0), stop=(s == PASSES - 1),
                     )
                 nc.scalar.activation(
@@ -189,20 +197,16 @@ def tile_moe_shf_mlp_silu_kernel(
                 )
             return hidden
 
-        def turn(e0, e1, hidden):
-            nb = e1 - e0
-            words = hidden[:].bitcast(F32)
-            turned = psum.tile([P, W], F32, name="turned", bufs=2)
+        def turn(hidden, grouped, b0, b1, b, copy):
+            nb = b1 - b0
+            words = hidden[:, W * b0 : W * b1].bitcast(F32)
+            turned = bank(b)
             for j in range(2 * nb):
                 nc.tensor.transpose(turned[:, P * j : P * (j + 1)], words[:, P * j : P * (j + 1)], ident[:])
-            grouped = keep.tile([P, nb * W], BF16, name="grouped_%d" % e0, align_bytes=64)
-            dst = grouped[:].bitcast(F32).rearrange("p (b r u) -> p b r u", b=nb, u=2)
-            src = turned[:, 0 : 2 * P * nb].rearrange("p (b u r) -> p b r u", b=nb, u=2)
-            if e1 <= TURNS_ON_SCALAR:
-                nc.scalar.copy(dst, src)
-            else:
-                nc.vector.tensor_copy(dst, src)
-            return grouped
+            copy(
+                grouped[:, W * b0 : W * b1].bitcast(F32).rearrange("p (b r u) -> p b r u", b=nb, u=2),
+                turned[:, 0 : 2 * P * nb].rearrange("p (b u r) -> p b r u", b=nb, u=2),
+            )
 
         def quantize(name, values, width):
             words = keep.tile([P, width], U32, name="codes_" + name, align_bytes=64)
@@ -219,13 +223,13 @@ def tile_moe_shf_mlp_silu_kernel(
 
         y_sb = keep.tile([P, SLOTS], F32, name="y_sb")
 
-        def second_layer_routed(e0, e1):
-            y = psum.tile([P, W], F32, name="acc", bufs=4)
+        def second_layer_routed(e0, e1, b):
+            y = bank(b)
             for e in range(e0, e1):
                 nc.tensor.matmul_mx(
                     out=y[:, C * (e - e0) : C * (e - e0 + 1)],
                     lhsT=w2_t[:, 2 * N * e : 2 * N * (e + 1)].bitcast(FP4X4),
-                    lhsT_scale=w2_plane[:].bitcast(U8)[:, N * e : N * (e + 1)],
+                    lhsT_scale=w2_plane[:, N * e : N * (e + 1)],
                     rhs=codes[e][0].bitcast(FP8X4), rhs_scale=codes[e][1],
                     start=True, stop=True,
                 )
@@ -236,8 +240,7 @@ def tile_moe_shf_mlp_silu_kernel(
 
         hs = [keep.tile([P, TILES * W], BF16, name="hs_%d" % h, align_bytes=64) for h in range(2)]
 
-        def first_layer_shared(j, h):
-            acc = psum.tile([P, W], F32, name="acc", bufs=4)
+        def first_layer_shared(j, h, acc):
             for t in range(4):
                 for s in range(PASSES):
                     nc.tensor.matmul_mx(
@@ -254,23 +257,34 @@ def tile_moe_shf_mlp_silu_kernel(
                 SILU,
             )
 
-        shared = [(j, h) for h in range(2) for j in range(TILES - 1)] + [(TILES - 1, h) for h in range(2)]
-        for j, h in shared[:HEAD_TILES]:
-            first_layer_shared(j, h)
-        units = WEIGHT_LOADS
+        for j in range(HEAD_TILES):
+            first_layer_shared(j, 0, bank(3 + j))
+        pairs = E // 2
         hidden = {}
         grouped = {}
-        for step in range(len(units) + 2):
-            if step < len(units):
-                hidden[step] = first_layer_routed(*units[step])
-            if 0 <= step - 1 < len(units):
-                grouped[step - 1] = turn(*units[step - 1], hidden[step - 1])
-            if 0 <= step - 2 < len(units):
-                quantize_routed(*units[step - 2], grouped[step - 2])
-        for e0, e1 in [(0, 4), (4, 8), (8, 10)]:
-            second_layer_routed(e0, e1)
-        for j, h in shared[HEAD_TILES:]:
-            first_layer_shared(j, h)
+        for step in range(pairs + 2):
+            if step < pairs:
+                hidden[step] = first_layer_routed(2 * step, 2 * step + 2)
+            if 0 <= step - 1 < pairs:
+                g = step - 1
+                grouped[g] = keep.tile([P, 2 * W], BF16, name="grouped_%d" % g, tag="grouped_%d" % g, align_bytes=64)
+                if g < pairs - 1:
+                    turn(hidden[g], grouped[g], 0, 2, (2 * g + 2) % 6, nc.vector.tensor_copy)
+                else:
+                    turn(hidden[g], grouped[g], 0, 1, 6, nc.scalar.copy)
+                    turn(hidden[g], grouped[g], 1, 2, 7, nc.scalar.copy)
+            if step == 1:
+                for j in range(HEAD_TILES, TILES):
+                    first_layer_shared(j, 0, bank(1 + 2 * (j - HEAD_TILES)))
+            if 0 <= step - 2 < pairs:
+                quantize_routed(2 * step - 4, 2 * step - 2, grouped[step - 2])
+        permute_words(1, nc.vector, "grouped_%d" % (pairs - 1), [(0, 2)])
+        for e0, e1, b in [(0, 4, 3), (4, 8, 1), (8, 10, 5)]:
+            second_layer_routed(e0, e1, b)
+        last_banks = [7, 6, 0]
+        last = [(j, 1) for j in range(TILES)]
+        for i, (j, h) in enumerate(last):
+            first_layer_shared(j, h, bank(last_banks[i % 3]))
 
         parts = [keep.tile([P, T], F32, name="part_%d" % r) for r in range(2)]
         both = keep.tile([P, T], F32, name="both")
@@ -289,13 +303,13 @@ def tile_moe_shf_mlp_silu_kernel(
         sums = {}
 
         def second_layer_shared(t0, t1):
-            ys = psum.tile([P, W], F32, name="ys", bufs=2)
+            ys = bank(last_banks[last.index((t1 // P - 1, 1)) % 3])
             for h in range(2):
                 words, scales = hs_codes[(h, t0)]
                 nc.tensor.matmul_mx(
                     out=ys[:, 0 : t1 - t0],
                     lhsT=w2s_t[:, N * h : N * (h + 1)].bitcast(FP8X4),
-                    lhsT_scale=w2s_plane[:].bitcast(U8)[:, N * h : N * (h + 1)],
+                    lhsT_scale=w2s_plane[:, N * h : N * (h + 1)],
                     rhs=words[:].bitcast(FP8X4), rhs_scale=scales[:],
                     start=(h == 0), stop=(h == 1),
                 )
@@ -310,14 +324,14 @@ def tile_moe_shf_mlp_silu_kernel(
             nc.sync.dma_start(out[:, t0:t1], result[:, t0:t1])
 
         stores = [(0, 2 * P), (2 * P, 4 * P), (4 * P, T)]
-        fetch(0, 0, T)
         quantize_shared(0, *chunks[0])
+        quantize_shared(0, *chunks[1])
+        fetch(0, 0, T)
         fetch(1, *stores[0])
         quantize_shared(1, *chunks[0])
         second_layer_shared(*chunks[0])
         fetch(1, *stores[1])
         add_parts(*stores[0])
-        quantize_shared(0, *chunks[1])
         quantize_shared(1, *chunks[1])
         second_layer_shared(*chunks[1])
         finish(*stores[0])

@@ -25,10 +25,10 @@ SLOTS = E * C
 TILES = T // P
 EXPERT_BYTES = PASSES * 2 * H
 SCALE_WINDOW = 1792
-EARLY = 4
 LIVE_ROWS = 100
 WORD_GATHERS = [(0, 3), (3, 6), (6, 8), (8, 10)]
-HEAD_TILES = 3
+HEAD_TILES = 4
+TURNS_ON_SCALAR = 3
 TOKEN_CHUNKS = [(0, 4), (4, 5)]
 
 
@@ -39,13 +39,14 @@ def tile_moe_shf_mlp_silu_kernel(
     nc = tc.nc
     with ExitStack() as ctx:
         keep = ctx.enter_context(tc.tile_pool(name="keep", bufs=1))
+        reuse = ctx.enter_context(tc.tile_pool(name="reuse", bufs=1))
         psum = ctx.enter_context(tc.psum_pool(name="psum", bufs=1))
 
         def bank(b):
             return psum.tile([P, W], F32, name="bank_%d" % b, tag="bank_%d" % b)
 
         def zeroed_plane(name, nbytes, engine):
-            plane = keep.tile([P, nbytes // 4], I32, name=name, align_bytes=64)
+            plane = keep.tile([P, nbytes // 4], I32, name=name, tag=name, align_bytes=64)
             engine.memset(plane[:], 0)
             return plane
 
@@ -67,25 +68,20 @@ def tile_moe_shf_mlp_silu_kernel(
         window = keep.tile([P, SCALE_WINDOW // 4], I32, name="window", align_bytes=64)
         nc.gpsimd.memset(window[:, 0 : T // 4], 0)
         w1s_plane = zeroed_plane("w1s_plane", HS, nc.gpsimd)
-        early_planes = zeroed_plane("early_planes", EARLY * PASSES * H, nc.vector)
-        nc.vector.memset(window[:, T // 4 :], 0)
-        moved = zeroed_plane("moved", SLOTS, nc.vector)
-        w2_planes = zeroed_plane("w2_planes", E * N, nc.gpsimd)
-        w2s_planes = zeroed_plane("w2s_planes", 2 * N, nc.gpsimd)
-        ident = keep.tile([P, P], F32, name="ident")
-        make_identity(nc, ident[:])
+        w1_planes = zeroed_plane("w1_planes", E * PASSES * H, nc.vector)
+        nc.gpsimd.memset(window[:, T // 4 :], 0)
 
         offs_t = keep.tile([P, SLOTS // 16], U16, name="offs_t")
         xw = keep.tile([P, PASSES * T], I32, name="xw", align_bytes=64)
         w1s_raw = [
-            keep.tile([P, PASSES * W], I32, name="w1s_raw_%d" % h, tag="w1s_raw_%d" % h, align_bytes=64) for h in range(2)
+            reuse.tile([P, PASSES * W], I32, name="w1s_raw_0", offset=0, align_bytes=64),
+            keep.tile([P, PASSES * W], I32, name="w1s_raw_1", align_bytes=64),
         ]
         pos_t = [keep.tile([P, T // 16], U16, name="pos%d_t" % (r + 1)) for r in range(2)]
         w2_t = keep.tile([P, 2 * E * N], U8, name="w2_t", align_bytes=64)
         w2s_t = keep.tile([P, 2 * N], I32, name="w2s_t", align_bytes=64)
         gate_t = keep.tile([P, 2 * T], F32, name="gate_t")
         slot_scales = keep.tile([P, SLOTS], U8, name="slot_scales", align_bytes=64)
-        slot_planes = [slot_scales[:], moved[:].bitcast(U8)]
         slot_words = {}
         w1_t = {}
 
@@ -109,8 +105,6 @@ def tile_moe_shf_mlp_silu_kernel(
 
         xs_b = window[:].bitcast(U8)
         w1s_plane_b = w1s_plane[:].bitcast(U8)
-        w2_plane = w2_planes[:].bitcast(U8)
-        w2s_plane = w2s_planes[:].bitcast(U8)
         w1s_perm = {}
         w1s_perm_plane = {}
 
@@ -140,31 +134,31 @@ def tile_moe_shf_mlp_silu_kernel(
             in_=x_words.rearrange("s p t d -> p s (t d)").bitcast(I32),
         )
         w1_rows = w1_scales.rearrange("e s b i -> (e s) b i")
-        load_planes_side_by_side(nc.sync, early_planes, w1_rows[0 : PASSES * EARLY])
+        load_planes_side_by_side(nc.sync, w1_planes, w1_rows)
         load_w1(0, 2)
         nc.vector.tensor_copy(slot_scales[:], xs_b.indirect(offs_t[:]))
-        nc.sync.dma_start(out=moved[0:LIVE_ROWS, :], in_=slot_scales[:].bitcast(I32)[4 : 4 + LIVE_ROWS, :])
-        load_w1(2, 4)
         permute_words(0, nc.gpsimd, "w1s_perm_0", [(0, 1), (1, 2)])
-        permute_plane(0, nc.vector)
-        later_planes = keep.tile(
-            [P, (E - EARLY) * PASSES * H // 4], I32, name="later_planes", tag="w1s_raw_0", align_bytes=64
-        )
-        nc.gpsimd.memset(later_planes[:], 0)
-        load_planes_side_by_side(nc.sync, later_planes, w1_rows[PASSES * EARLY :])
-        load_w1(4, 6)
-        load_w1(6, 8)
+        permute_plane(0, nc.gpsimd)
+        moved = reuse.tile([P, SLOTS // 4], I32, name="moved", offset=0, align_bytes=64)
+        w2_planes = reuse.tile([P, E * N // 4], I32, name="w2_planes", offset=SLOTS, align_bytes=64)
+        w2s_planes = reuse.tile([P, 2 * N // 4], I32, name="w2s_planes", offset=SLOTS + E * N, align_bytes=64)
+        slot_planes = [slot_scales[:], moved[:].bitcast(U8)]
+        w2_plane = w2_planes[:].bitcast(U8)
+        w2s_plane = w2s_planes[:].bitcast(U8)
+        nc.sync.dma_start(out=moved[0:LIVE_ROWS, :], in_=slot_scales[:].bitcast(I32)[4 : 4 + LIVE_ROWS, :])
+        for e0 in range(2, E - 2, 2):
+            load_w1(e0, e0 + 2)
         load_planes_side_by_side(nc.sync, w2_planes, w2_scales.rearrange("e s b i -> (e s) b i"))
         load_w1(8, 10)
+        nc.sync.dma_start(
+            out=w1s_raw[1][:].rearrange("p (s l) -> p s l", s=PASSES),
+            in_=w1s_words.rearrange("s p l d -> p s (l d)")[:, :, 4 * W : 8 * W].bitcast(I32),
+        )
         nc.sync.dma_start(
             out=w2_t[:].bitcast(I32).rearrange("p (e b) -> p e b", e=E),
             in_=w2_words.rearrange("e s p b -> p (e s) b").bitcast(I32),
         )
         nc.sync.dma_start(out=gate_t[:].rearrange("p (r t) -> p r t", r=2), in_=gate.rearrange("r p t -> p r t"))
-        nc.sync.dma_start(
-            out=w1s_raw[1][:].rearrange("p (s l) -> p s l", s=PASSES),
-            in_=w1s_words.rearrange("s p l d -> p s (l d)")[:, :, 4 * W : 8 * W].bitcast(I32),
-        )
         nc.sync.dma_start(pos_t[0][:], pos1)
         nc.sync.dma_start(pos_t[1][:], pos2)
         nc.sync.dma_start(
@@ -173,6 +167,8 @@ def tile_moe_shf_mlp_silu_kernel(
         load_planes_side_by_side(nc.sync, w2s_planes, w2s_scales)
 
         permute_plane(1, nc.gpsimd)
+        ident = keep.tile([P, P], F32, name="ident", tag="w1s_plane", align_bytes=64)
+        make_identity(nc, ident[:])
         for e0, e1 in WORD_GATHERS:
             gather_words(e0, e1)
 
@@ -181,13 +177,13 @@ def tile_moe_shf_mlp_silu_kernel(
             for e in range(e0, e1):
                 acc = bank(e % 6)
                 for s in range(PASSES):
-                    planes, a = (early_planes, PASSES * e + s) if e < EARLY else (later_planes, PASSES * (e - EARLY) + s)
+                    a = PASSES * e + s
                     nc.tensor.matmul_mx(
                         out=acc[:],
                         lhsT=slot_words[(e, s)].bitcast(FP8X4),
                         lhsT_scale=slot_planes[s][:, C * e : C * (e + 1)],
                         rhs=w1_t[e][:, 2 * H * s : 2 * H * (s + 1)].bitcast(FP4X4),
-                        rhs_scale=planes[:].bitcast(U8)[:, H * a : H * (a + 1)],
+                        rhs_scale=w1_planes[:].bitcast(U8)[:, H * a : H * (a + 1)],
                         start=(s == 0), stop=(s == PASSES - 1),
                     )
                 nc.scalar.activation(
@@ -238,7 +234,15 @@ def tile_moe_shf_mlp_silu_kernel(
             else:
                 nc.vector.tensor_copy(y_sb[:, C * e0 : C * e1], y[:, 0 : C * (e1 - e0)])
 
-        hs = [keep.tile([P, TILES * W], BF16, name="hs_%d" % h, align_bytes=64) for h in range(2)]
+        hs = {}
+        hs_chunk = {}
+        for h in range(2):
+            for j0, j1 in TOKEN_CHUNKS:
+                name = "hs_%d_%d" % (h, j0)
+                chunk = keep.tile([P, (j1 - j0) * W], BF16, name=name, tag=name, align_bytes=64)
+                hs_chunk[(h, P * j0)] = chunk
+                for j in range(j0, j1):
+                    hs[(h, j)] = chunk[:, W * (j - j0) : W * (j - j0 + 1)]
 
         def first_layer_shared(j, h, acc):
             for t in range(4):
@@ -252,7 +256,7 @@ def tile_moe_shf_mlp_silu_kernel(
                         start=(s == 0), stop=(s == PASSES - 1),
                     )
             nc.scalar.activation(
-                hs[h][:, W * j : W * (j + 1)].rearrange("p (r t) -> p r t", t=4),
+                hs[(h, j)].rearrange("p (r t) -> p r t", t=4),
                 acc[:].rearrange("p (t r) -> p r t", t=4),
                 SILU,
             )
@@ -269,38 +273,39 @@ def tile_moe_shf_mlp_silu_kernel(
                 g = step - 1
                 grouped[g] = keep.tile([P, 2 * W], BF16, name="grouped_%d" % g, tag="grouped_%d" % g, align_bytes=64)
                 if g < pairs - 1:
-                    turn(hidden[g], grouped[g], 0, 2, (2 * g + 2) % 6, nc.vector.tensor_copy)
+                    turn(hidden[g], grouped[g], 0, 2, (2 * g + 2) % 6, nc.scalar.copy if g < TURNS_ON_SCALAR else nc.vector.tensor_copy)
                 else:
                     turn(hidden[g], grouped[g], 0, 1, 6, nc.scalar.copy)
                     turn(hidden[g], grouped[g], 1, 2, 7, nc.scalar.copy)
-            if step == 1:
-                for j in range(HEAD_TILES, TILES):
-                    first_layer_shared(j, 0, bank(1 + 2 * (j - HEAD_TILES)))
             if 0 <= step - 2 < pairs:
                 quantize_routed(2 * step - 4, 2 * step - 2, grouped[step - 2])
-        permute_words(1, nc.vector, "grouped_%d" % (pairs - 1), [(0, 2)])
+        permute_words(1, nc.vector, "grouped_%d" % (pairs - 3), [(0, 2)])
         for e0, e1, b in [(0, 4, 3), (4, 8, 1), (8, 10, 5)]:
             second_layer_routed(e0, e1, b)
-        last_banks = [7, 6, 0]
-        last = [(j, 1) for j in range(TILES)]
+        last_banks = [6, 7, 1]
+        last = [(j, 0) for j in range(HEAD_TILES, TILES)] + [(j, 1) for j in range(TILES)]
         for i, (j, h) in enumerate(last):
             first_layer_shared(j, h, bank(last_banks[i % 3]))
 
-        parts = [keep.tile([P, T], F32, name="part_%d" % r) for r in range(2)]
+        first_part = keep.tile([P, T], F32, name="first_part")
+        second_part = {}
         both = keep.tile([P, T], F32, name="both")
         result = keep.tile([P, T], F32, name="result")
         chunks = [(P * j0, P * j1) for j0, j1 in TOKEN_CHUNKS]
         hs_codes = {}
+        sums = {}
 
-        def fetch(r, t0, t1):
+        def fetch(part, r, t0, t1):
             nc.vector.tensor_tensor(
-                parts[r][:, t0:t1], y_sb[:].indirect(pos_t[r][:, t0 // 16 : t1 // 16]), gate_t[:, T * r + t0 : T * r + t1], MULT
+                part, y_sb[:].indirect(pos_t[r][:, t0 // 16 : t1 // 16]), gate_t[:, T * r + t0 : T * r + t1], MULT
             )
 
-        def quantize_shared(h, t0, t1):
-            hs_codes[(h, t0)] = quantize("shared_%d_%d" % (h, t0), hs[h][:, 4 * t0 : 4 * t1], t1 - t0)
+        def fetch_second(t0, t1, tag):
+            second_part[t0] = keep.tile([P, t1 - t0], F32, name="second_part_%d" % t0, tag=tag, align_bytes=64)
+            fetch(second_part[t0][:], 1, t0, t1)
 
-        sums = {}
+        def quantize_shared(h, t0, t1):
+            hs_codes[(h, t0)] = quantize("shared_%d_%d" % (h, t0), hs_chunk[(h, t0)][:], t1 - t0)
 
         def second_layer_shared(t0, t1):
             ys = bank(last_banks[last.index((t1 // P - 1, 1)) % 3])
@@ -317,26 +322,24 @@ def tile_moe_shf_mlp_silu_kernel(
                 sums[P * j] = ys[:, P * j - t0 :]
 
         def add_parts(t0, t1):
-            nc.vector.tensor_tensor(both[:, t0:t1], parts[0][:, t0:t1], parts[1][:, t0:t1], ADD)
+            nc.vector.tensor_tensor(both[:, t0:t1], first_part[:, t0:t1], second_part[t0][:], ADD)
 
         def finish(t0, t1):
             nc.vector.tensor_tensor(result[:, t0:t1], sums[t0][:, 0 : t1 - t0], both[:, t0:t1], ADD)
             nc.sync.dma_start(out[:, t0:t1], result[:, t0:t1])
 
-        stores = [(0, 2 * P), (2 * P, 4 * P), (4 * P, T)]
+        cut = 2 * P
         quantize_shared(0, *chunks[0])
+        fetch(first_part[:], 0, 0, T)
         quantize_shared(0, *chunks[1])
-        fetch(0, 0, T)
-        fetch(1, *stores[0])
+        fetch_second(0, cut, "hs_0_0")
         quantize_shared(1, *chunks[0])
         second_layer_shared(*chunks[0])
-        fetch(1, *stores[1])
-        add_parts(*stores[0])
+        fetch_second(cut, T, "hs_1_0")
+        add_parts(0, cut)
         quantize_shared(1, *chunks[1])
         second_layer_shared(*chunks[1])
-        finish(*stores[0])
-        fetch(1, *stores[2])
-        add_parts(*stores[1])
-        add_parts(*stores[2])
-        finish(*stores[1])
-        finish(*stores[2])
+        finish(0, cut)
+        add_parts(cut, T)
+        finish(cut, 4 * P)
+        finish(4 * P, T)

@@ -28,7 +28,7 @@ SCALE_WINDOW = 1792
 LIVE_ROWS = 100
 WORD_GATHERS = [(0, 3), (3, 6), (6, 8), (8, 10)]
 HEAD_TILES = 4
-TURNS_ON_SCALAR = 3
+EARLY = 6
 TOKEN_CHUNKS = [(0, 4), (4, 5)]
 
 
@@ -68,7 +68,10 @@ def tile_moe_shf_mlp_silu_kernel(
         window = keep.tile([P, SCALE_WINDOW // 4], I32, name="window", align_bytes=64)
         nc.gpsimd.memset(window[:, 0 : T // 4], 0)
         w1s_plane = zeroed_plane("w1s_plane", HS, nc.gpsimd)
-        w1_planes = zeroed_plane("w1_planes", E * PASSES * H, nc.vector)
+        early_planes = zeroed_plane("early_planes", EARLY * PASSES * H, nc.vector)
+        moved = zeroed_plane("moved", SLOTS, nc.vector)
+        w2_planes = zeroed_plane("w2_planes", E * N, nc.vector)
+        w2s_planes = zeroed_plane("w2s_planes", 2 * N, nc.vector)
         nc.gpsimd.memset(window[:, T // 4 :], 0)
 
         offs_t = keep.tile([P, SLOTS // 16], U16, name="offs_t")
@@ -134,22 +137,21 @@ def tile_moe_shf_mlp_silu_kernel(
             in_=x_words.rearrange("s p t d -> p s (t d)").bitcast(I32),
         )
         w1_rows = w1_scales.rearrange("e s b i -> (e s) b i")
-        load_planes_side_by_side(nc.sync, w1_planes, w1_rows)
+        load_planes_side_by_side(nc.sync, early_planes, w1_rows[0 : PASSES * EARLY])
         load_w1(0, 2)
         nc.vector.tensor_copy(slot_scales[:], xs_b.indirect(offs_t[:]))
         permute_words(0, nc.gpsimd, "w1s_perm_0", [(0, 1), (1, 2)])
         permute_plane(0, nc.gpsimd)
-        moved = reuse.tile([P, SLOTS // 4], I32, name="moved", offset=0, align_bytes=64)
-        w2_planes = reuse.tile([P, E * N // 4], I32, name="w2_planes", offset=SLOTS, align_bytes=64)
-        w2s_planes = reuse.tile([P, 2 * N // 4], I32, name="w2s_planes", offset=SLOTS + E * N, align_bytes=64)
+        later_planes = reuse.tile([P, (E - EARLY) * PASSES * H // 4], I32, name="later_planes", offset=0, align_bytes=64)
         slot_planes = [slot_scales[:], moved[:].bitcast(U8)]
         w2_plane = w2_planes[:].bitcast(U8)
         w2s_plane = w2s_planes[:].bitcast(U8)
         nc.sync.dma_start(out=moved[0:LIVE_ROWS, :], in_=slot_scales[:].bitcast(I32)[4 : 4 + LIVE_ROWS, :])
-        for e0 in range(2, E - 2, 2):
+        for e0 in range(2, E, 2):
+            if e0 == EARLY:
+                load_planes_side_by_side(nc.sync, later_planes, w1_rows[PASSES * EARLY :])
+                load_planes_side_by_side(nc.sync, w2_planes, w2_scales.rearrange("e s b i -> (e s) b i"))
             load_w1(e0, e0 + 2)
-        load_planes_side_by_side(nc.sync, w2_planes, w2_scales.rearrange("e s b i -> (e s) b i"))
-        load_w1(8, 10)
         nc.sync.dma_start(
             out=w1s_raw[1][:].rearrange("p (s l) -> p s l", s=PASSES),
             in_=w1s_words.rearrange("s p l d -> p s (l d)")[:, :, 4 * W : 8 * W].bitcast(I32),
@@ -177,13 +179,13 @@ def tile_moe_shf_mlp_silu_kernel(
             for e in range(e0, e1):
                 acc = bank(e % 6)
                 for s in range(PASSES):
-                    a = PASSES * e + s
+                    planes, a = (early_planes, PASSES * e + s) if e < EARLY else (later_planes, PASSES * (e - EARLY) + s)
                     nc.tensor.matmul_mx(
                         out=acc[:],
                         lhsT=slot_words[(e, s)].bitcast(FP8X4),
                         lhsT_scale=slot_planes[s][:, C * e : C * (e + 1)],
                         rhs=w1_t[e][:, 2 * H * s : 2 * H * (s + 1)].bitcast(FP4X4),
-                        rhs_scale=w1_planes[:].bitcast(U8)[:, H * a : H * (a + 1)],
+                        rhs_scale=planes[:].bitcast(U8)[:, H * a : H * (a + 1)],
                         start=(s == 0), stop=(s == PASSES - 1),
                     )
                 nc.scalar.activation(
@@ -193,13 +195,13 @@ def tile_moe_shf_mlp_silu_kernel(
                 )
             return hidden
 
-        def turn(hidden, grouped, b0, b1, b, copy):
+        def turn(hidden, grouped, b0, b1, b):
             nb = b1 - b0
             words = hidden[:, W * b0 : W * b1].bitcast(F32)
             turned = bank(b)
             for j in range(2 * nb):
                 nc.tensor.transpose(turned[:, P * j : P * (j + 1)], words[:, P * j : P * (j + 1)], ident[:])
-            copy(
+            nc.vector.tensor_copy(
                 grouped[:, W * b0 : W * b1].bitcast(F32).rearrange("p (b r u) -> p b r u", b=nb, u=2),
                 turned[:, 0 : 2 * P * nb].rearrange("p (b u r) -> p b r u", b=nb, u=2),
             )
@@ -229,10 +231,7 @@ def tile_moe_shf_mlp_silu_kernel(
                     rhs=codes[e][0].bitcast(FP8X4), rhs_scale=codes[e][1],
                     start=True, stop=True,
                 )
-            if e1 < E:
-                nc.scalar.copy(y_sb[:, C * e0 : C * e1], y[:, 0 : C * (e1 - e0)])
-            else:
-                nc.vector.tensor_copy(y_sb[:, C * e0 : C * e1], y[:, 0 : C * (e1 - e0)])
+            nc.vector.tensor_copy(y_sb[:, C * e0 : C * e1], y[:, 0 : C * (e1 - e0)])
 
         hs = {}
         hs_chunk = {}
@@ -273,16 +272,16 @@ def tile_moe_shf_mlp_silu_kernel(
                 g = step - 1
                 grouped[g] = keep.tile([P, 2 * W], BF16, name="grouped_%d" % g, tag="grouped_%d" % g, align_bytes=64)
                 if g < pairs - 1:
-                    turn(hidden[g], grouped[g], 0, 2, (2 * g + 2) % 6, nc.scalar.copy if g < TURNS_ON_SCALAR else nc.vector.tensor_copy)
+                    turn(hidden[g], grouped[g], 0, 2, 6 + g % 2)
                 else:
-                    turn(hidden[g], grouped[g], 0, 1, 6, nc.scalar.copy)
-                    turn(hidden[g], grouped[g], 1, 2, 7, nc.scalar.copy)
+                    turn(hidden[g], grouped[g], 0, 1, 6)
+                    turn(hidden[g], grouped[g], 1, 2, 0)
             if 0 <= step - 2 < pairs:
                 quantize_routed(2 * step - 4, 2 * step - 2, grouped[step - 2])
         permute_words(1, nc.vector, "grouped_%d" % (pairs - 3), [(0, 2)])
         for e0, e1, b in [(0, 4, 3), (4, 8, 1), (8, 10, 5)]:
             second_layer_routed(e0, e1, b)
-        last_banks = [6, 7, 1]
+        last_banks = [6, 0, 1]
         last = [(j, 0) for j in range(HEAD_TILES, TILES)] + [(j, 1) for j in range(TILES)]
         for i, (j, h) in enumerate(last):
             first_layer_shared(j, h, bank(last_banks[i % 3]))

@@ -255,8 +255,8 @@ def tile_moe_shf_mlp_silu_kernel(
                         start=(s == 0), stop=(s == PASSES - 1),
                     )
             nc.scalar.activation(
-                hs[(h, j)].rearrange("p (r t) -> p r t", t=4),
-                acc[:].rearrange("p (t r) -> p r t", t=4),
+                hs[(h, j)].rearrange("p (c i t) -> p c t i", t=4, i=4),
+                acc[:].rearrange("p (t c i) -> p c t i", t=4, i=4),
                 SILU,
             )
 

@@ -281,7 +281,7 @@ def tile_moe_shf_mlp_silu_kernel(
         permute_words(1, nc.vector, "grouped_%d" % (pairs - 3), [(0, 2)])
         for e0, e1, b in [(0, 4, 3), (4, 8, 1), (8, 10, 5)]:
             second_layer_routed(e0, e1, b)
-        last_banks = [6, 0, 1]
+        last_banks = [0, 1, 5]
         last = [(j, 0) for j in range(HEAD_TILES, TILES)] + [(j, 1) for j in range(TILES)]
         for i, (j, h) in enumerate(last):
             first_layer_shared(j, h, bank(last_banks[i % 3]))

@@ -113,10 +113,10 @@ def tile_moe_shf_mlp_silu_kernel(
 
         def permute_words(h, engine, tag, cuts):
             w1s_perm[h] = keep.tile([P, PASSES * W], I32, name="w1s_perm_%d" % h, tag=tag, align_bytes=64)
-            dst = w1s_perm[h][:].rearrange("p (s t a i) -> p s a t i", s=PASSES, t=4, i=4)
-            src = w1s_raw[h][:].rearrange("p (s a i t) -> p s a t i", s=PASSES, t=4, i=4)
+            dst = w1s_perm[h][:].bitcast(U32).rearrange("p (s t a i) -> p s a t i", s=PASSES, t=4, i=4)
+            src = w1s_raw[h][:].bitcast(U32).rearrange("p (s a i t) -> p s a t i", s=PASSES, t=4, i=4)
             for s0, s1 in cuts:
-                engine.tensor_copy(dst[:, s0:s1], src[:, s0:s1])
+                engine(dst[:, s0:s1], src[:, s0:s1])
 
         def permute_plane(h, engine):
             w1s_perm_plane[h] = keep.tile([P, W], U8, name="w1s_perm_plane_%d" % h, align_bytes=64)
@@ -127,20 +127,20 @@ def tile_moe_shf_mlp_silu_kernel(
 
         nc.sync.dma_start(offs_t[:], offs)
         load_planes_stacked(nc.sync, window, x_scales)
-        for s in range(PASSES):
-            nc.sync.dma_start(
-                w1s_raw[0][:, W * s : W * (s + 1)], w1s_words[s].rearrange("p l d -> p (l d)")[:, 0 : 4 * W].bitcast(I32)
-            )
-        load_planes_stacked(nc.sync, w1s_plane, w1s_scales)
+        nc.sync.dma_start(
+            out=w1s_raw[0][:].rearrange("p (s l) -> p s l", s=PASSES),
+            in_=w1s_words.rearrange("s p l d -> p s (l d)")[:, :, 0 : 4 * W].bitcast(I32),
+        )
         nc.sync.dma_start(
             out=xw[:].rearrange("p (s t) -> p s t", s=PASSES),
             in_=x_words.rearrange("s p t d -> p s (t d)").bitcast(I32),
         )
+        load_planes_stacked(nc.sync, w1s_plane, w1s_scales)
         w1_rows = w1_scales.rearrange("e s b i -> (e s) b i")
         load_planes_side_by_side(nc.sync, early_planes, w1_rows[0 : PASSES * EARLY])
         load_w1(0, 2)
         nc.vector.tensor_copy(slot_scales[:], xs_b.indirect(offs_t[:]))
-        permute_words(0, nc.gpsimd, "w1s_perm_0", [(0, 1), (1, 2)])
+        permute_words(0, nc.scalar.copy, "w1s_perm_0", [(0, 1), (1, 2)])
         permute_plane(0, nc.gpsimd)
         later_planes = reuse.tile([P, (E - EARLY) * PASSES * H // 4], I32, name="later_planes", offset=0, align_bytes=64)
         slot_planes = [slot_scales[:], moved[:].bitcast(U8)]
@@ -278,7 +278,7 @@ def tile_moe_shf_mlp_silu_kernel(
                     turn(hidden[g], grouped[g], 1, 2, 0)
             if 0 <= step - 2 < pairs:
                 quantize_routed(2 * step - 4, 2 * step - 2, grouped[step - 2])
-        permute_words(1, nc.vector, "grouped_%d" % (pairs - 3), [(0, 2)])
+        permute_words(1, nc.vector.tensor_copy, "grouped_%d" % (pairs - 3), [(0, 2)])
         for e0, e1, b in [(0, 4, 3), (4, 8, 1), (8, 10, 5)]:
             second_layer_routed(e0, e1, b)
         last_banks = [0, 1, 5]

@@ -15,6 +15,7 @@ U8 = mybir.dt.uint8
 FP8X4 = mybir.dt.float8_e4m3fn_x4
 FP4X4 = mybir.dt.float4_e2m1fn_x4
 SILU = mybir.ActivationFunctionType.Silu
+COPY = mybir.ActivationFunctionType.Copy
 MULT = mybir.AluOpType.mult
 ADD = mybir.AluOpType.add
 
@@ -28,8 +29,9 @@ SCALE_WINDOW = 1792
 LIVE_ROWS = 100
 WORD_GATHERS = [(0, 3), (3, 6), (6, 8), (8, 10)]
 HEAD_TILES = 4
-EARLY = 6
-TOKEN_CHUNKS = [(0, 4), (4, 5)]
+TURNED_TILES = 2
+EARLY = 4
+TOKEN_CHUNKS = [(0, 2), (2, 4), (4, 5)]
 
 
 def tile_moe_shf_mlp_silu_kernel(
@@ -39,7 +41,6 @@ def tile_moe_shf_mlp_silu_kernel(
     nc = tc.nc
     with ExitStack() as ctx:
         keep = ctx.enter_context(tc.tile_pool(name="keep", bufs=1))
-        reuse = ctx.enter_context(tc.tile_pool(name="reuse", bufs=1))
         psum = ctx.enter_context(tc.psum_pool(name="psum", bufs=1))
 
         def bank(b):
@@ -70,20 +71,21 @@ def tile_moe_shf_mlp_silu_kernel(
         w1s_plane = zeroed_plane("w1s_plane", HS, nc.gpsimd)
         early_planes = zeroed_plane("early_planes", EARLY * PASSES * H, nc.vector)
         moved = zeroed_plane("moved", SLOTS, nc.vector)
-        w2_planes = zeroed_plane("w2_planes", E * N, nc.vector)
-        w2s_planes = zeroed_plane("w2s_planes", 2 * N, nc.vector)
+        later_planes = zeroed_plane("later_planes", (E - EARLY) * PASSES * H, nc.vector)
         nc.gpsimd.memset(window[:, T // 4 :], 0)
+        w2_planes = zeroed_plane("w2_planes", E * N, nc.gpsimd)
+        w2s_planes = zeroed_plane("w2s_planes", 2 * N, nc.gpsimd)
 
         offs_t = keep.tile([P, SLOTS // 16], U16, name="offs_t")
         xw = keep.tile([P, PASSES * T], I32, name="xw", align_bytes=64)
         w1s_raw = [
-            reuse.tile([P, PASSES * W], I32, name="w1s_raw_0", offset=0, align_bytes=64),
+            keep.tile([P, PASSES * W], I32, name="w1s_raw_0", align_bytes=64),
             keep.tile([P, PASSES * W], I32, name="w1s_raw_1", align_bytes=64),
         ]
         pos_t = [keep.tile([P, T // 16], U16, name="pos%d_t" % (r + 1)) for r in range(2)]
         w2_t = keep.tile([P, 2 * E * N], U8, name="w2_t", align_bytes=64)
         w2s_t = keep.tile([P, 2 * N], I32, name="w2s_t", align_bytes=64)
-        gate_t = keep.tile([P, 2 * T], F32, name="gate_t")
+        gate_t = [keep.tile([P, T], F32, name="gate_%d" % r) for r in range(2)]
         slot_scales = keep.tile([P, SLOTS], U8, name="slot_scales", align_bytes=64)
         slot_words = {}
         w1_t = {}
@@ -118,38 +120,41 @@ def tile_moe_shf_mlp_silu_kernel(
             for s0, s1 in cuts:
                 engine(dst[:, s0:s1], src[:, s0:s1])
 
-        def permute_plane(h, engine):
-            w1s_perm_plane[h] = keep.tile([P, W], U8, name="w1s_perm_plane_%d" % h, align_bytes=64)
-            engine.tensor_copy(
-                w1s_perm_plane[h][:].rearrange("p (t m) -> p t m", t=4),
-                w1s_plane_b[:, W * h : W * (h + 1)].rearrange("p (m t) -> p t m", t=4),
+        def permute_planes():
+            permuted = keep.tile([P, HS], U8, name="w1s_perm_plane", align_bytes=64)
+            nc.vector.tensor_copy(
+                permuted[:].rearrange("p (h t m) -> p h t m", h=2, t=4),
+                w1s_plane_b.rearrange("p (h m t) -> p h t m", h=2, t=4),
             )
+            for h in range(2):
+                w1s_perm_plane[h] = permuted[:, W * h : W * (h + 1)]
 
         nc.sync.dma_start(offs_t[:], offs)
         load_planes_stacked(nc.sync, window, x_scales)
-        nc.sync.dma_start(
-            out=w1s_raw[0][:].rearrange("p (s l) -> p s l", s=PASSES),
-            in_=w1s_words.rearrange("s p l d -> p s (l d)")[:, :, 0 : 4 * W].bitcast(I32),
-        )
-        nc.sync.dma_start(
-            out=xw[:].rearrange("p (s t) -> p s t", s=PASSES),
-            in_=x_words.rearrange("s p t d -> p s (t d)").bitcast(I32),
-        )
+        for s in range(PASSES):
+            nc.sync.dma_start(
+                w1s_raw[0][:, W * s : W * (s + 1)], w1s_words[s].rearrange("p l d -> p (l d)")[:, 0 : 4 * W].bitcast(I32)
+            )
         load_planes_stacked(nc.sync, w1s_plane, w1s_scales)
+        for t0, t1 in [(0, P * TURNED_TILES), (P * TURNED_TILES, T)]:
+            nc.sync.dma_start(
+                out=xw[:].rearrange("p (s t) -> p s t", s=PASSES)[:, :, t0:t1],
+                in_=x_words.rearrange("s p t d -> p s (t d)").bitcast(I32)[:, :, t0:t1],
+            )
         w1_rows = w1_scales.rearrange("e s b i -> (e s) b i")
         load_planes_side_by_side(nc.sync, early_planes, w1_rows[0 : PASSES * EARLY])
         load_w1(0, 2)
         nc.vector.tensor_copy(slot_scales[:], xs_b.indirect(offs_t[:]))
         permute_words(0, nc.scalar.copy, "w1s_perm_0", [(0, 1), (1, 2)])
-        permute_plane(0, nc.gpsimd)
-        later_planes = reuse.tile([P, (E - EARLY) * PASSES * H // 4], I32, name="later_planes", offset=0, align_bytes=64)
+        permute_planes()
         slot_planes = [slot_scales[:], moved[:].bitcast(U8)]
         w2_plane = w2_planes[:].bitcast(U8)
         w2s_plane = w2s_planes[:].bitcast(U8)
-        nc.sync.dma_start(out=moved[0:LIVE_ROWS, :], in_=slot_scales[:].bitcast(I32)[4 : 4 + LIVE_ROWS, :])
+        nc.scalar.dma_start(out=moved[0:LIVE_ROWS, :], in_=slot_scales[:].bitcast(I32)[4 : 4 + LIVE_ROWS, :])
         for e0 in range(2, E, 2):
             if e0 == EARLY:
                 load_planes_side_by_side(nc.sync, later_planes, w1_rows[PASSES * EARLY :])
+            if e0 == E - 4:
                 load_planes_side_by_side(nc.sync, w2_planes, w2_scales.rearrange("e s b i -> (e s) b i"))
             load_w1(e0, e0 + 2)
         nc.sync.dma_start(
@@ -160,16 +165,16 @@ def tile_moe_shf_mlp_silu_kernel(
             out=w2_t[:].bitcast(I32).rearrange("p (e b) -> p e b", e=E),
             in_=w2_words.rearrange("e s p b -> p (e s) b").bitcast(I32),
         )
-        nc.sync.dma_start(out=gate_t[:].rearrange("p (r t) -> p r t", r=2), in_=gate.rearrange("r p t -> p r t"))
         nc.sync.dma_start(pos_t[0][:], pos1)
         nc.sync.dma_start(pos_t[1][:], pos2)
+        nc.sync.dma_start(gate_t[0][:], gate[0])
+        nc.sync.dma_start(gate_t[1][:], gate[1])
         nc.sync.dma_start(
             out=w2s_t[:].rearrange("p (s n) -> p s n", s=2), in_=w2s_words.rearrange("s p n d -> p s (n d)").bitcast(I32)
         )
         load_planes_side_by_side(nc.sync, w2s_planes, w2s_scales)
 
-        permute_plane(1, nc.gpsimd)
-        ident = keep.tile([P, P], F32, name="ident", tag="w1s_plane", align_bytes=64)
+        ident = keep.tile([P, P], F32, name="ident", align_bytes=64)
         make_identity(nc, ident[:])
         for e0, e1 in WORD_GATHERS:
             gather_words(e0, e1)
@@ -195,13 +200,13 @@ def tile_moe_shf_mlp_silu_kernel(
                 )
             return hidden
 
-        def turn(hidden, grouped, b0, b1, b):
+        def turn(hidden, grouped, b0, b1, b, copy):
             nb = b1 - b0
             words = hidden[:, W * b0 : W * b1].bitcast(F32)
             turned = bank(b)
             for j in range(2 * nb):
                 nc.tensor.transpose(turned[:, P * j : P * (j + 1)], words[:, P * j : P * (j + 1)], ident[:])
-            nc.vector.tensor_copy(
+            copy(
                 grouped[:, W * b0 : W * b1].bitcast(F32).rearrange("p (b r u) -> p b r u", b=nb, u=2),
                 turned[:, 0 : 2 * P * nb].rearrange("p (b u r) -> p b r u", b=nb, u=2),
             )
@@ -260,8 +265,26 @@ def tile_moe_shf_mlp_silu_kernel(
                 SILU,
             )
 
-        for j in range(HEAD_TILES):
-            first_layer_shared(j, 0, bank(3 + j))
+        hidden_shared = keep.tile([P, TURNED_TILES * W], BF16, name="hidden_shared", align_bytes=64)
+        for j in range(TURNED_TILES):
+            acc = bank(3 + j)
+            for s in range(PASSES):
+                nc.tensor.matmul_mx(
+                    out=acc[:],
+                    lhsT=xw[:, T * s + P * j : T * s + P * (j + 1)].bitcast(FP8X4),
+                    lhsT_scale=xs_b[4 * s : P, P * j : P * (j + 1)],
+                    rhs=w1s_raw[0][:, W * s : W * (s + 1)].bitcast(FP8X4),
+                    rhs_scale=w1s_plane_b[4 * s : P, 0:W],
+                    start=(s == 0), stop=(s == PASSES - 1),
+                )
+            nc.scalar.activation(
+                hidden_shared[:, W * j : W * (j + 1)].rearrange("r (u p e) -> r u p e", u=2, e=2),
+                acc[:].rearrange("r (p u e) -> r u p e", u=2, e=2),
+                SILU,
+            )
+        for j in range(TURNED_TILES, HEAD_TILES):
+            first_layer_shared(j, 0, bank((3 + j) % 6))
+        turn(hidden_shared, hs_chunk[(0, 0)], 0, TURNED_TILES, 7, nc.scalar.copy)
         pairs = E // 2
         hidden = {}
         grouped = {}
@@ -272,42 +295,42 @@ def tile_moe_shf_mlp_silu_kernel(
                 g = step - 1
                 grouped[g] = keep.tile([P, 2 * W], BF16, name="grouped_%d" % g, tag="grouped_%d" % g, align_bytes=64)
                 if g < pairs - 1:
-                    turn(hidden[g], grouped[g], 0, 2, 6 + g % 2)
+                    turn(hidden[g], grouped[g], 0, 2, 6 + g % 2, nc.scalar.copy if g < 2 else nc.vector.tensor_copy)
                 else:
-                    turn(hidden[g], grouped[g], 0, 1, 6)
-                    turn(hidden[g], grouped[g], 1, 2, 0)
+                    turn(hidden[g], grouped[g], 0, 1, 6, nc.vector.tensor_copy)
+                    turn(hidden[g], grouped[g], 1, 2, 0, nc.vector.tensor_copy)
             if 0 <= step - 2 < pairs:
                 quantize_routed(2 * step - 4, 2 * step - 2, grouped[step - 2])
         permute_words(1, nc.vector.tensor_copy, "grouped_%d" % (pairs - 3), [(0, 2)])
         for e0, e1, b in [(0, 4, 3), (4, 8, 1), (8, 10, 5)]:
             second_layer_routed(e0, e1, b)
-        last_banks = [0, 1, 5]
+        last_banks = [2, 0, 3, 1, 5, 2]
         last = [(j, 0) for j in range(HEAD_TILES, TILES)] + [(j, 1) for j in range(TILES)]
         for i, (j, h) in enumerate(last):
-            first_layer_shared(j, h, bank(last_banks[i % 3]))
+            first_layer_shared(j, h, bank(last_banks[i]))
 
         first_part = keep.tile([P, T], F32, name="first_part")
-        second_part = {}
+        fetched = keep.tile([P, T], F32, name="fetched")
+        second_part = keep.tile([P, T], F32, name="second_part")
         both = keep.tile([P, T], F32, name="both")
         result = keep.tile([P, T], F32, name="result")
         chunks = [(P * j0, P * j1) for j0, j1 in TOKEN_CHUNKS]
         hs_codes = {}
-        sums = {}
-
-        def fetch(part, r, t0, t1):
-            nc.vector.tensor_tensor(
-                part, y_sb[:].indirect(pos_t[r][:, t0 // 16 : t1 // 16]), gate_t[:, T * r + t0 : T * r + t1], MULT
-            )
-
-        def fetch_second(t0, t1, tag):
-            second_part[t0] = keep.tile([P, t1 - t0], F32, name="second_part_%d" % t0, tag=tag, align_bytes=64)
-            fetch(second_part[t0][:], 1, t0, t1)
 
         def quantize_shared(h, t0, t1):
             hs_codes[(h, t0)] = quantize("shared_%d_%d" % (h, t0), hs_chunk[(h, t0)][:], t1 - t0)
 
-        def second_layer_shared(t0, t1):
-            ys = bank(last_banks[last.index((t1 // P - 1, 1)) % 3])
+        def routed_sum(t0, t1):
+            listed = y_sb[:].indirect(pos_t[1][:, t0 // 16 : t1 // 16])
+            if t0 > 0:
+                nc.scalar.activation(fetched[:, t0:t1], listed, COPY)
+                listed = fetched[:, t0:t1]
+            nc.vector.tensor_tensor(second_part[:, t0:t1], listed, gate_t[1][:, t0:t1], MULT)
+            nc.vector.tensor_tensor(both[:, t0:t1], first_part[:, t0:t1], second_part[:, t0:t1], ADD)
+
+        def finish(t0, t1):
+            quantize_shared(1, t0, t1)
+            ys = bank(last_banks[last.index((t1 // P - 1, 1))])
             for h in range(2):
                 words, scales = hs_codes[(h, t0)]
                 nc.tensor.matmul_mx(
@@ -317,28 +340,14 @@ def tile_moe_shf_mlp_silu_kernel(
                     rhs=words[:].bitcast(FP8X4), rhs_scale=scales[:],
                     start=(h == 0), stop=(h == 1),
                 )
-            for j in range(t0 // P, t1 // P):
-                sums[P * j] = ys[:, P * j - t0 :]
-
-        def add_parts(t0, t1):
-            nc.vector.tensor_tensor(both[:, t0:t1], first_part[:, t0:t1], second_part[t0][:], ADD)
-
-        def finish(t0, t1):
-            nc.vector.tensor_tensor(result[:, t0:t1], sums[t0][:, 0 : t1 - t0], both[:, t0:t1], ADD)
+            nc.vector.tensor_tensor(result[:, t0:t1], ys[:, 0 : t1 - t0], both[:, t0:t1], ADD)
             nc.sync.dma_start(out[:, t0:t1], result[:, t0:t1])
 
-        cut = 2 * P
-        quantize_shared(0, *chunks[0])
-        fetch(first_part[:], 0, 0, T)
-        quantize_shared(0, *chunks[1])
-        fetch_second(0, cut, "hs_0_0")
-        quantize_shared(1, *chunks[0])
-        second_layer_shared(*chunks[0])
-        fetch_second(cut, T, "hs_1_0")
-        add_parts(0, cut)
-        quantize_shared(1, *chunks[1])
-        second_layer_shared(*chunks[1])
-        finish(0, cut)
-        add_parts(cut, T)
-        finish(cut, 4 * P)
-        finish(4 * P, T)
+        for t0, t1 in chunks:
+            quantize_shared(0, t0, t1)
+        nc.vector.tensor_tensor(first_part[:], y_sb[:].indirect(pos_t[0][:]), gate_t[0][:], MULT)
+        routed_sum(0, 2 * P)
+        finish(*chunks[0])
+        routed_sum(2 * P, T)
+        finish(*chunks[1])
+        finish(*chunks[2])

@@ -25,8 +25,8 @@ PASSES = K // W
 SLOTS = E * C
 TILES = T // P
 EXPERT_BYTES = PASSES * 2 * H
-SCALE_WINDOW = 1792
-LIVE_ROWS = 100
+SCALE_WINDOW = 1344
+BYTE_GATHERS = [(0, 3), (3, 6), (6, 10)]
 WORD_GATHERS = [(0, 3), (3, 6), (6, 8), (8, 10)]
 HEAD_TILES = 4
 TURNED_TILES = 2
@@ -67,12 +67,14 @@ def tile_moe_shf_mlp_silu_kernel(
                 )
 
         window = keep.tile([P, SCALE_WINDOW // 4], I32, name="window", align_bytes=64)
-        nc.gpsimd.memset(window[:, 0 : T // 4], 0)
+        nc.gpsimd.memset(window[:, 0 : PASSES * T // 4], 0)
         w1s_plane = zeroed_plane("w1s_plane", HS, nc.gpsimd)
+        warm = keep.tile([P, 2], F32, name="warm")
+        nc.vector.memset(warm[:, 0:1], 0.0)
+        nc.scalar.activation(warm[:, 1:2], warm[:, 0:1], SILU)
         early_planes = zeroed_plane("early_planes", EARLY * PASSES * H, nc.vector)
-        moved = zeroed_plane("moved", SLOTS, nc.vector)
         later_planes = zeroed_plane("later_planes", (E - EARLY) * PASSES * H, nc.vector)
-        nc.gpsimd.memset(window[:, T // 4 :], 0)
+        nc.gpsimd.memset(window[:, PASSES * T // 4 :], 0)
         w2_planes = zeroed_plane("w2_planes", E * N, nc.gpsimd)
         w2s_planes = zeroed_plane("w2s_planes", 2 * N, nc.gpsimd)
 
@@ -86,7 +88,7 @@ def tile_moe_shf_mlp_silu_kernel(
         w2_t = keep.tile([P, 2 * E * N], U8, name="w2_t", align_bytes=64)
         w2s_t = keep.tile([P, 2 * N], I32, name="w2s_t", align_bytes=64)
         gate_t = [keep.tile([P, T], F32, name="gate_%d" % r) for r in range(2)]
-        slot_scales = keep.tile([P, SLOTS], U8, name="slot_scales", align_bytes=64)
+        slot_scales = {}
         slot_words = {}
         w1_t = {}
 
@@ -109,6 +111,16 @@ def tile_moe_shf_mlp_silu_kernel(
                     slot_words[(e, s)] = gathered[:, C * (e - e0) : C * (e - e0 + 1)]
 
         xs_b = window[:].bitcast(U8)
+
+        def gather_bytes(e0, e1, into, first):
+            width = T if e1 - e0 < 4 else SCALE_WINDOW - T
+            held = into.shape[1] // PASSES
+            for s in range(PASSES):
+                gathered = into[:, held * s + C * (e0 - first) : held * s + C * (e1 - first)]
+                nc.vector.tensor_copy(gathered, xs_b[:, T * s : T * s + width].indirect(offs_t[:, 8 * e0 : 8 * e1]))
+                for e in range(e0, e1):
+                    slot_scales[(e, s)] = gathered[:, C * (e - e0) : C * (e - e0 + 1)]
+
         w1s_plane_b = w1s_plane[:].bitcast(U8)
         w1s_perm = {}
         w1s_perm_plane = {}
@@ -130,7 +142,7 @@ def tile_moe_shf_mlp_silu_kernel(
                 w1s_perm_plane[h] = permuted[:, W * h : W * (h + 1)]
 
         nc.sync.dma_start(offs_t[:], offs)
-        load_planes_stacked(nc.sync, window, x_scales)
+        load_planes_side_by_side(nc.sync, window[:, 0 : PASSES * T // 4], x_scales)
         for s in range(PASSES):
             nc.sync.dma_start(
                 w1s_raw[0][:, W * s : W * (s + 1)], w1s_words[s].rearrange("p l d -> p (l d)")[:, 0 : 4 * W].bitcast(I32)
@@ -144,13 +156,10 @@ def tile_moe_shf_mlp_silu_kernel(
         w1_rows = w1_scales.rearrange("e s b i -> (e s) b i")
         load_planes_side_by_side(nc.sync, early_planes, w1_rows[0 : PASSES * EARLY])
         load_w1(0, 2)
-        nc.vector.tensor_copy(slot_scales[:], xs_b.indirect(offs_t[:]))
         permute_words(0, nc.scalar.copy, "w1s_perm_0", [(0, 1), (1, 2)])
         permute_planes()
-        slot_planes = [slot_scales[:], moved[:].bitcast(U8)]
         w2_plane = w2_planes[:].bitcast(U8)
         w2s_plane = w2s_planes[:].bitcast(U8)
-        nc.scalar.dma_start(out=moved[0:LIVE_ROWS, :], in_=slot_scales[:].bitcast(I32)[4 : 4 + LIVE_ROWS, :])
         for e0 in range(2, E, 2):
             if e0 == EARLY:
                 load_planes_side_by_side(nc.sync, later_planes, w1_rows[PASSES * EARLY :])
@@ -176,8 +185,10 @@ def tile_moe_shf_mlp_silu_kernel(
 
         ident = keep.tile([P, P], F32, name="ident", align_bytes=64)
         make_identity(nc, ident[:])
-        for e0, e1 in WORD_GATHERS:
-            gather_words(e0, e1)
+        first = BYTE_GATHERS[0][1]
+        scales_first = keep.tile([P, PASSES * first * C], U8, name="scales_first", align_bytes=64)
+        gather_bytes(*BYTE_GATHERS[0], scales_first[:], 0)
+        gather_words(*WORD_GATHERS[0])
 
         def first_layer_routed(e0, e1):
             hidden = keep.tile([P, (e1 - e0) * W], BF16, name="hidden_%d" % e0, align_bytes=64)
@@ -188,7 +199,7 @@ def tile_moe_shf_mlp_silu_kernel(
                     nc.tensor.matmul_mx(
                         out=acc[:],
                         lhsT=slot_words[(e, s)].bitcast(FP8X4),
-                        lhsT_scale=slot_planes[s][:, C * e : C * (e + 1)],
+                        lhsT_scale=slot_scales[(e, s)],
                         rhs=w1_t[e][:, 2 * H * s : 2 * H * (s + 1)].bitcast(FP4X4),
                         rhs_scale=planes[:].bitcast(U8)[:, H * a : H * (a + 1)],
                         start=(s == 0), stop=(s == PASSES - 1),
@@ -256,7 +267,7 @@ def tile_moe_shf_mlp_silu_kernel(
                         lhsT=w1s_perm[h][:, W * s + P * t : W * s + P * (t + 1)].bitcast(FP8X4),
                         lhsT_scale=w1s_perm_plane[h][4 * s : P, P * t : P * (t + 1)],
                         rhs=xw[:, T * s + P * j : T * s + P * (j + 1)].bitcast(FP8X4),
-                        rhs_scale=xs_b[4 * s : P, P * j : P * (j + 1)],
+                        rhs_scale=xs_b[:, T * s + P * j : T * s + P * (j + 1)],
                         start=(s == 0), stop=(s == PASSES - 1),
                     )
             nc.scalar.activation(
@@ -272,7 +283,7 @@ def tile_moe_shf_mlp_silu_kernel(
                 nc.tensor.matmul_mx(
                     out=acc[:],
                     lhsT=xw[:, T * s + P * j : T * s + P * (j + 1)].bitcast(FP8X4),
-                    lhsT_scale=xs_b[4 * s : P, P * j : P * (j + 1)],
+                    lhsT_scale=xs_b[:, T * s + P * j : T * s + P * (j + 1)],
                     rhs=w1s_raw[0][:, W * s : W * (s + 1)].bitcast(FP8X4),
                     rhs_scale=w1s_plane_b[4 * s : P, 0:W],
                     start=(s == 0), stop=(s == PASSES - 1),
@@ -282,6 +293,12 @@ def tile_moe_shf_mlp_silu_kernel(
                 acc[:].rearrange("r (p u e) -> r u p e", u=2, e=2),
                 SILU,
             )
+        scales_rest = keep.tile([P, PASSES * (E - first) * C], U8, name="scales_rest", tag="w1s_plane", align_bytes=64)
+        gather_bytes(*BYTE_GATHERS[1], scales_rest[:], first)
+        gather_words(*WORD_GATHERS[1])
+        gather_bytes(*BYTE_GATHERS[2], scales_rest[:], first)
+        gather_words(*WORD_GATHERS[2])
+        gather_words(*WORD_GATHERS[3])
         for j in range(TURNED_TILES, HEAD_TILES):
             first_layer_shared(j, 0, bank((3 + j) % 6))
         turn(hidden_shared, hs_chunk[(0, 0)], 0, TURNED_TILES, 7, nc.scalar.copy)
@@ -295,7 +312,7 @@ def tile_moe_shf_mlp_silu_kernel(
                 g = step - 1
                 grouped[g] = keep.tile([P, 2 * W], BF16, name="grouped_%d" % g, tag="grouped_%d" % g, align_bytes=64)
                 if g < pairs - 1:
-                    turn(hidden[g], grouped[g], 0, 2, 6 + g % 2, nc.scalar.copy if g < 2 else nc.vector.tensor_copy)
+                    turn(hidden[g], grouped[g], 0, 2, 6 + g % 2, nc.scalar.copy if g < 3 else nc.vector.tensor_copy)
                 else:
                     turn(hidden[g], grouped[g], 0, 1, 6, nc.vector.tensor_copy)
                     turn(hidden[g], grouped[g], 1, 2, 0, nc.vector.tensor_copy)

@@ -41,6 +41,7 @@ def tile_moe_shf_mlp_silu_kernel(
     nc = tc.nc
     with ExitStack() as ctx:
         keep = ctx.enter_context(tc.tile_pool(name="keep", bufs=1))
+        reuse = ctx.enter_context(tc.tile_pool(name="reuse", bufs=1))
         psum = ctx.enter_context(tc.psum_pool(name="psum", bufs=1))
 
         def bank(b):
@@ -68,10 +69,9 @@ def tile_moe_shf_mlp_silu_kernel(
 
         window = keep.tile([P, SCALE_WINDOW // 4], I32, name="window", align_bytes=64)
         nc.gpsimd.memset(window[:, 0 : PASSES * T // 4], 0)
-        w1s_plane = zeroed_plane("w1s_plane", HS, nc.gpsimd)
-        warm = keep.tile([P, 2], F32, name="warm")
-        nc.vector.memset(warm[:, 0:1], 0.0)
-        nc.scalar.activation(warm[:, 1:2], warm[:, 0:1], SILU)
+        rest_bytes = PASSES * (E - BYTE_GATHERS[0][1]) * C
+        w1s_plane = reuse.tile([P, HS // 4], I32, name="w1s_plane", offset=rest_bytes - HS // 2, align_bytes=64)
+        nc.gpsimd.memset(w1s_plane[:], 0)
         early_planes = zeroed_plane("early_planes", EARLY * PASSES * H, nc.vector)
         later_planes = zeroed_plane("later_planes", (E - EARLY) * PASSES * H, nc.vector)
         nc.gpsimd.memset(window[:, PASSES * T // 4 :], 0)
@@ -81,7 +81,7 @@ def tile_moe_shf_mlp_silu_kernel(
         offs_t = keep.tile([P, SLOTS // 16], U16, name="offs_t")
         xw = keep.tile([P, PASSES * T], I32, name="xw", align_bytes=64)
         w1s_raw = [
-            keep.tile([P, PASSES * W], I32, name="w1s_raw_0", align_bytes=64),
+            keep.tile([P, PASSES * W], I32, name="w1s_raw_0", tag="w1s_raw_0", align_bytes=64),
             keep.tile([P, PASSES * W], I32, name="w1s_raw_1", align_bytes=64),
         ]
         pos_t = [keep.tile([P, T // 16], U16, name="pos%d_t" % (r + 1)) for r in range(2)]
@@ -101,11 +101,12 @@ def tile_moe_shf_mlp_silu_kernel(
                 in_=w1_words[e0:e1].rearrange("e s p b -> p (e s) b").bitcast(I32),
             )
 
-        def gather_words(e0, e1):
+        def gather_words(e0, e1, into, first):
+            held = into.shape[1] // PASSES
             for s in range(PASSES):
-                gathered = keep.tile([P, (e1 - e0) * C], U32, name="slot_words_%d_%d" % (e0, s), align_bytes=64)
+                gathered = into[:, held * s + C * (e0 - first) : held * s + C * (e1 - first)]
                 nc.vector.tensor_copy(
-                    gathered[:], xw[:, T * s : T * (s + 1)].bitcast(U32).indirect(offs_t[:, 8 * e0 : 8 * e1])
+                    gathered, xw[:, T * s : T * (s + 1)].bitcast(U32).indirect(offs_t[:, 8 * e0 : 8 * e1])
                 )
                 for e in range(e0, e1):
                     slot_words[(e, s)] = gathered[:, C * (e - e0) : C * (e - e0 + 1)]
@@ -134,12 +135,12 @@ def tile_moe_shf_mlp_silu_kernel(
 
         def permute_planes():
             permuted = keep.tile([P, HS], U8, name="w1s_perm_plane", align_bytes=64)
-            nc.vector.tensor_copy(
-                permuted[:].rearrange("p (h t m) -> p h t m", h=2, t=4),
-                w1s_plane_b.rearrange("p (h m t) -> p h t m", h=2, t=4),
-            )
             for h in range(2):
                 w1s_perm_plane[h] = permuted[:, W * h : W * (h + 1)]
+                nc.gpsimd.tensor_copy(
+                    w1s_perm_plane[h].rearrange("p (t m) -> p t m", t=4),
+                    w1s_plane_b[:, W * h : W * (h + 1)].rearrange("p (m t) -> p t m", t=4),
+                )
 
         nc.sync.dma_start(offs_t[:], offs)
         load_planes_side_by_side(nc.sync, window[:, 0 : PASSES * T // 4], x_scales)
@@ -156,7 +157,7 @@ def tile_moe_shf_mlp_silu_kernel(
         w1_rows = w1_scales.rearrange("e s b i -> (e s) b i")
         load_planes_side_by_side(nc.sync, early_planes, w1_rows[0 : PASSES * EARLY])
         load_w1(0, 2)
-        permute_words(0, nc.scalar.copy, "w1s_perm_0", [(0, 1), (1, 2)])
+        permute_words(0, nc.gpsimd.tensor_copy, "w1s_perm_0", [(0, 1), (1, 2)])
         permute_planes()
         w2_plane = w2_planes[:].bitcast(U8)
         w2s_plane = w2s_planes[:].bitcast(U8)
@@ -188,7 +189,8 @@ def tile_moe_shf_mlp_silu_kernel(
         first = BYTE_GATHERS[0][1]
         scales_first = keep.tile([P, PASSES * first * C], U8, name="scales_first", align_bytes=64)
         gather_bytes(*BYTE_GATHERS[0], scales_first[:], 0)
-        gather_words(*WORD_GATHERS[0])
+        words_first = keep.tile([P, PASSES * first * C], U32, name="words_first", align_bytes=64)
+        gather_words(*WORD_GATHERS[0], words_first[:], 0)
 
         def first_layer_routed(e0, e1):
             hidden = keep.tile([P, (e1 - e0) * W], BF16, name="hidden_%d" % e0, align_bytes=64)
@@ -293,12 +295,13 @@ def tile_moe_shf_mlp_silu_kernel(
                 acc[:].rearrange("r (p u e) -> r u p e", u=2, e=2),
                 SILU,
             )
-        scales_rest = keep.tile([P, PASSES * (E - first) * C], U8, name="scales_rest", tag="w1s_plane", align_bytes=64)
+        scales_rest = reuse.tile([P, rest_bytes], U8, name="scales_rest", offset=0, align_bytes=64)
+        words_rest = reuse.tile([P, rest_bytes], U32, name="words_rest", offset=rest_bytes, align_bytes=64)
         gather_bytes(*BYTE_GATHERS[1], scales_rest[:], first)
-        gather_words(*WORD_GATHERS[1])
+        gather_words(*WORD_GATHERS[1], words_rest[:], first)
         gather_bytes(*BYTE_GATHERS[2], scales_rest[:], first)
-        gather_words(*WORD_GATHERS[2])
-        gather_words(*WORD_GATHERS[3])
+        gather_words(*WORD_GATHERS[2], words_rest[:], first)
+        gather_words(*WORD_GATHERS[3], words_rest[:], first)
         for j in range(TURNED_TILES, HEAD_TILES):
             first_layer_shared(j, 0, bank((3 + j) % 6))
         turn(hidden_shared, hs_chunk[(0, 0)], 0, TURNED_TILES, 7, nc.scalar.copy)

@@ -26,10 +26,10 @@ SLOTS = E * C
 TILES = T // P
 EXPERT_BYTES = PASSES * 2 * H
 SCALE_WINDOW = 1344
-BYTE_GATHERS = [(0, 3), (3, 6), (6, 10)]
-WORD_GATHERS = [(0, 3), (3, 6), (6, 8), (8, 10)]
-HEAD_TILES = 4
-TURNED_TILES = 2
+BYTE_GATHERS = [(0, 3), (3, 7), (7, 10)]
+WORD_GATHERS = [(0, 2), (2, 4), (4, 7), (7, 10)]
+HEAD_TILES = 5
+FIRST_TILES = 2
 EARLY = 4
 TOKEN_CHUNKS = [(0, 2), (2, 4), (4, 5)]
 
@@ -41,14 +41,13 @@ def tile_moe_shf_mlp_silu_kernel(
     nc = tc.nc
     with ExitStack() as ctx:
         keep = ctx.enter_context(tc.tile_pool(name="keep", bufs=1))
-        reuse = ctx.enter_context(tc.tile_pool(name="reuse", bufs=1))
         psum = ctx.enter_context(tc.psum_pool(name="psum", bufs=1))
 
         def bank(b):
             return psum.tile([P, W], F32, name="bank_%d" % b, tag="bank_%d" % b)
 
         def zeroed_plane(name, nbytes, engine):
-            plane = keep.tile([P, nbytes // 4], I32, name=name, tag=name, align_bytes=64)
+            plane = keep.tile([P, nbytes // 4], I32, name=name, tag=name, align_bytes=256)
             engine.memset(plane[:], 0)
             return plane
 
@@ -67,33 +66,34 @@ def tile_moe_shf_mlp_silu_kernel(
                     out=plane[32 * q : 32 * q + 8, 0:width], in_=rows[:, 4 * q : 4 * q + 4, :].bitcast(I32)
                 )
 
-        window = keep.tile([P, SCALE_WINDOW // 4], I32, name="window", align_bytes=64)
+        window = keep.tile([P, SCALE_WINDOW // 4], I32, name="window", align_bytes=256)
         nc.gpsimd.memset(window[:, 0 : PASSES * T // 4], 0)
-        rest_bytes = PASSES * (E - BYTE_GATHERS[0][1]) * C
-        w1s_plane = reuse.tile([P, HS // 4], I32, name="w1s_plane", offset=rest_bytes - HS // 2, align_bytes=64)
-        nc.gpsimd.memset(w1s_plane[:], 0)
+        w1s_plane = zeroed_plane("w1s_plane", HS, nc.gpsimd)
+        warm = keep.tile([P, 2], F32, name="warm", align_bytes=256)
+        nc.vector.memset(warm[:, 0:1], 0.0)
+        nc.scalar.activation(warm[:, 1:2], warm[:, 0:1], SILU)
         early_planes = zeroed_plane("early_planes", EARLY * PASSES * H, nc.vector)
         later_planes = zeroed_plane("later_planes", (E - EARLY) * PASSES * H, nc.vector)
         nc.gpsimd.memset(window[:, PASSES * T // 4 :], 0)
         w2_planes = zeroed_plane("w2_planes", E * N, nc.gpsimd)
         w2s_planes = zeroed_plane("w2s_planes", 2 * N, nc.gpsimd)
 
-        offs_t = keep.tile([P, SLOTS // 16], U16, name="offs_t")
-        xw = keep.tile([P, PASSES * T], I32, name="xw", align_bytes=64)
+        offs_t = keep.tile([P, SLOTS // 16], U16, name="offs_t", align_bytes=256)
+        xw = keep.tile([P, PASSES * T], I32, name="xw", align_bytes=256)
         w1s_raw = [
-            keep.tile([P, PASSES * W], I32, name="w1s_raw_0", tag="w1s_raw_0", align_bytes=64),
-            keep.tile([P, PASSES * W], I32, name="w1s_raw_1", align_bytes=64),
+            keep.tile([P, PASSES * W], I32, name="w1s_raw_0", tag="w1s_raw_0", align_bytes=256),
+            keep.tile([P, PASSES * W], I32, name="w1s_raw_1", align_bytes=256),
         ]
-        pos_t = [keep.tile([P, T // 16], U16, name="pos%d_t" % (r + 1)) for r in range(2)]
-        w2_t = keep.tile([P, 2 * E * N], U8, name="w2_t", align_bytes=64)
-        w2s_t = keep.tile([P, 2 * N], I32, name="w2s_t", align_bytes=64)
-        gate_t = [keep.tile([P, T], F32, name="gate_%d" % r) for r in range(2)]
+        pos_t = [keep.tile([P, T // 16], U16, name="pos%d_t" % (r + 1), align_bytes=256) for r in range(2)]
+        w2_t = keep.tile([P, 2 * E * N], U8, name="w2_t", align_bytes=256)
+        w2s_t = keep.tile([P, 2 * N], I32, name="w2s_t", align_bytes=256)
+        gate_t = [keep.tile([P, T], F32, name="gate_%d" % r, align_bytes=256) for r in range(2)]
         slot_scales = {}
         slot_words = {}
         w1_t = {}
 
         def load_w1(e0, e1):
-            pair = keep.tile([P, (e1 - e0) * EXPERT_BYTES], U8, name="w1_%d" % e0, align_bytes=64)
+            pair = keep.tile([P, (e1 - e0) * EXPERT_BYTES], U8, name="w1_%d" % e0, align_bytes=256)
             for e in range(e0, e1):
                 w1_t[e] = pair[:, EXPERT_BYTES * (e - e0) : EXPERT_BYTES * (e - e0 + 1)]
             nc.sync.dma_start(
@@ -127,17 +127,17 @@ def tile_moe_shf_mlp_silu_kernel(
         w1s_perm_plane = {}
 
         def permute_words(h, engine, tag, cuts):
-            w1s_perm[h] = keep.tile([P, PASSES * W], I32, name="w1s_perm_%d" % h, tag=tag, align_bytes=64)
+            w1s_perm[h] = keep.tile([P, PASSES * W], I32, name="w1s_perm_%d" % h, tag=tag, align_bytes=256)
             dst = w1s_perm[h][:].bitcast(U32).rearrange("p (s t a i) -> p s a t i", s=PASSES, t=4, i=4)
             src = w1s_raw[h][:].bitcast(U32).rearrange("p (s a i t) -> p s a t i", s=PASSES, t=4, i=4)
             for s0, s1 in cuts:
                 engine(dst[:, s0:s1], src[:, s0:s1])
 
         def permute_planes():
-            permuted = keep.tile([P, HS], U8, name="w1s_perm_plane", align_bytes=64)
+            permuted = keep.tile([P, HS], U8, name="w1s_perm_plane", align_bytes=256)
             for h in range(2):
                 w1s_perm_plane[h] = permuted[:, W * h : W * (h + 1)]
-                nc.gpsimd.tensor_copy(
+                nc.vector.tensor_copy(
                     w1s_perm_plane[h].rearrange("p (t m) -> p t m", t=4),
                     w1s_plane_b[:, W * h : W * (h + 1)].rearrange("p (m t) -> p t m", t=4),
                 )
@@ -149,7 +149,7 @@ def tile_moe_shf_mlp_silu_kernel(
                 w1s_raw[0][:, W * s : W * (s + 1)], w1s_words[s].rearrange("p l d -> p (l d)")[:, 0 : 4 * W].bitcast(I32)
             )
         load_planes_stacked(nc.sync, w1s_plane, w1s_scales)
-        for t0, t1 in [(0, P * TURNED_TILES), (P * TURNED_TILES, T)]:
+        for t0, t1 in [(0, P * FIRST_TILES), (P * FIRST_TILES, T)]:
             nc.sync.dma_start(
                 out=xw[:].rearrange("p (s t) -> p s t", s=PASSES)[:, :, t0:t1],
                 in_=x_words.rearrange("s p t d -> p s (t d)").bitcast(I32)[:, :, t0:t1],
@@ -157,7 +157,9 @@ def tile_moe_shf_mlp_silu_kernel(
         w1_rows = w1_scales.rearrange("e s b i -> (e s) b i")
         load_planes_side_by_side(nc.sync, early_planes, w1_rows[0 : PASSES * EARLY])
         load_w1(0, 2)
-        permute_words(0, nc.gpsimd.tensor_copy, "w1s_perm_0", [(0, 1), (1, 2)])
+        permute_words(0, nc.scalar.copy, "w1s_perm_0", [(0, 1), (1, 2)])
+        scales_head = keep.tile([P, PASSES * BYTE_GATHERS[0][1] * C], U8, name="scales_head", align_bytes=256)
+        gather_bytes(*BYTE_GATHERS[0], scales_head[:], 0)
         permute_planes()
         w2_plane = w2_planes[:].bitcast(U8)
         w2s_plane = w2s_planes[:].bitcast(U8)
@@ -184,16 +186,17 @@ def tile_moe_shf_mlp_silu_kernel(
         )
         load_planes_side_by_side(nc.sync, w2s_planes, w2s_scales)
 
-        ident = keep.tile([P, P], F32, name="ident", align_bytes=64)
+        ident = keep.tile([P, P], F32, name="ident", align_bytes=256)
         make_identity(nc, ident[:])
-        first = BYTE_GATHERS[0][1]
-        scales_first = keep.tile([P, PASSES * first * C], U8, name="scales_first", align_bytes=64)
-        gather_bytes(*BYTE_GATHERS[0], scales_first[:], 0)
-        words_first = keep.tile([P, PASSES * first * C], U32, name="words_first", align_bytes=64)
-        gather_words(*WORD_GATHERS[0], words_first[:], 0)
+        e0, e1 = BYTE_GATHERS[1]
+        scales_middle = keep.tile([P, PASSES * (e1 - e0) * C], U8, name="scales_middle", tag="w1s_plane", align_bytes=256)
+        gather_bytes(e0, e1, scales_middle[:], e0)
+        slot_words_all = keep.tile([P, PASSES * SLOTS], U32, name="slot_words_all", align_bytes=256)
+        for e0, e1 in WORD_GATHERS:
+            gather_words(e0, e1, slot_words_all[:], 0)
 
         def first_layer_routed(e0, e1):
-            hidden = keep.tile([P, (e1 - e0) * W], BF16, name="hidden_%d" % e0, align_bytes=64)
+            hidden = keep.tile([P, (e1 - e0) * W], BF16, name="hidden_%d" % e0, tag="hidden_%d" % e0, align_bytes=256)
             for e in range(e0, e1):
                 acc = bank(e % 6)
                 for s in range(PASSES):
@@ -225,8 +228,8 @@ def tile_moe_shf_mlp_silu_kernel(
             )
 
         def quantize(name, values, width):
-            words = keep.tile([P, width], U32, name="codes_" + name, align_bytes=64)
-            scales = keep.tile([P, width], U8, name="scales_" + name, align_bytes=64)
+            words = keep.tile([P, width], U32, name="codes_" + name, align_bytes=256)
+            scales = keep.tile([P, width], U8, name="scales_" + name, align_bytes=256)
             nc.vector.quantize_mx(out=words[:].bitcast(FP8X4), scales=scales[:], in_=values)
             return words, scales
 
@@ -237,7 +240,7 @@ def tile_moe_shf_mlp_silu_kernel(
             for e in range(e0, e1):
                 codes[e] = (words[:, C * (e - e0) : C * (e - e0 + 1)], scales[:, C * (e - e0) : C * (e - e0 + 1)])
 
-        y_sb = keep.tile([P, SLOTS], F32, name="y_sb")
+        y_sb = keep.tile([P, SLOTS], F32, name="y_sb", align_bytes=256)
 
         def second_layer_routed(e0, e1, b):
             y = bank(b)
@@ -256,7 +259,7 @@ def tile_moe_shf_mlp_silu_kernel(
         for h in range(2):
             for j0, j1 in TOKEN_CHUNKS:
                 name = "hs_%d_%d" % (h, j0)
-                chunk = keep.tile([P, (j1 - j0) * W], BF16, name=name, tag=name, align_bytes=64)
+                chunk = keep.tile([P, (j1 - j0) * W], BF16, name=name, tag=name, align_bytes=256)
                 hs_chunk[(h, P * j0)] = chunk
                 for j in range(j0, j1):
                     hs[(h, j)] = chunk[:, W * (j - j0) : W * (j - j0 + 1)]
@@ -278,33 +281,8 @@ def tile_moe_shf_mlp_silu_kernel(
                 SILU,
             )
 
-        hidden_shared = keep.tile([P, TURNED_TILES * W], BF16, name="hidden_shared", align_bytes=64)
-        for j in range(TURNED_TILES):
-            acc = bank(3 + j)
-            for s in range(PASSES):
-                nc.tensor.matmul_mx(
-                    out=acc[:],
-                    lhsT=xw[:, T * s + P * j : T * s + P * (j + 1)].bitcast(FP8X4),
-                    lhsT_scale=xs_b[:, T * s + P * j : T * s + P * (j + 1)],
-                    rhs=w1s_raw[0][:, W * s : W * (s + 1)].bitcast(FP8X4),
-                    rhs_scale=w1s_plane_b[4 * s : P, 0:W],
-                    start=(s == 0), stop=(s == PASSES - 1),
-                )
-            nc.scalar.activation(
-                hidden_shared[:, W * j : W * (j + 1)].rearrange("r (u p e) -> r u p e", u=2, e=2),
-                acc[:].rearrange("r (p u e) -> r u p e", u=2, e=2),
-                SILU,
-            )
-        scales_rest = reuse.tile([P, rest_bytes], U8, name="scales_rest", offset=0, align_bytes=64)
-        words_rest = reuse.tile([P, rest_bytes], U32, name="words_rest", offset=rest_bytes, align_bytes=64)
-        gather_bytes(*BYTE_GATHERS[1], scales_rest[:], first)
-        gather_words(*WORD_GATHERS[1], words_rest[:], first)
-        gather_bytes(*BYTE_GATHERS[2], scales_rest[:], first)
-        gather_words(*WORD_GATHERS[2], words_rest[:], first)
-        gather_words(*WORD_GATHERS[3], words_rest[:], first)
-        for j in range(TURNED_TILES, HEAD_TILES):
-            first_layer_shared(j, 0, bank((3 + j) % 6))
-        turn(hidden_shared, hs_chunk[(0, 0)], 0, TURNED_TILES, 7, nc.scalar.copy)
+        for j in range(HEAD_TILES):
+            first_layer_shared(j, 0, bank((1 + j) % 6))
         pairs = E // 2
         hidden = {}
         grouped = {}
@@ -313,27 +291,31 @@ def tile_moe_shf_mlp_silu_kernel(
                 hidden[step] = first_layer_routed(2 * step, 2 * step + 2)
             if 0 <= step - 1 < pairs:
                 g = step - 1
-                grouped[g] = keep.tile([P, 2 * W], BF16, name="grouped_%d" % g, tag="grouped_%d" % g, align_bytes=64)
+                grouped[g] = keep.tile([P, 2 * W], BF16, name="grouped_%d" % g, tag="grouped_%d" % g, align_bytes=256)
                 if g < pairs - 1:
                     turn(hidden[g], grouped[g], 0, 2, 6 + g % 2, nc.scalar.copy if g < 3 else nc.vector.tensor_copy)
                 else:
                     turn(hidden[g], grouped[g], 0, 1, 6, nc.vector.tensor_copy)
                     turn(hidden[g], grouped[g], 1, 2, 0, nc.vector.tensor_copy)
+            if step == 1:
+                e0, e1 = BYTE_GATHERS[2]
+                scales_last = keep.tile([P, PASSES * (e1 - e0) * C], U8, name="scales_last", tag="hidden_0", align_bytes=256)
+                gather_bytes(e0, e1, scales_last[:], e0)
             if 0 <= step - 2 < pairs:
                 quantize_routed(2 * step - 4, 2 * step - 2, grouped[step - 2])
-        permute_words(1, nc.vector.tensor_copy, "grouped_%d" % (pairs - 3), [(0, 2)])
+        permute_words(1, nc.scalar.copy, "hidden_%d" % (E - 4), [(0, 1), (1, 2)])
         for e0, e1, b in [(0, 4, 3), (4, 8, 1), (8, 10, 5)]:
             second_layer_routed(e0, e1, b)
-        last_banks = [2, 0, 3, 1, 5, 2]
+        last_banks = [0, 3, 1, 5, 0]
         last = [(j, 0) for j in range(HEAD_TILES, TILES)] + [(j, 1) for j in range(TILES)]
         for i, (j, h) in enumerate(last):
             first_layer_shared(j, h, bank(last_banks[i]))
 
-        first_part = keep.tile([P, T], F32, name="first_part")
-        fetched = keep.tile([P, T], F32, name="fetched")
-        second_part = keep.tile([P, T], F32, name="second_part")
-        both = keep.tile([P, T], F32, name="both")
-        result = keep.tile([P, T], F32, name="result")
+        first_part = keep.tile([P, T], F32, name="first_part", align_bytes=256)
+        fetched = keep.tile([P, T], F32, name="fetched", align_bytes=256)
+        second_part = keep.tile([P, T], F32, name="second_part", align_bytes=256)
+        both = keep.tile([P, T], F32, name="both", align_bytes=256)
+        result = keep.tile([P, T], F32, name="result", align_bytes=256)
         chunks = [(P * j0, P * j1) for j0, j1 in TOKEN_CHUNKS]
         hs_codes = {}
 

@@ -69,9 +69,6 @@ def tile_moe_shf_mlp_silu_kernel(
         window = keep.tile([P, SCALE_WINDOW // 4], I32, name="window", align_bytes=256)
         nc.gpsimd.memset(window[:, 0 : PASSES * T // 4], 0)
         w1s_plane = zeroed_plane("w1s_plane", HS, nc.gpsimd)
-        warm = keep.tile([P, 2], F32, name="warm", align_bytes=256)
-        nc.vector.memset(warm[:, 0:1], 0.0)
-        nc.scalar.activation(warm[:, 1:2], warm[:, 0:1], SILU)
         early_planes = zeroed_plane("early_planes", EARLY * PASSES * H, nc.vector)
         later_planes = zeroed_plane("later_planes", (E - EARLY) * PASSES * H, nc.vector)
         nc.gpsimd.memset(window[:, PASSES * T // 4 :], 0)
@@ -137,7 +134,7 @@ def tile_moe_shf_mlp_silu_kernel(
             permuted = keep.tile([P, HS], U8, name="w1s_perm_plane", align_bytes=256)
             for h in range(2):
                 w1s_perm_plane[h] = permuted[:, W * h : W * (h + 1)]
-                nc.vector.tensor_copy(
+                nc.gpsimd.tensor_copy(
                     w1s_perm_plane[h].rearrange("p (t m) -> p t m", t=4),
                     w1s_plane_b[:, W * h : W * (h + 1)].rearrange("p (m t) -> p t m", t=4),
                 )
@@ -157,7 +154,7 @@ def tile_moe_shf_mlp_silu_kernel(
         w1_rows = w1_scales.rearrange("e s b i -> (e s) b i")
         load_planes_side_by_side(nc.sync, early_planes, w1_rows[0 : PASSES * EARLY])
         load_w1(0, 2)
-        permute_words(0, nc.scalar.copy, "w1s_perm_0", [(0, 1), (1, 2)])
+        permute_words(0, nc.gpsimd.tensor_copy, "w1s_perm_0", [(0, 1), (1, 2)])
         scales_head = keep.tile([P, PASSES * BYTE_GATHERS[0][1] * C], U8, name="scales_head", align_bytes=256)
         gather_bytes(*BYTE_GATHERS[0], scales_head[:], 0)
         permute_planes()
@@ -189,7 +186,7 @@ def tile_moe_shf_mlp_silu_kernel(
         ident = keep.tile([P, P], F32, name="ident", align_bytes=256)
         make_identity(nc, ident[:])
         e0, e1 = BYTE_GATHERS[1]
-        scales_middle = keep.tile([P, PASSES * (e1 - e0) * C], U8, name="scales_middle", tag="w1s_plane", align_bytes=256)
+        scales_middle = keep.tile([P, PASSES * (e1 - e0) * C], U8, name="scales_middle", align_bytes=256)
         gather_bytes(e0, e1, scales_middle[:], e0)
         slot_words_all = keep.tile([P, PASSES * SLOTS], U32, name="slot_words_all", align_bytes=256)
         for e0, e1 in WORD_GATHERS:

@@ -72,7 +72,6 @@ def tile_moe_shf_mlp_silu_kernel(
         early_planes = zeroed_plane("early_planes", EARLY * PASSES * H, nc.vector)
         later_planes = zeroed_plane("later_planes", (E - EARLY) * PASSES * H, nc.vector)
         nc.gpsimd.memset(window[:, PASSES * T // 4 :], 0)
-        w2_planes = zeroed_plane("w2_planes", E * N, nc.gpsimd)
         w2s_planes = zeroed_plane("w2s_planes", 2 * N, nc.gpsimd)
 
         offs_t = keep.tile([P, SLOTS // 16], U16, name="offs_t", align_bytes=256)
@@ -158,13 +157,14 @@ def tile_moe_shf_mlp_silu_kernel(
         scales_head = keep.tile([P, PASSES * BYTE_GATHERS[0][1] * C], U8, name="scales_head", align_bytes=256)
         gather_bytes(*BYTE_GATHERS[0], scales_head[:], 0)
         permute_planes()
+        w2_planes = keep.tile([P, E * N // 4], I32, name="w2_planes", tag="w1s_plane", align_bytes=256)
+        nc.gpsimd.memset(w2_planes[:], 0)
+        load_planes_side_by_side(nc.gpsimd, w2_planes, w2_scales.rearrange("e s b i -> (e s) b i"))
         w2_plane = w2_planes[:].bitcast(U8)
         w2s_plane = w2s_planes[:].bitcast(U8)
         for e0 in range(2, E, 2):
             if e0 == EARLY:
                 load_planes_side_by_side(nc.sync, later_planes, w1_rows[PASSES * EARLY :])
-            if e0 == E - 4:
-                load_planes_side_by_side(nc.sync, w2_planes, w2_scales.rearrange("e s b i -> (e s) b i"))
             load_w1(e0, e0 + 2)
         nc.sync.dma_start(
             out=w1s_raw[1][:].rearrange("p (s l) -> p s l", s=PASSES),

@@ -28,7 +28,7 @@ EXPERT_BYTES = PASSES * 2 * H
 SCALE_WINDOW = 1344
 BYTE_GATHERS = [(0, 3), (3, 7), (7, 10)]
 WORD_GATHERS = [(0, 2), (2, 4), (4, 7), (7, 10)]
-HEAD_TILES = 5
+HEAD_TILES = 4
 FIRST_TILES = 2
 EARLY = 4
 TOKEN_CHUNKS = [(0, 2), (2, 4), (4, 5)]
@@ -279,7 +279,7 @@ def tile_moe_shf_mlp_silu_kernel(
             )
 
         for j in range(HEAD_TILES):
-            first_layer_shared(j, 0, bank((1 + j) % 6))
+            first_layer_shared(j, 0, bank((2 + j) % 6))
         pairs = E // 2
         hidden = {}
         grouped = {}
@@ -303,7 +303,7 @@ def tile_moe_shf_mlp_silu_kernel(
         permute_words(1, nc.scalar.copy, "hidden_%d" % (E - 4), [(0, 1), (1, 2)])
         for e0, e1, b in [(0, 4, 3), (4, 8, 1), (8, 10, 5)]:
             second_layer_routed(e0, e1, b)
-        last_banks = [0, 3, 1, 5, 0]
+        last_banks = [2, 0, 3, 1, 5, 2]
         last = [(j, 0) for j in range(HEAD_TILES, TILES)] + [(j, 1) for j in range(TILES)]
         for i, (j, h) in enumerate(last):
             first_layer_shared(j, h, bank(last_banks[i]))

@@ -25,10 +25,10 @@ PASSES = K // W
 SLOTS = E * C
 TILES = T // P
 EXPERT_BYTES = PASSES * 2 * H
-SCALE_WINDOW = 1344
-BYTE_GATHERS = [(0, 3), (3, 7), (7, 10)]
-WORD_GATHERS = [(0, 2), (2, 4), (4, 7), (7, 10)]
-HEAD_TILES = 4
+SCALE_WINDOW = 1536
+BYTE_GATHERS = [(0, 3), (3, 8), (8, 10)]
+WORD_GATHERS = [(0, 2), (2, 4), (4, 6), (6, 8), (8, 10)]
+HEAD_TILES = 5
 FIRST_TILES = 2
 EARLY = 4
 TOKEN_CHUNKS = [(0, 2), (2, 4), (4, 5)]
@@ -188,8 +188,8 @@ def tile_moe_shf_mlp_silu_kernel(
         e0, e1 = BYTE_GATHERS[1]
         scales_middle = keep.tile([P, PASSES * (e1 - e0) * C], U8, name="scales_middle", align_bytes=256)
         gather_bytes(e0, e1, scales_middle[:], e0)
-        slot_words_all = keep.tile([P, PASSES * SLOTS], U32, name="slot_words_all", align_bytes=256)
-        for e0, e1 in WORD_GATHERS:
+        slot_words_all = keep.tile([P, PASSES * (E - 2) * C], U32, name="slot_words_all", align_bytes=256)
+        for e0, e1 in WORD_GATHERS[:-1]:
             gather_words(e0, e1, slot_words_all[:], 0)
 
         def first_layer_routed(e0, e1):
@@ -279,7 +279,7 @@ def tile_moe_shf_mlp_silu_kernel(
             )
 
         for j in range(HEAD_TILES):
-            first_layer_shared(j, 0, bank((2 + j) % 6))
+            first_layer_shared(j, 0, bank((1 + j) % 6))
         pairs = E // 2
         hidden = {}
         grouped = {}
@@ -294,16 +294,18 @@ def tile_moe_shf_mlp_silu_kernel(
                 else:
                     turn(hidden[g], grouped[g], 0, 1, 6, nc.vector.tensor_copy)
                     turn(hidden[g], grouped[g], 1, 2, 0, nc.vector.tensor_copy)
-            if step == 1:
+            if step == 2:
                 e0, e1 = BYTE_GATHERS[2]
                 scales_last = keep.tile([P, PASSES * (e1 - e0) * C], U8, name="scales_last", tag="hidden_0", align_bytes=256)
                 gather_bytes(e0, e1, scales_last[:], e0)
+                words_last = keep.tile([P, PASSES * (e1 - e0) * C], U32, name="words_last", tag="hidden_2", align_bytes=256)
+                gather_words(e0, e1, words_last[:], e0)
             if 0 <= step - 2 < pairs:
                 quantize_routed(2 * step - 4, 2 * step - 2, grouped[step - 2])
         permute_words(1, nc.scalar.copy, "hidden_%d" % (E - 4), [(0, 1), (1, 2)])
         for e0, e1, b in [(0, 4, 3), (4, 8, 1), (8, 10, 5)]:
             second_layer_routed(e0, e1, b)
-        last_banks = [2, 0, 3, 1, 5, 2]
+        last_banks = [2, 0, 3, 1, 5]
         last = [(j, 0) for j in range(HEAD_TILES, TILES)] + [(j, 1) for j in range(TILES)]
         for i, (j, h) in enumerate(last):
             first_layer_shared(j, h, bank(last_banks[i]))

from contextlib import ExitStack

import concourse.mybir as mybir
from concourse.masks import make_identity

K, T, E, C, H, HS, N = 1024, 640, 10, 128, 512, 1024, 128
FLOPS = 2 * (K * H + H * N) * E * C + 2 * (K * HS + HS * N) * T

F32 = mybir.dt.float32
BF16 = mybir.dt.bfloat16
I32 = mybir.dt.int32
U32 = mybir.dt.uint32
U16 = mybir.dt.uint16
U8 = mybir.dt.uint8
FP8X4 = mybir.dt.float8_e4m3fn_x4
FP4X4 = mybir.dt.float4_e2m1fn_x4
SILU = mybir.ActivationFunctionType.Silu
COPY = mybir.ActivationFunctionType.Copy
MULT = mybir.AluOpType.mult
ADD = mybir.AluOpType.add

P = 128
W = 512
PASSES = K // W
SLOTS = E * C
TILES = T // P
EXPERT_BYTES = PASSES * 2 * H
SCALE_WINDOW = 1536
BYTE_GATHERS = [(0, 3), (3, 8), (8, 10)]
WORD_GATHERS = [(0, 2), (2, 4), (4, 6), (6, 8), (8, 10)]
HEAD_TILES = 5
FIRST_TILES = 2
EARLY = 4
TOKEN_CHUNKS = [(0, 2), (2, 4), (4, 5)]


def tile_moe_shf_mlp_silu_kernel(
    tc, x_words, x_scales, w1_words, w1_scales, w2_words, w2_scales, w1s_words, w1s_scales,
    w2s_words, w2s_scales, gate, offs, pos1, pos2, out,
):
    nc = tc.nc
    with ExitStack() as ctx:
        keep = ctx.enter_context(tc.tile_pool(name="keep", bufs=1))
        psum = ctx.enter_context(tc.psum_pool(name="psum", bufs=1))

        def bank(b):
            return psum.tile([P, W], F32, name="bank_%d" % b, tag="bank_%d" % b)

        def zeroed_plane(name, nbytes, engine):
            plane = keep.tile([P, nbytes // 4], I32, name=name, tag=name, align_bytes=256)
            engine.memset(plane[:], 0)
            return plane

        def load_planes_side_by_side(queue, plane, rows):
            groups = rows.shape[0]
            src = rows.rearrange("g (q r) w -> r q g w", r=4)
            for r in range(4):
                queue.dma_start(
                    out=plane[r:P:32, :].rearrange("q (g w) -> q g w", g=groups), in_=src[r].bitcast(I32)
                )

        def load_planes_stacked(queue, plane, rows):
            width = rows.shape[2] // 4
            for q in range(4):
                queue.dma_start(
                    out=plane[32 * q : 32 * q + 8, 0:width], in_=rows[:, 4 * q : 4 * q + 4, :].bitcast(I32)
                )

        window = keep.tile([P, SCALE_WINDOW // 4], I32, name="window", align_bytes=256)
        nc.gpsimd.memset(window[:, 0 : PASSES * T // 4], 0)
        w1s_plane = zeroed_plane("w1s_plane", HS, nc.gpsimd)
        early_planes = zeroed_plane("early_planes", EARLY * PASSES * H, nc.vector)
        later_planes = zeroed_plane("later_planes", (E - EARLY) * PASSES * H, nc.vector)
        nc.gpsimd.memset(window[:, PASSES * T // 4 :], 0)
        w2s_planes = zeroed_plane("w2s_planes", 2 * N, nc.gpsimd)

        offs_t = keep.tile([P, SLOTS // 16], U16, name="offs_t", align_bytes=256)
        xw = keep.tile([P, PASSES * T], I32, name="xw", align_bytes=256)
        w1s_raw = [
            keep.tile([P, PASSES * W], I32, name="w1s_raw_0", tag="w1s_raw_0", align_bytes=256),
            keep.tile([P, PASSES * W], I32, name="w1s_raw_1", align_bytes=256),
        ]
        pos_t = [keep.tile([P, T // 16], U16, name="pos%d_t" % (r + 1), align_bytes=256) for r in range(2)]
        w2_t = keep.tile([P, 2 * E * N], U8, name="w2_t", align_bytes=256)
        w2s_t = keep.tile([P, 2 * N], I32, name="w2s_t", align_bytes=256)
        gate_t = [keep.tile([P, T], F32, name="gate_%d" % r, align_bytes=256) for r in range(2)]
        slot_scales = {}
        slot_words = {}
        w1_t = {}

        def load_w1(e0, e1):
            pair = keep.tile([P, (e1 - e0) * EXPERT_BYTES], U8, name="w1_%d" % e0, align_bytes=256)
            for e in range(e0, e1):
                w1_t[e] = pair[:, EXPERT_BYTES * (e - e0) : EXPERT_BYTES * (e - e0 + 1)]
            nc.sync.dma_start(
                out=pair[:].bitcast(I32).rearrange("p (a b) -> p a b", a=PASSES * (e1 - e0)),
                in_=w1_words[e0:e1].rearrange("e s p b -> p (e s) b").bitcast(I32),
            )

        def gather_words(e0, e1, into, first):
            held = into.shape[1] // PASSES
            for s in range(PASSES):
                gathered = into[:, held * s + C * (e0 - first) : held * s + C * (e1 - first)]
                nc.vector.tensor_copy(
                    gathered, xw[:, T * s : T * (s + 1)].bitcast(U32).indirect(offs_t[:, 8 * e0 : 8 * e1])
                )
                for e in range(e0, e1):
                    slot_words[(e, s)] = gathered[:, C * (e - e0) : C * (e - e0 + 1)]

        xs_b = window[:].bitcast(U8)

        def gather_bytes(e0, e1, into, first):
            width = T if e1 - e0 < 4 else SCALE_WINDOW - T
            held = into.shape[1] // PASSES
            for s in range(PASSES):
                gathered = into[:, held * s + C * (e0 - first) : held * s + C * (e1 - first)]
                nc.vector.tensor_copy(gathered, xs_b[:, T * s : T * s + width].indirect(offs_t[:, 8 * e0 : 8 * e1]))
                for e in range(e0, e1):
                    slot_scales[(e, s)] = gathered[:, C * (e - e0) : C * (e - e0 + 1)]

        w1s_plane_b = w1s_plane[:].bitcast(U8)
        w1s_perm = {}
        w1s_perm_plane = {}

        def permute_words(h, engine, tag, cuts):
            w1s_perm[h] = keep.tile([P, PASSES * W], I32, name="w1s_perm_%d" % h, tag=tag, align_bytes=256)
            dst = w1s_perm[h][:].bitcast(U32).rearrange("p (s t a i) -> p s a t i", s=PASSES, t=4, i=4)
            src = w1s_raw[h][:].bitcast(U32).rearrange("p (s a i t) -> p s a t i", s=PASSES, t=4, i=4)
            for s0, s1 in cuts:
                engine(dst[:, s0:s1], src[:, s0:s1])

        def permute_planes():
            permuted = keep.tile([P, HS], U8, name="w1s_perm_plane", align_bytes=256)
            for h in range(2):
                w1s_perm_plane[h] = permuted[:, W * h : W * (h + 1)]
                nc.gpsimd.tensor_copy(
                    w1s_perm_plane[h].rearrange("p (t m) -> p t m", t=4),
                    w1s_plane_b[:, W * h : W * (h + 1)].rearrange("p (m t) -> p t m", t=4),
                )

        nc.sync.dma_start(offs_t[:], offs)
        load_planes_side_by_side(nc.sync, window[:, 0 : PASSES * T // 4], x_scales)
        for s in range(PASSES):
            nc.sync.dma_start(
                w1s_raw[0][:, W * s : W * (s + 1)], w1s_words[s].rearrange("p l d -> p (l d)")[:, 0 : 4 * W].bitcast(I32)
            )
        load_planes_stacked(nc.sync, w1s_plane, w1s_scales)
        for t0, t1 in [(0, P * FIRST_TILES), (P * FIRST_TILES, T)]:
            nc.sync.dma_start(
                out=xw[:].rearrange("p (s t) -> p s t", s=PASSES)[:, :, t0:t1],
                in_=x_words.rearrange("s p t d -> p s (t d)").bitcast(I32)[:, :, t0:t1],
            )
        w1_rows = w1_scales.rearrange("e s b i -> (e s) b i")
        load_planes_side_by_side(nc.sync, early_planes, w1_rows[0 : PASSES * EARLY])
        load_w1(0, 2)
        permute_words(0, nc.gpsimd.tensor_copy, "w1s_perm_0", [(0, 1), (1, 2)])
        scales_head = keep.tile([P, PASSES * BYTE_GATHERS[0][1] * C], U8, name="scales_head", align_bytes=256)
        gather_bytes(*BYTE_GATHERS[0], scales_head[:], 0)
        permute_planes()
        w2_planes = keep.tile([P, E * N // 4], I32, name="w2_planes", tag="w1s_plane", align_bytes=256)
        nc.gpsimd.memset(w2_planes[:], 0)
        load_planes_side_by_side(nc.gpsimd, w2_planes, w2_scales.rearrange("e s b i -> (e s) b i"))
        w2_plane = w2_planes[:].bitcast(U8)
        w2s_plane = w2s_planes[:].bitcast(U8)
        for e0 in range(2, E, 2):
            if e0 == EARLY:
                load_planes_side_by_side(nc.sync, later_planes, w1_rows[PASSES * EARLY :])
            load_w1(e0, e0 + 2)
        nc.sync.dma_start(
            out=w1s_raw[1][:].rearrange("p (s l) -> p s l", s=PASSES),
            in_=w1s_words.rearrange("s p l d -> p s (l d)")[:, :, 4 * W : 8 * W].bitcast(I32),
        )
        nc.sync.dma_start(
            out=w2_t[:].bitcast(I32).rearrange("p (e b) -> p e b", e=E),
            in_=w2_words.rearrange("e s p b -> p (e s) b").bitcast(I32),
        )
        nc.sync.dma_start(pos_t[0][:], pos1)
        nc.sync.dma_start(pos_t[1][:], pos2)
        nc.sync.dma_start(gate_t[0][:], gate[0])
        nc.sync.dma_start(gate_t[1][:], gate[1])
        nc.sync.dma_start(
            out=w2s_t[:].rearrange("p (s n) -> p s n", s=2), in_=w2s_words.rearrange("s p n d -> p s (n d)").bitcast(I32)
        )
        load_planes_side_by_side(nc.sync, w2s_planes, w2s_scales)

        ident = keep.tile([P, P], F32, name="ident", align_bytes=256)
        make_identity(nc, ident[:])
        e0, e1 = BYTE_GATHERS[1]
        scales_middle = keep.tile([P, PASSES * (e1 - e0) * C], U8, name="scales_middle", align_bytes=256)
        gather_bytes(e0, e1, scales_middle[:], e0)
        slot_words_all = keep.tile([P, PASSES * (E - 2) * C], U32, name="slot_words_all", align_bytes=256)
        for e0, e1 in WORD_GATHERS[:-1]:
            gather_words(e0, e1, slot_words_all[:], 0)

        def first_layer_routed(e0, e1):
            hidden = keep.tile([P, (e1 - e0) * W], BF16, name="hidden_%d" % e0, tag="hidden_%d" % e0, align_bytes=256)
            for e in range(e0, e1):
                acc = bank(e % 6)
                for s in range(PASSES):
                    planes, a = (early_planes, PASSES * e + s) if e < EARLY else (later_planes, PASSES * (e - EARLY) + s)
                    nc.tensor.matmul_mx(
                        out=acc[:],
                        lhsT=slot_words[(e, s)].bitcast(FP8X4),
                        lhsT_scale=slot_scales[(e, s)],
                        rhs=w1_t[e][:, 2 * H * s : 2 * H * (s + 1)].bitcast(FP4X4),
                        rhs_scale=planes[:].bitcast(U8)[:, H * a : H * (a + 1)],
                        start=(s == 0), stop=(s == PASSES - 1),
                    )
                nc.scalar.activation(
                    hidden[:, W * (e - e0) : W * (e - e0 + 1)].rearrange("r (u p e) -> r u p e", u=2, e=2),
                    acc[:].rearrange("r (p u e) -> r u p e", u=2, e=2),
                    SILU,
                )
            return hidden

        def turn(hidden, grouped, b0, b1, b, copy):
            nb = b1 - b0
            words = hidden[:, W * b0 : W * b1].bitcast(F32)
            turned = bank(b)
            for j in range(2 * nb):
                nc.tensor.transpose(turned[:, P * j : P * (j + 1)], words[:, P * j : P * (j + 1)], ident[:])
            copy(
                grouped[:, W * b0 : W * b1].bitcast(F32).rearrange("p (b r u) -> p b r u", b=nb, u=2),
                turned[:, 0 : 2 * P * nb].rearrange("p (b u r) -> p b r u", b=nb, u=2),
            )

        def quantize(name, values, width):
            words = keep.tile([P, width], U32, name="codes_" + name, align_bytes=256)
            scales = keep.tile([P, width], U8, name="scales_" + name, align_bytes=256)
            nc.vector.quantize_mx(out=words[:].bitcast(FP8X4), scales=scales[:], in_=values)
            return words, scales

        codes = {}

        def quantize_routed(e0, e1, grouped):
            words, scales = quantize("routed_%d" % e0, grouped[:], (e1 - e0) * C)
            for e in range(e0, e1):
                codes[e] = (words[:, C * (e - e0) : C * (e - e0 + 1)], scales[:, C * (e - e0) : C * (e - e0 + 1)])

        y_sb = keep.tile([P, SLOTS], F32, name="y_sb", align_bytes=256)

        def second_layer_routed(e0, e1, b):
            y = bank(b)
            for e in range(e0, e1):
                nc.tensor.matmul_mx(
                    out=y[:, C * (e - e0) : C * (e - e0 + 1)],
                    lhsT=w2_t[:, 2 * N * e : 2 * N * (e + 1)].bitcast(FP4X4),
                    lhsT_scale=w2_plane[:, N * e : N * (e + 1)],
                    rhs=codes[e][0].bitcast(FP8X4), rhs_scale=codes[e][1],
                    start=True, stop=True,
                )
            nc.vector.tensor_copy(y_sb[:, C * e0 : C * e1], y[:, 0 : C * (e1 - e0)])

        hs = {}
        hs_chunk = {}
        for h in range(2):
            for j0, j1 in TOKEN_CHUNKS:
                name = "hs_%d_%d" % (h, j0)
                chunk = keep.tile([P, (j1 - j0) * W], BF16, name=name, tag=name, align_bytes=256)
                hs_chunk[(h, P * j0)] = chunk
                for j in range(j0, j1):
                    hs[(h, j)] = chunk[:, W * (j - j0) : W * (j - j0 + 1)]

        def first_layer_shared(j, h, acc):
            for t in range(4):
                for s in range(PASSES):
                    nc.tensor.matmul_mx(
                        out=acc[:, P * t : P * (t + 1)],
                        lhsT=w1s_perm[h][:, W * s + P * t : W * s + P * (t + 1)].bitcast(FP8X4),
                        lhsT_scale=w1s_perm_plane[h][4 * s : P, P * t : P * (t + 1)],
                        rhs=xw[:, T * s + P * j : T * s + P * (j + 1)].bitcast(FP8X4),
                        rhs_scale=xs_b[:, T * s + P * j : T * s + P * (j + 1)],
                        start=(s == 0), stop=(s == PASSES - 1),
                    )
            nc.scalar.activation(
                hs[(h, j)].rearrange("p (c i t) -> p c t i", t=4, i=4),
                acc[:].rearrange("p (t c i) -> p c t i", t=4, i=4),
                SILU,
            )

        for j in range(HEAD_TILES):
            first_layer_shared(j, 0, bank((1 + j) % 6))
        pairs = E // 2
        hidden = {}
        grouped = {}
        for step in range(pairs + 2):
            if step < pairs:
                hidden[step] = first_layer_routed(2 * step, 2 * step + 2)
            if 0 <= step - 1 < pairs:
                g = step - 1
                grouped[g] = keep.tile([P, 2 * W], BF16, name="grouped_%d" % g, tag="grouped_%d" % g, align_bytes=256)
                if g < pairs - 1:
                    turn(hidden[g], grouped[g], 0, 2, 6 + g % 2, nc.scalar.copy if g < 3 else nc.vector.tensor_copy)
                else:
                    turn(hidden[g], grouped[g], 0, 1, 6, nc.vector.tensor_copy)
                    turn(hidden[g], grouped[g], 1, 2, 0, nc.vector.tensor_copy)
            if step == 2:
                e0, e1 = BYTE_GATHERS[2]
                scales_last = keep.tile([P, PASSES * (e1 - e0) * C], U8, name="scales_last", tag="hidden_0", align_bytes=256)
                gather_bytes(e0, e1, scales_last[:], e0)
                words_last = keep.tile([P, PASSES * (e1 - e0) * C], U32, name="words_last", tag="hidden_2", align_bytes=256)
                gather_words(e0, e1, words_last[:], e0)
            if 0 <= step - 2 < pairs:
                quantize_routed(2 * step - 4, 2 * step - 2, grouped[step - 2])
        permute_words(1, nc.scalar.copy, "hidden_%d" % (E - 4), [(0, 1), (1, 2)])
        for e0, e1, b in [(0, 4, 3), (4, 8, 1), (8, 10, 5)]:
            second_layer_routed(e0, e1, b)
        last_banks = [2, 0, 3, 1, 5]
        last = [(j, 0) for j in range(HEAD_TILES, TILES)] + [(j, 1) for j in range(TILES)]
        for i, (j, h) in enumerate(last):
            first_layer_shared(j, h, bank(last_banks[i]))

        first_part = keep.tile([P, T], F32, name="first_part", align_bytes=256)
        fetched = keep.tile([P, T], F32, name="fetched", align_bytes=256)
        second_part = keep.tile([P, T], F32, name="second_part", align_bytes=256)
        both = keep.tile([P, T], F32, name="both", align_bytes=256)
        result = keep.tile([P, T], F32, name="result", align_bytes=256)
        chunks = [(P * j0, P * j1) for j0, j1 in TOKEN_CHUNKS]
        hs_codes = {}

        def quantize_shared(h, t0, t1):
            hs_codes[(h, t0)] = quantize("shared_%d_%d" % (h, t0), hs_chunk[(h, t0)][:], t1 - t0)

        def routed_sum(t0, t1):
            listed = y_sb[:].indirect(pos_t[1][:, t0 // 16 : t1 // 16])
            if t0 > 0:
                nc.scalar.activation(fetched[:, t0:t1], listed, COPY)
                listed = fetched[:, t0:t1]
            nc.vector.tensor_tensor(second_part[:, t0:t1], listed, gate_t[1][:, t0:t1], MULT)
            nc.vector.tensor_tensor(both[:, t0:t1], first_part[:, t0:t1], second_part[:, t0:t1], ADD)

        def finish(t0, t1):
            quantize_shared(1, t0, t1)
            ys = bank(last_banks[last.index((t1 // P - 1, 1))])
            for h in range(2):
                words, scales = hs_codes[(h, t0)]
                nc.tensor.matmul_mx(
                    out=ys[:, 0 : t1 - t0],
                    lhsT=w2s_t[:, N * h : N * (h + 1)].bitcast(FP8X4),
                    lhsT_scale=w2s_plane[:, N * h : N * (h + 1)],
                    rhs=words[:].bitcast(FP8X4), rhs_scale=scales[:],
                    start=(h == 0), stop=(h == 1),
                )
            nc.vector.tensor_tensor(result[:, t0:t1], ys[:, 0 : t1 - t0], both[:, t0:t1], ADD)
            nc.sync.dma_start(out[:, t0:t1], result[:, t0:t1])

        for t0, t1 in chunks:
            quantize_shared(0, t0, t1)
        nc.vector.tensor_tensor(first_part[:], y_sb[:].indirect(pos_t[0][:]), gate_t[0][:], MULT)
        routed_sum(0, 2 * P)
        finish(*chunks[0])
        routed_sum(2 * P, T)
        finish(*chunks[1])
        finish(*chunks[2])
